import numpy as np
import ml_dtypes


def mxq(x, axis, fmt="e4m3"):
    dtype, down = {"e4m3": (ml_dtypes.float8_e4m3fn, 7), "e5m2": (ml_dtypes.float8_e5m2, 14)}[fmt]
    v = np.moveaxis(np.asarray(x, np.float32).astype(ml_dtypes.bfloat16).astype(np.float64), axis, -1)
    blocks = v.reshape(v.shape[:-1] + (-1, 32))
    amax = np.abs(blocks).max(-1, keepdims=True)
    byte = np.maximum(np.where(amax > 0, np.frexp(amax)[1] - 1 + 127, 0) - down, 1)
    scale = np.exp2(byte - 127.0)
    codes = (blocks / scale).astype(np.float32).astype(dtype).astype(np.float64)
    return np.moveaxis((codes * scale).reshape(v.shape), -1, axis)


WIDE = False


def mx_kscale(k):
    if not WIDE:
        return np.ones(k)
    levels = np.array([10, -10, 5, -5, 0])
    if k % 512:
        return np.exp2(np.random.permutation(np.resize(levels, k // 32))).repeat(32)
    a = np.empty((k // 512, 16))
    for p in range(k // 512):
        a[p, :8] = np.random.permutation(np.resize(levels, 8))
        for g in range(8):
            far = levels[np.abs(levels - a[p, g]) >= 10]
            a[p, g + 8] = far[np.random.randint(len(far))]
    return np.exp2(a.ravel()).repeat(32)


def f64(x):
    return np.asarray(x).astype(np.float64)


def striped(idx):
    return np.tile(idx.reshape(-1, 16).T, (8, 1)).astype(np.uint16)


def unstriped(offs):
    return offs[:16].T.reshape(-1).astype(np.int64)


def relu(v):
    return np.maximum(v, 0.0)

def planes(y):
    n, m = y.shape
    v = y.astype(np.float32).astype(ml_dtypes.bfloat16).astype(np.float64).reshape(n // 32, 32, m)
    top = np.abs(v).max(1)
    byte = np.clip(np.where(top > 0, np.frexp(top)[1] - 1 + 127 - 7, 1), 1, 254)
    codes = (v * np.exp2(127.0 - byte)[:, None, :]).reshape(n, m).astype(np.float32).astype(ml_dtypes.float8_e4m3fn).view(np.uint8)
    words = codes.reshape(n // 512, 128, 4, m).transpose(0, 1, 3, 2)
    return np.ascontiguousarray(words), np.ascontiguousarray(byte.astype(np.uint8).reshape(n // 512, 16, m))


K, T, S, H, U, V = 512, 2048, 1024, 512, 1024, 512


def setup_inputs():
    n = np.random.standard_normal
    s = mx_kscale(K)[:, None]
    u = mx_kscale(H)
    return {
        "xT": (n((K, T)) * s).astype(np.float32),
        "w1": (n((K, H)) / np.sqrt(K) / s * u).astype(np.float32),
        "w2": (n((K, H)) / np.sqrt(K) / s * u).astype(np.float32),
        "w3": (n((H, H)) / np.sqrt(H) / u[:, None]).astype(np.float32),
        "offs": striped(np.random.permutation(T)[:S]),
        "near": striped(np.random.permutation(U)[:V]),
        "far": striped(np.random.permutation(U)[:V]),
    }


def reference(xT, w1, w2, w3, offs, near, far):
    xq = mxq(f64(xT)[:, unstriped(offs)], 0, "e4m3")
    a = np.zeros((H, S))
    a[:, unstriped(near)] = relu(mxq(f64(w1), 0, "e4m3").T @ xq[:, :V])
    e = np.zeros((H, S))
    e[:, unstriped(far)] = relu(mxq(f64(w2), 0, "e4m3").T @ xq[:, V:2 * V])
    z = np.maximum(a, e)
    out_0 = mxq(f64(w3), 0, "e4m3").T @ mxq(z, 0, "e4m3")
    return (out_0,) + planes(out_0)

@@ -1,0 +1,167 @@
+from contextlib import ExitStack
+
+import concourse.mybir as mybir
+
+K, T, S, H, V = 512, 2048, 1024, 512, 512
+FLOPS = 2 * K * H * 2 * V + 2 * H * H * S
+
+F32 = mybir.dt.float32
+BF16 = mybir.dt.bfloat16
+U32 = mybir.dt.uint32
+I32 = mybir.dt.int32
+U16 = mybir.dt.uint16
+U8 = mybir.dt.uint8
+FP8X4 = mybir.dt.float8_e4m3fn_x4
+RELU = mybir.ActivationFunctionType.Relu
+MAX = mybir.AluOpType.max
+
+P = 128
+PACK = 4
+CHUNK = 256
+LIST_ROWS = 16
+
+
+def tile_picked_bev_max_lo_kernel(
+    tc, xT, w1, w2, w3, offs, near, far, out_0, out_1, out_2
+):
+    nc = tc.nc
+    with ExitStack() as ctx:
+        lists = ctx.enter_context(tc.tile_pool(name="lists", bufs=1))
+        keep = ctx.enter_context(tc.tile_pool(name="keep", bufs=1))
+        psum = ctx.enter_context(tc.psum_pool(name="psum", bufs=1))
+
+        offs_sb = lists.tile([P, S // LIST_ROWS], U16, name="offs_sb")
+        cell_lists = [lists.tile([P, V // LIST_ROWS], U16, name=f"cells{s}") for s in range(2)]
+        x_rows = xT.rearrange("(p j) c -> p j c", j=PACK)
+        x_planes = [keep.tile([P, T], F32, name=f"x{j}") for j in range(PACK)]
+        w_raw = [keep.tile([P, PACK, H], F32, name=f"w_raw{i}") for i in range(3)]
+
+        nc.sync.dma_start(offs_sb[:], offs)
+        for j in range(PACK):
+            nc.sync.dma_start(x_planes[j][:], x_rows[:, j, :])
+        nc.sync.dma_start(w_raw[0][:], w1.rearrange("(p j) c -> p j c", j=PACK))
+        nc.sync.dma_start(cell_lists[0][:], near)
+        nc.sync.dma_start(cell_lists[1][:], far)
+        nc.sync.dma_start(w_raw[1][:], w2.rearrange("(p j) c -> p j c", j=PACK))
+        nc.sync.dma_start(w_raw[2][:], w3.rearrange("(p j) c -> p j c", j=PACK))
+
+        maps = [[keep.tile([P, S], F32, name=f"map{s}_{t}") for t in range(PACK)] for s in range(2)]
+        for s in range(2):
+            for t in range(PACK):
+                nc.vector.memset(maps[s][t][:], 0.0)
+
+        def quantize(codes, scales, grouped):
+            nc.vector.quantize_mx(out=codes.bitcast(FP8X4), scales=scales, in_=grouped)
+
+        picked = [keep.tile([P, PACK, V], BF16, name=f"picked{s}") for s in range(2)]
+        x_grouped = [keep.tile([P, V * PACK], BF16, name=f"x_grouped{s}", align_bytes=64) for s in range(2)]
+        x_codes = [keep.tile([P, V], U32, name=f"x_codes{s}", align_bytes=64) for s in range(2)]
+        x_scales = [keep.tile([P, V], U8, name=f"x_scales{s}", align_bytes=64) for s in range(2)]
+
+        def gather(s, j):
+            entries = offs_sb[:, s * V // LIST_ROWS : (s + 1) * V // LIST_ROWS]
+            nc.vector.tensor_copy(picked[s][:, j, :], x_planes[j][:].indirect(entries))
+
+        def x_views(s):
+            return (x_grouped[s][:].rearrange("p (v j) -> p v j", j=PACK), picked[s][:].rearrange("p j v -> p v j"))
+
+        for j in range(PACK - 1):
+            gather(0, j)
+            gather(1, j)
+        gather(0, PACK - 1)
+        nc.vector.tensor_copy(*x_views(0))
+        quantize(x_codes[0][:], x_scales[0][:], x_grouped[0][:])
+
+        w1_grouped = [keep.tile([P, P * PACK], BF16, name=f"w1_grouped{t}", align_bytes=64) for t in range(PACK)]
+        w1_codes = [keep.tile([P, P], U32, name=f"w1_codes{t}", align_bytes=64) for t in range(PACK)]
+        w1_scales = [keep.tile([P, P], U8, name=f"w1_scales{t}", align_bytes=64) for t in range(PACK)]
+        banks = [psum.tile([P, V], F32, name=f"bank{b}", tag=f"bank{b}") for b in range(2 * PACK)]
+        acts = [[keep.tile([P, V], F32, name=f"act{s}_{t}") for t in range(PACK)] for s in range(2)]
+
+        def layer(s, t, codes, scales):
+            bank = banks[s * PACK + t]
+            nc.tensor.matmul_mx(
+                out=bank[:], lhsT=codes.bitcast(FP8X4), lhsT_scale=scales,
+                rhs=x_codes[s][:].bitcast(FP8X4), rhs_scale=x_scales[s][:], start=True, stop=True,
+            )
+            nc.scalar.activation(acts[s][t][:], bank[:], RELU)
+
+        def scatter(s, t):
+            nc.vector.tensor_copy(maps[s][t][:].indirect(cell_lists[s][:]), acts[s][t][:])
+
+        for t in range(PACK):
+            nc.scalar.copy(
+                w1_grouped[t][:].rearrange("p (m j) -> p m j", j=PACK),
+                w_raw[0][:].rearrange("p j (m t) -> p t m j", t=PACK)[:, t],
+            )
+            quantize(w1_codes[t][:], w1_scales[t][:], w1_grouped[t][:])
+            layer(0, t, w1_codes[t][:], w1_scales[t][:])
+            if t == 0:
+                gather(1, PACK - 1)
+        for t in range(PACK):
+            scatter(0, t)
+
+        nc.scalar.copy(*x_views(1))
+        quantize(x_codes[1][:], x_scales[1][:], x_grouped[1][:])
+
+        w_grouped = [keep.tile([P, H * PACK], BF16, name=f"w_grouped{i}", align_bytes=64) for i in range(2)]
+        w_codes = [keep.tile([P, H], U32, name=f"w_codes{i}", align_bytes=64) for i in range(2)]
+        w_scales = [keep.tile([P, H], U8, name=f"w_scales{i}", align_bytes=64) for i in range(2)]
+
+        def prepare(i):
+            nc.scalar.copy(
+                w_grouped[i][:].rearrange("p (t m j) -> p m t j", t=PACK, j=PACK),
+                w_raw[i + 1][:].rearrange("p j (m t) -> p m t j", t=PACK),
+            )
+            quantize(w_codes[i][:], w_scales[i][:], w_grouped[i][:])
+
+        prepare(0)
+        for t in range(PACK):
+            layer(1, t, w_codes[0][:, t * P : (t + 1) * P], w_scales[0][:, t * P : (t + 1) * P])
+        prepare(1)
+
+        n_chunks = S // CHUNK
+        z_planes = [keep.tile([P, PACK, CHUNK], BF16, name=f"z_planes{c}") for c in range(n_chunks)]
+        for t in range(PACK):
+            scatter(1, t)
+            for c in range(n_chunks):
+                cells = slice(c * CHUNK, (c + 1) * CHUNK)
+                nc.vector.tensor_tensor(z_planes[c][:, t, :], maps[0][t][:, cells], maps[1][t][:, cells], MAX)
+
+        out_rows = out_0.rearrange("(p t) c -> p t c", t=PACK)
+        out_words = out_1[0].rearrange("p c r -> p (c r)").bitcast(I32)
+        out_codes = keep.tile([P, S], U32, name="out_codes", align_bytes=64)
+        out_scales = keep.tile([P, S], U8, name="out_scales", align_bytes=64)
+        for c in range(n_chunks):
+            cells = slice(c * CHUNK, (c + 1) * CHUNK)
+            z_grouped = keep.tile([P, CHUNK * PACK], BF16, name=f"z_grouped{c}", align_bytes=64)
+            z_codes = keep.tile([P, CHUNK], U32, name=f"z_codes{c}", align_bytes=64)
+            z_scales = keep.tile([P, CHUNK], U8, name=f"z_scales{c}", align_bytes=64)
+            views = (z_grouped[:].rearrange("p (r t) -> p r t", t=PACK), z_planes[c][:].rearrange("p t r -> p r t"))
+            if c == 0:
+                nc.vector.tensor_copy(*views)
+            else:
+                nc.scalar.copy(*views)
+            quantize(z_codes[:], z_scales[:], z_grouped[:])
+            result = keep.tile([P, PACK, CHUNK], F32, name=f"result{c}")
+            for half in range(2):
+                b = 2 * c + half
+                bank = psum.tile([P, 2, CHUNK], F32, name=f"out_bank{b}", tag=f"bank{b}")
+                for u in range(2):
+                    cols = slice((2 * half + u) * P, (2 * half + u + 1) * P)
+                    nc.tensor.matmul_mx(
+                        out=bank[:, u, :], lhsT=w_codes[1][:, cols].bitcast(FP8X4), lhsT_scale=w_scales[1][:, cols],
+                        rhs=z_codes[:].bitcast(FP8X4), rhs_scale=z_scales[:], start=True, stop=True,
+                    )
+                nc.scalar.copy(result[:, 2 * half : 2 * half + 2, :], bank[:])
+            nc.sync.dma_start(out_rows[:, :, cells], result[:])
+            out_grouped = keep.tile([P, CHUNK * PACK], BF16, name=f"out_grouped{c}", align_bytes=64)
+            nc.vector.tensor_copy(
+                out_grouped[:].rearrange("p (r t) -> p r t", t=PACK), result[:].rearrange("p t r -> p r t")
+            )
+            quantize(out_codes[:, cells], out_scales[:, cells], out_grouped[:])
+            nc.sync.dma_start(out_words[:, cells], out_codes[:, cells].bitcast(I32))
+        for q in range(P // 32):
+            nc.sync.dma_start(
+                out_2[0, 4 * q : 4 * q + 4, :].bitcast(I32), out_scales[32 * q : 32 * q + 4, :].bitcast(I32)
+            )

@@ -13,11 +13,12 @@ U16 = mybir.dt.uint16
 U8 = mybir.dt.uint8
 FP8X4 = mybir.dt.float8_e4m3fn_x4
 RELU = mybir.ActivationFunctionType.Relu
+COPY = mybir.ActivationFunctionType.Copy
 MAX = mybir.AluOpType.max
 
 P = 128
 PACK = 4
-CHUNK = 256
+CHUNKS = (1, 2, 2, 2, 1)
 LIST_ROWS = 16
 
 
@@ -48,120 +49,156 @@ def tile_picked_bev_max_lo_kernel(
         maps = [[keep.tile([P, S], F32, name=f"map{s}_{t}") for t in range(PACK)] for s in range(2)]
         for s in range(2):
             for t in range(PACK):
-                nc.vector.memset(maps[s][t][:], 0.0)
+                nc.gpsimd.memset(maps[s][t][:].bitcast(I32), 0)
+
+        def weave_views(grouped, planes):
+            return (
+                grouped.rearrange("p (c i j) -> p c j i", i=PACK, j=PACK),
+                planes.rearrange("p j (c i) -> p c j i", i=PACK),
+            )
 
         def quantize(codes, scales, grouped):
             nc.vector.quantize_mx(out=codes.bitcast(FP8X4), scales=scales, in_=grouped)
 
-        picked = [keep.tile([P, PACK, V], BF16, name=f"picked{s}") for s in range(2)]
-        x_grouped = [keep.tile([P, V * PACK], BF16, name=f"x_grouped{s}", align_bytes=64) for s in range(2)]
+        picked = [keep.tile([P, PACK, V], BF16, name=f"picked{s}", align_bytes=64) for s in range(2)]
+        x_grouped = [keep.tile([P, V * PACK], BF16, name="x_grouped0", align_bytes=64)]
         x_codes = [keep.tile([P, V], U32, name=f"x_codes{s}", align_bytes=64) for s in range(2)]
         x_scales = [keep.tile([P, V], U8, name=f"x_scales{s}", align_bytes=64) for s in range(2)]
 
-        def gather(s, j):
-            entries = offs_sb[:, s * V // LIST_ROWS : (s + 1) * V // LIST_ROWS]
-            nc.vector.tensor_copy(picked[s][:, j, :], x_planes[j][:].indirect(entries))
+        def gather(s, j, lo, hi):
+            entries = offs_sb[:, (s * V + lo) // LIST_ROWS : (s * V + hi) // LIST_ROWS]
+            nc.vector.tensor_copy(picked[s][:, j, lo:hi], x_planes[j][:].indirect(entries))
 
-        def x_views(s):
-            return (x_grouped[s][:].rearrange("p (v j) -> p v j", j=PACK), picked[s][:].rearrange("p j v -> p v j"))
+        def gather_rounded(s, j):
+            rounded = keep.tile([P, T], BF16, name=f"x_rounded{j}")
+            nc.scalar.copy(rounded[:], x_planes[j][:])
+            entries = offs_sb[:, s * V // LIST_ROWS : (s + 1) * V // LIST_ROWS]
+            nc.scalar.activation(picked[s][:, j, :], rounded[:].indirect(entries), COPY)
+
+        def x_views(s, lo, hi):
+            return weave_views(x_grouped[s][:, lo * PACK : hi * PACK], picked[s][:, :, lo:hi])
 
         for j in range(PACK - 1):
-            gather(0, j)
-            gather(1, j)
-        gather(0, PACK - 1)
-        nc.vector.tensor_copy(*x_views(0))
+            gather(0, j, 0, V)
+            if j < 2:
+                gather_rounded(1, j)
+            else:
+                gather(1, j, 0, V)
+        gather(0, PACK - 1, 0, V // 2)
+        nc.scalar.copy(*x_views(0, 0, V // 2))
+        gather(0, PACK - 1, V // 2, V)
+        nc.vector.tensor_copy(*x_views(0, V // 2, V))
         quantize(x_codes[0][:], x_scales[0][:], x_grouped[0][:])
 
-        w1_grouped = [keep.tile([P, P * PACK], BF16, name=f"w1_grouped{t}", align_bytes=64) for t in range(PACK)]
-        w1_codes = [keep.tile([P, P], U32, name=f"w1_codes{t}", align_bytes=64) for t in range(PACK)]
-        w1_scales = [keep.tile([P, P], U8, name=f"w1_scales{t}", align_bytes=64) for t in range(PACK)]
         banks = [psum.tile([P, V], F32, name=f"bank{b}", tag=f"bank{b}") for b in range(2 * PACK)]
         acts = [[keep.tile([P, V], F32, name=f"act{s}_{t}") for t in range(PACK)] for s in range(2)]
 
-        def layer(s, t, codes, scales):
-            bank = banks[s * PACK + t]
+        def product(s, t, codes, scales):
             nc.tensor.matmul_mx(
-                out=bank[:], lhsT=codes.bitcast(FP8X4), lhsT_scale=scales,
+                out=banks[s * PACK + t][:], lhsT=codes.bitcast(FP8X4), lhsT_scale=scales,
                 rhs=x_codes[s][:].bitcast(FP8X4), rhs_scale=x_scales[s][:], start=True, stop=True,
             )
-            nc.scalar.activation(acts[s][t][:], bank[:], RELU)
+
+        def activate(s, t):
+            nc.scalar.activation(acts[s][t][:], banks[s * PACK + t][:], RELU)
 
         def scatter(s, t):
             nc.vector.tensor_copy(maps[s][t][:].indirect(cell_lists[s][:]), acts[s][t][:])
 
-        for t in range(PACK):
+        def first_products(t0, n, grouped):
+            codes = keep.tile([P, n * P], U32, name=f"w1_codes{t0}", tag=f"w1_codes{t0}", align_bytes=64)
+            scales = keep.tile([P, n * P], U8, name=f"w1_scales{t0}", tag=f"w1_scales{t0}", align_bytes=64)
             nc.scalar.copy(
-                w1_grouped[t][:].rearrange("p (m j) -> p m j", j=PACK),
-                w_raw[0][:].rearrange("p j (m t) -> p t m j", t=PACK)[:, t],
+                grouped.rearrange("p (t m j) -> p m j t", t=n, j=PACK),
+                w_raw[0][:].rearrange("p j (m t) -> p m j t", t=PACK)[:, :, :, t0 : t0 + n],
             )
-            quantize(w1_codes[t][:], w1_scales[t][:], w1_grouped[t][:])
-            layer(0, t, w1_codes[t][:], w1_scales[t][:])
-            if t == 0:
-                gather(1, PACK - 1)
-        for t in range(PACK):
-            scatter(0, t)
+            quantize(codes[:], scales[:], grouped)
+            for u in range(n):
+                product(0, t0 + u, codes[:, u * P : (u + 1) * P], scales[:, u * P : (u + 1) * P])
 
-        nc.scalar.copy(*x_views(1))
-        quantize(x_codes[1][:], x_scales[1][:], x_grouped[1][:])
-
-        w_grouped = [keep.tile([P, H * PACK], BF16, name=f"w_grouped{i}", align_bytes=64) for i in range(2)]
         w_codes = [keep.tile([P, H], U32, name=f"w_codes{i}", align_bytes=64) for i in range(2)]
         w_scales = [keep.tile([P, H], U8, name=f"w_scales{i}", align_bytes=64) for i in range(2)]
 
-        def prepare(i):
+        def prepare(i, tag):
+            grouped = keep.tile([P, H * PACK], BF16, name=f"w_grouped{i}", tag=tag, align_bytes=64)
             nc.scalar.copy(
-                w_grouped[i][:].rearrange("p (t m j) -> p m t j", t=PACK, j=PACK),
-                w_raw[i + 1][:].rearrange("p j (m t) -> p m t j", t=PACK),
+                grouped[:].rearrange("p (t m j) -> p m j t", t=PACK, j=PACK),
+                w_raw[i + 1][:].rearrange("p j (m t) -> p m j t", t=PACK),
             )
-            quantize(w_codes[i][:], w_scales[i][:], w_grouped[i][:])
+            quantize(w_codes[i][:], w_scales[i][:], grouped[:])
 
-        prepare(0)
+        first_products(0, 1, picked[1][:, PACK - 1, :])
+        gather(1, PACK - 1, 0, V)
+        activate(0, 0)
+        scatter(0, 0)
+        first_products(1, 1, keep.tile([P, P * PACK], BF16, name="w1_grouped1", align_bytes=64)[:])
+        activate(0, 1)
+        scatter(0, 1)
+        first_products(2, 2, keep.tile([P, 2 * P * PACK], BF16, name="w1_grouped2", tag="w1_codes0", align_bytes=64)[:])
+        x_grouped.append(keep.tile([P, V * PACK], BF16, name="x_grouped1", tag="w1_codes1", align_bytes=64))
+        nc.scalar.copy(*x_views(1, 0, V))
+        quantize(x_codes[1][:], x_scales[1][:], x_grouped[1][:])
+        activate(0, 2)
+        scatter(0, 2)
+        prepare(0, "w1_scales0")
+        activate(0, 3)
+        scatter(0, 3)
+        prepare(1, "w3_grouped")
         for t in range(PACK):
-            layer(1, t, w_codes[0][:, t * P : (t + 1) * P], w_scales[0][:, t * P : (t + 1) * P])
-        prepare(1)
+            product(1, t, w_codes[0][:, t * P : (t + 1) * P], w_scales[0][:, t * P : (t + 1) * P])
+            activate(1, t)
 
-        n_chunks = S // CHUNK
-        z_planes = [keep.tile([P, PACK, CHUNK], BF16, name=f"z_planes{c}") for c in range(n_chunks)]
-        for t in range(PACK):
+        z_planes = keep.tile([P, S // P, PACK, P], BF16, name="z_planes")
+
+        def fuse(t, lo, hi):
+            a_map, e_map = (maps[s][t][:, lo * P : hi * P].rearrange("p (g r) -> p g r", r=P) for s in range(2))
+            nc.vector.tensor_tensor(z_planes[:, lo:hi, t, :], a_map, e_map, MAX)
+
+        for t in range(PACK - 1):
             scatter(1, t)
-            for c in range(n_chunks):
-                cells = slice(c * CHUNK, (c + 1) * CHUNK)
-                nc.vector.tensor_tensor(z_planes[c][:, t, :], maps[0][t][:, cells], maps[1][t][:, cells], MAX)
+            fuse(t, 0, S // P)
+        scatter(1, PACK - 1)
 
         out_rows = out_0.rearrange("(p t) c -> p t c", t=PACK)
         out_words = out_1[0].rearrange("p c r -> p (c r)").bitcast(I32)
         out_codes = keep.tile([P, S], U32, name="out_codes", align_bytes=64)
         out_scales = keep.tile([P, S], U8, name="out_scales", align_bytes=64)
-        for c in range(n_chunks):
-            cells = slice(c * CHUNK, (c + 1) * CHUNK)
-            z_grouped = keep.tile([P, CHUNK * PACK], BF16, name=f"z_grouped{c}", align_bytes=64)
-            z_codes = keep.tile([P, CHUNK], U32, name=f"z_codes{c}", align_bytes=64)
-            z_scales = keep.tile([P, CHUNK], U8, name=f"z_scales{c}", align_bytes=64)
-            views = (z_grouped[:].rearrange("p (r t) -> p r t", t=PACK), z_planes[c][:].rearrange("p t r -> p r t"))
-            if c == 0:
-                nc.vector.tensor_copy(*views)
-            else:
-                nc.scalar.copy(*views)
+        spans = [(sum(CHUNKS[:c]), sum(CHUNKS[: c + 1])) for c in range(len(CHUNKS))]
+        results = []
+        for c, (lo, hi) in enumerate(spans):
+            width = (hi - lo) * P
+            fuse(PACK - 1, lo, hi)
+            z_grouped = keep.tile([P, width * PACK], BF16, name=f"z_grouped{c}", align_bytes=64)
+            z_codes = keep.tile([P, width], U32, name=f"z_codes{c}", align_bytes=64)
+            z_scales = keep.tile([P, width], U8, name=f"z_scales{c}", align_bytes=64)
+            weave = nc.scalar.copy if c % 2 else nc.vector.tensor_copy
+            weave(
+                z_grouped[:].rearrange("p (g c i j) -> p g c j i", i=PACK, j=PACK, g=hi - lo),
+                z_planes[:, lo:hi].rearrange("p g j (c i) -> p g c j i", i=PACK),
+            )
             quantize(z_codes[:], z_scales[:], z_grouped[:])
-            result = keep.tile([P, PACK, CHUNK], F32, name=f"result{c}")
-            for half in range(2):
-                b = 2 * c + half
-                bank = psum.tile([P, 2, CHUNK], F32, name=f"out_bank{b}", tag=f"bank{b}")
-                for u in range(2):
-                    cols = slice((2 * half + u) * P, (2 * half + u + 1) * P)
+            result = keep.tile([P, PACK, width], F32, name=f"result{c}")
+            per_bank = PACK // (hi - lo)
+            for b in range(lo, hi):
+                bank = psum.tile([P, per_bank, width], F32, name=f"out_bank{b}", tag=f"bank{b}")
+                first = (b - lo) * per_bank
+                for u in range(per_bank):
+                    cols = slice((first + u) * P, (first + u + 1) * P)
                     nc.tensor.matmul_mx(
                         out=bank[:, u, :], lhsT=w_codes[1][:, cols].bitcast(FP8X4), lhsT_scale=w_scales[1][:, cols],
                         rhs=z_codes[:].bitcast(FP8X4), rhs_scale=z_scales[:], start=True, stop=True,
                     )
-                nc.scalar.copy(result[:, 2 * half : 2 * half + 2, :], bank[:])
-            nc.sync.dma_start(out_rows[:, :, cells], result[:])
-            out_grouped = keep.tile([P, CHUNK * PACK], BF16, name=f"out_grouped{c}", align_bytes=64)
-            nc.vector.tensor_copy(
-                out_grouped[:].rearrange("p (r t) -> p r t", t=PACK), result[:].rearrange("p t r -> p r t")
-            )
+                nc.scalar.copy(result[:, first : first + per_bank, :], bank[:])
+            results.append(result)
+        for c, (lo, hi) in enumerate(spans):
+            cells = slice(lo * P, hi * P)
+            nc.sync.dma_start(out_rows[:, :, cells], results[c][:])
+            out_grouped = keep.tile([P, (hi - lo) * P * PACK], BF16, name=f"out_grouped{c}", align_bytes=64)
+            nc.vector.tensor_copy(*weave_views(out_grouped[:], results[c][:]))
             quantize(out_codes[:, cells], out_scales[:, cells], out_grouped[:])
             nc.sync.dma_start(out_words[:, cells], out_codes[:, cells].bitcast(I32))
         for q in range(P // 32):
-            nc.sync.dma_start(
+            queue = nc.scalar if q % 2 else nc.sync
+            queue.dma_start(
                 out_2[0, 4 * q : 4 * q + 4, :].bitcast(I32), out_scales[32 * q : 32 * q + 4, :].bitcast(I32)
             )

@@ -15,6 +15,8 @@ FP8X4 = mybir.dt.float8_e4m3fn_x4
 RELU = mybir.ActivationFunctionType.Relu
 COPY = mybir.ActivationFunctionType.Copy
 MAX = mybir.AluOpType.max
+ADD = mybir.AluOpType.add
+SUBTRACT = mybir.AluOpType.subtract
 
 P = 128
 PACK = 4
@@ -154,9 +156,27 @@ def tile_picked_bev_max_lo_kernel(
             a_map, e_map = (maps[s][t][:, lo * P : hi * P].rearrange("p (g r) -> p g r", r=P) for s in range(2))
             nc.vector.tensor_tensor(z_planes[:, lo:hi, t, :], a_map, e_map, MAX)
 
+        def fuse_aside(t, lo, hi):
+            cells = slice(lo * P, hi * P)
+            gap = keep.tile([P, (hi - lo) * P], F32, name=f"gap{t}_{lo}")
+            excess = keep.tile([P, (hi - lo) * P], F32, name=f"excess{t}_{lo}")
+            nc.gpsimd.tensor_tensor(gap[:], maps[1][t][:, cells], maps[0][t][:, cells], SUBTRACT)
+            nc.scalar.activation(excess[:], gap[:], RELU)
+            return lambda: nc.gpsimd.tensor_tensor(
+                z_planes[:, lo:hi, t, :],
+                maps[0][t][:, cells].rearrange("p (g r) -> p g r", r=P),
+                excess[:].rearrange("p (g r) -> p g r", r=P),
+                ADD,
+            )
+
+        half = S // P // 2
         for t in range(PACK - 1):
             scatter(1, t)
-            fuse(t, 0, S // P)
+            if t < 2:
+                for finish in [fuse_aside(t, 0, half), fuse_aside(t, half, 2 * half)]:
+                    finish()
+            else:
+                fuse(t, 0, S // P)
         scatter(1, PACK - 1)
 
         out_rows = out_0.rearrange("(p t) c -> p t c", t=PACK)

@@ -121,100 +121,102 @@ def tile_picked_bev_max_lo_kernel(
         w_codes = [keep.tile([P, H], U32, name=f"w_codes{i}", align_bytes=64) for i in range(2)]
         w_scales = [keep.tile([P, H], U8, name=f"w_scales{i}", align_bytes=64) for i in range(2)]
 
-        def prepare(i, tag):
+        def prepare(i, tag, parts):
             grouped = keep.tile([P, H * PACK], BF16, name=f"w_grouped{i}", tag=tag, align_bytes=64)
             nc.scalar.copy(
                 grouped[:].rearrange("p (t m j) -> p m j t", t=PACK, j=PACK),
                 w_raw[i + 1][:].rearrange("p j (m t) -> p m j t", t=PACK),
             )
-            quantize(w_codes[i][:], w_scales[i][:], grouped[:])
+            for lo in range(0, H, H // parts):
+                hi = lo + H // parts
+                quantize(w_codes[i][:, lo:hi], w_scales[i][:, lo:hi], grouped[:, lo * PACK : hi * PACK])
 
         first_products(0, 1, picked[1][:, PACK - 1, :])
         gather(1, PACK - 1, 0, V)
         activate(0, 0)
-        scatter(0, 0)
         first_products(1, 1, keep.tile([P, P * PACK], BF16, name="w1_grouped1", align_bytes=64)[:])
         activate(0, 1)
+        scatter(0, 0)
         scatter(0, 1)
-        first_products(2, 2, keep.tile([P, 2 * P * PACK], BF16, name="w1_grouped2", tag="w1_codes0", align_bytes=64)[:])
         x_grouped.append(keep.tile([P, V * PACK], BF16, name="x_grouped1", tag="w1_codes1", align_bytes=64))
         nc.scalar.copy(*x_views(1, 0, V))
         quantize(x_codes[1][:], x_scales[1][:], x_grouped[1][:])
-        activate(0, 2)
-        scatter(0, 2)
-        prepare(0, "w1_scales0")
-        activate(0, 3)
-        scatter(0, 3)
-        prepare(1, "w3_grouped")
+        prepare(0, "w1_scales1", 2)
         for t in range(PACK):
             product(1, t, w_codes[0][:, t * P : (t + 1) * P], w_scales[0][:, t * P : (t + 1) * P])
-            activate(1, t)
+        first_products(2, 2, keep.tile([P, 2 * P * PACK], BF16, name="w1_grouped2", tag="w1_codes0", align_bytes=64)[:])
+        prepare(1, "w3_grouped", 1)
+        remaining = [(1, 0), (1, 1), (0, 2), (1, 2), (0, 3), (1, 3)]
+        for s, t in remaining:
+            activate(s, t)
+        for s, t in remaining:
+            scatter(s, t)
 
-        z_planes = keep.tile([P, S // P, PACK, P], BF16, name="z_planes")
+        z_words = keep.tile([P, S // P, 2, P], F32, name="z_words")
+
+        def slot(t, lo, hi):
+            pairs = z_words[:, lo:hi, t // 2, :].bitcast(BF16)
+            return pairs.rearrange("p g (r e) -> p g r e", e=2)[:, :, :, t % 2]
+
+        def by_group(ap):
+            return ap.rearrange("p (g r) -> p g r", r=P)
 
         def fuse(t, lo, hi):
-            a_map, e_map = (maps[s][t][:, lo * P : hi * P].rearrange("p (g r) -> p g r", r=P) for s in range(2))
-            nc.vector.tensor_tensor(z_planes[:, lo:hi, t, :], a_map, e_map, MAX)
+            a_map, e_map = (by_group(maps[s][t][:, lo * P : hi * P]) for s in range(2))
+            nc.vector.tensor_tensor(slot(t, lo, hi), a_map, e_map, MAX)
 
         def fuse_aside(t, lo, hi):
             cells = slice(lo * P, hi * P)
-            gap = keep.tile([P, (hi - lo) * P], F32, name=f"gap{t}_{lo}")
-            excess = keep.tile([P, (hi - lo) * P], F32, name=f"excess{t}_{lo}")
+            gap = keep.tile([P, (hi - lo) * P], F32, name="gap", bufs=2)
+            excess = z_words[:, lo:hi, (t + 1) // 2, :]
             nc.gpsimd.tensor_tensor(gap[:], maps[1][t][:, cells], maps[0][t][:, cells], SUBTRACT)
-            nc.scalar.activation(excess[:], gap[:], RELU)
-            return lambda: nc.gpsimd.tensor_tensor(
-                z_planes[:, lo:hi, t, :],
-                maps[0][t][:, cells].rearrange("p (g r) -> p g r", r=P),
-                excess[:].rearrange("p (g r) -> p g r", r=P),
-                ADD,
-            )
+            nc.scalar.activation(excess, by_group(gap[:]), RELU)
+            return lambda: nc.gpsimd.tensor_tensor(slot(t, lo, hi), by_group(maps[0][t][:, cells]), excess, ADD)
 
         half = S // P // 2
         for t in range(PACK - 1):
-            scatter(1, t)
-            if t < 2:
-                for finish in [fuse_aside(t, 0, half), fuse_aside(t, half, 2 * half)]:
-                    finish()
-            else:
-                fuse(t, 0, S // P)
-        scatter(1, PACK - 1)
+            for finish in [fuse_aside(t, 0, half), fuse_aside(t, half, 2 * half)]:
+                finish()
 
         out_rows = out_0.rearrange("(p t) c -> p t c", t=PACK)
         out_words = out_1[0].rearrange("p c r -> p (c r)").bitcast(I32)
         out_codes = keep.tile([P, S], U32, name="out_codes", align_bytes=64)
         out_scales = keep.tile([P, S], U8, name="out_scales", align_bytes=64)
         spans = [(sum(CHUNKS[:c]), sum(CHUNKS[: c + 1])) for c in range(len(CHUNKS))]
-        results = []
+        out_banks = []
         for c, (lo, hi) in enumerate(spans):
             width = (hi - lo) * P
             fuse(PACK - 1, lo, hi)
             z_grouped = keep.tile([P, width * PACK], BF16, name=f"z_grouped{c}", align_bytes=64)
             z_codes = keep.tile([P, width], U32, name=f"z_codes{c}", align_bytes=64)
             z_scales = keep.tile([P, width], U8, name=f"z_scales{c}", align_bytes=64)
-            weave = nc.scalar.copy if c % 2 else nc.vector.tensor_copy
+            weave = nc.scalar.copy if c else nc.vector.tensor_copy
             weave(
-                z_grouped[:].rearrange("p (g c i j) -> p g c j i", i=PACK, j=PACK, g=hi - lo),
-                z_planes[:, lo:hi].rearrange("p g j (c i) -> p g c j i", i=PACK),
+                z_grouped[:].bitcast(F32).rearrange("p (g r u) -> p g r u", u=2, r=P),
+                z_words[:, lo:hi].rearrange("p g u r -> p g r u"),
             )
             quantize(z_codes[:], z_scales[:], z_grouped[:])
-            result = keep.tile([P, PACK, width], F32, name=f"result{c}")
             per_bank = PACK // (hi - lo)
             for b in range(lo, hi):
                 bank = psum.tile([P, per_bank, width], F32, name=f"out_bank{b}", tag=f"bank{b}")
-                first = (b - lo) * per_bank
                 for u in range(per_bank):
-                    cols = slice((first + u) * P, (first + u + 1) * P)
+                    t = (b - lo) * per_bank + u
+                    cols = slice(t * P, (t + 1) * P)
                     nc.tensor.matmul_mx(
                         out=bank[:, u, :], lhsT=w_codes[1][:, cols].bitcast(FP8X4), lhsT_scale=w_scales[1][:, cols],
                         rhs=z_codes[:].bitcast(FP8X4), rhs_scale=z_scales[:], start=True, stop=True,
                     )
-                nc.scalar.copy(result[:, first : first + per_bank, :], bank[:])
-            results.append(result)
-        for c, (lo, hi) in enumerate(spans):
+                out_banks.append(bank)
+        for lo, hi in spans:
             cells = slice(lo * P, hi * P)
-            nc.sync.dma_start(out_rows[:, :, cells], results[c][:])
-            out_grouped = keep.tile([P, (hi - lo) * P * PACK], BF16, name=f"out_grouped{c}", align_bytes=64)
-            nc.vector.tensor_copy(*weave_views(out_grouped[:], results[c][:]))
+            per_bank = PACK // (hi - lo)
+            result = keep.tile([P, PACK, (hi - lo) * P], F32, name=f"result{lo}")
+            for b in range(lo, hi):
+                first = (b - lo) * per_bank
+                nc.scalar.copy(result[:, first : first + per_bank, :], out_banks[b][:])
+            nc.sync.dma_start(out_rows[:, :, cells], result[:])
+            out_grouped = keep.tile([P, (hi - lo) * P * PACK], BF16, name=f"out_grouped{lo}", align_bytes=64)
+            nc.vector.tensor_copy(*weave_views(out_grouped[:], result[:]))
             quantize(out_codes[:, cells], out_scales[:, cells], out_grouped[:])
             nc.sync.dma_start(out_words[:, cells], out_codes[:, cells].bitcast(I32))
         for q in range(P // 32):

@@ -16,6 +16,7 @@ RELU = mybir.ActivationFunctionType.Relu
 COPY = mybir.ActivationFunctionType.Copy
 MAX = mybir.AluOpType.max
 ADD = mybir.AluOpType.add
+MULT = mybir.AluOpType.mult
 SUBTRACT = mybir.AluOpType.subtract
 
 P = 128
@@ -93,21 +94,25 @@ def tile_picked_bev_max_lo_kernel(
         quantize(x_codes[0][:], x_scales[0][:], x_grouped[0][:])
 
         banks = [psum.tile([P, V], F32, name=f"bank{b}", tag=f"bank{b}") for b in range(2 * PACK)]
-        acts = [[keep.tile([P, V], F32, name=f"act{s}_{t}") for t in range(PACK)] for s in range(2)]
+        acts = [
+            [keep.tile([P, V], F32, name=f"act{s}_{t}", tag=f"act{s}_{t}", align_bytes=64) for t in range(PACK)]
+            for s in range(2)
+        ]
 
-        def product(s, t, codes, scales):
+        def product(s, bank, codes, scales, lo, hi):
             nc.tensor.matmul_mx(
-                out=banks[s * PACK + t][:], lhsT=codes.bitcast(FP8X4), lhsT_scale=scales,
-                rhs=x_codes[s][:].bitcast(FP8X4), rhs_scale=x_scales[s][:], start=True, stop=True,
+                out=bank[:, lo:hi], lhsT=codes.bitcast(FP8X4), lhsT_scale=scales,
+                rhs=x_codes[s][:, lo:hi].bitcast(FP8X4), rhs_scale=x_scales[s][:, lo:hi], start=True, stop=True,
             )
 
-        def activate(s, t):
-            nc.scalar.activation(acts[s][t][:], banks[s * PACK + t][:], RELU)
+        def activate(s, t, bank, lo, hi):
+            nc.scalar.activation(acts[s][t][:, lo:hi], bank[:, lo:hi], RELU)
 
-        def scatter(s, t):
-            nc.vector.tensor_copy(maps[s][t][:].indirect(cell_lists[s][:]), acts[s][t][:])
+        def scatter(s, t, lo, hi):
+            entries = cell_lists[s][:, lo // LIST_ROWS : hi // LIST_ROWS]
+            nc.vector.tensor_copy(maps[s][t][:].indirect(entries), acts[s][t][:, lo:hi])
 
-        def first_products(t0, n, grouped):
+        def first_weights(t0, n, grouped):
             codes = keep.tile([P, n * P], U32, name=f"w1_codes{t0}", tag=f"w1_codes{t0}", align_bytes=64)
             scales = keep.tile([P, n * P], U8, name=f"w1_scales{t0}", tag=f"w1_scales{t0}", align_bytes=64)
             nc.scalar.copy(
@@ -115,42 +120,59 @@ def tile_picked_bev_max_lo_kernel(
                 w_raw[0][:].rearrange("p j (m t) -> p m j t", t=PACK)[:, :, :, t0 : t0 + n],
             )
             quantize(codes[:], scales[:], grouped)
-            for u in range(n):
-                product(0, t0 + u, codes[:, u * P : (u + 1) * P], scales[:, u * P : (u + 1) * P])
+            return codes, scales
 
-        w_codes = [keep.tile([P, H], U32, name=f"w_codes{i}", align_bytes=64) for i in range(2)]
-        w_scales = [keep.tile([P, H], U8, name=f"w_scales{i}", align_bytes=64) for i in range(2)]
-
-        def prepare(i, tag, parts):
-            grouped = keep.tile([P, H * PACK], BF16, name=f"w_grouped{i}", tag=tag, align_bytes=64)
-            nc.scalar.copy(
-                grouped[:].rearrange("p (t m j) -> p m j t", t=PACK, j=PACK),
-                w_raw[i + 1][:].rearrange("p j (m t) -> p m j t", t=PACK),
-            )
-            for lo in range(0, H, H // parts):
-                hi = lo + H // parts
-                quantize(w_codes[i][:, lo:hi], w_scales[i][:, lo:hi], grouped[:, lo * PACK : hi * PACK])
-
-        first_products(0, 1, picked[1][:, PACK - 1, :])
+        halves = [(banks[0], 0, V // 2), (banks[PACK], V // 2, V)]
+        codes, scales = first_weights(0, 1, picked[1][:, PACK - 1, :])
+        for bank, lo, hi in halves:
+            product(0, bank, codes[:], scales[:], lo, hi)
         gather(1, PACK - 1, 0, V)
-        activate(0, 0)
-        first_products(1, 1, keep.tile([P, P * PACK], BF16, name="w1_grouped1", align_bytes=64)[:])
-        activate(0, 1)
-        scatter(0, 0)
-        scatter(0, 1)
+        for bank, lo, hi in halves:
+            activate(0, 0, bank, lo, hi)
+        codes, scales = first_weights(1, 1, keep.tile([P, P * PACK], BF16, name="w1_grouped1", align_bytes=64)[:])
+        product(0, banks[1], codes[:], scales[:], 0, V)
+        activate(0, 1, banks[1], 0, V)
+        for bank, lo, hi in halves:
+            scatter(0, 0, lo, hi)
+        scatter(0, 1, 0, V)
+
+        w3_grouped = keep.tile([P, H * PACK], BF16, name="w3_grouped", align_bytes=64)
+        nc.gpsimd.tensor_scalar(
+            w3_grouped[:].rearrange("p (t m j) -> p t m j", t=PACK, j=PACK),
+            w_raw[2][:].rearrange("p j (m t) -> p t m j", t=PACK),
+            1.0, 0.0, MULT, ADD,
+        )
+
         x_grouped.append(keep.tile([P, V * PACK], BF16, name="x_grouped1", tag="w1_codes1", align_bytes=64))
         nc.scalar.copy(*x_views(1, 0, V))
         quantize(x_codes[1][:], x_scales[1][:], x_grouped[1][:])
-        prepare(0, "w1_scales1", 2)
+        w2_grouped = keep.tile([P, H * PACK], BF16, name="w2_grouped", tag="w1_scales1", align_bytes=64)
+        w2_codes = keep.tile([P, H], U32, name="w2_codes", align_bytes=64)
+        w2_scales = keep.tile([P, H], U8, name="w2_scales", align_bytes=64)
+        nc.scalar.copy(
+            w2_grouped[:].rearrange("p (t m j) -> p m j t", t=PACK, j=PACK),
+            w_raw[1][:].rearrange("p j (m t) -> p m j t", t=PACK),
+        )
+        for lo in range(0, H, H // 2):
+            hi = lo + H // 2
+            quantize(w2_codes[:, lo:hi], w2_scales[:, lo:hi], w2_grouped[:, lo * PACK : hi * PACK])
         for t in range(PACK):
-            product(1, t, w_codes[0][:, t * P : (t + 1) * P], w_scales[0][:, t * P : (t + 1) * P])
-        first_products(2, 2, keep.tile([P, 2 * P * PACK], BF16, name="w1_grouped2", tag="w1_codes0", align_bytes=64)[:])
-        prepare(1, "w3_grouped", 1)
+            cols = slice(t * P, (t + 1) * P)
+            product(1, banks[PACK + t], w2_codes[:, cols], w2_scales[:, cols], 0, V)
+        w3_codes = keep.tile([P, H], U32, name="w3_codes", tag="w1_scales1", align_bytes=64)
+        w3_scales = keep.tile([P, H], U8, name="w3_scales", align_bytes=64)
+        quantize(w3_codes[:], w3_scales[:], w3_grouped[:])
+        codes, scales = first_weights(
+            2, 2, keep.tile([P, 2 * P * PACK], BF16, name="w1_grouped2", tag="act0_0", align_bytes=64)[:]
+        )
+        for u in range(2):
+            cols = slice(u * P, (u + 1) * P)
+            product(0, banks[2 + u], codes[:, cols], scales[:, cols], 0, V)
         remaining = [(1, 0), (1, 1), (0, 2), (1, 2), (0, 3), (1, 3)]
         for s, t in remaining:
-            activate(s, t)
+            activate(s, t, banks[s * PACK + t], 0, V)
         for s, t in remaining:
-            scatter(s, t)
+            scatter(s, t, 0, V)
 
         z_words = keep.tile([P, S // P, 2, P], F32, name="z_words")
 
@@ -203,7 +225,7 @@ def tile_picked_bev_max_lo_kernel(
                     t = (b - lo) * per_bank + u
                     cols = slice(t * P, (t + 1) * P)
                     nc.tensor.matmul_mx(
-                        out=bank[:, u, :], lhsT=w_codes[1][:, cols].bitcast(FP8X4), lhsT_scale=w_scales[1][:, cols],
+                        out=bank[:, u, :], lhsT=w3_codes[:, cols].bitcast(FP8X4), lhsT_scale=w3_scales[:, cols],
                         rhs=z_codes[:].bitcast(FP8X4), rhs_scale=z_scales[:], start=True, stop=True,
                     )
                 out_banks.append(bank)

@@ -23,6 +23,8 @@ P = 128
 PACK = 4
 CHUNKS = (1, 2, 2, 2, 1)
 LIST_ROWS = 16
+FILL = 320
+EARLY = 5
 
 
 def tile_picked_bev_max_lo_kernel(
@@ -38,10 +40,11 @@ def tile_picked_bev_max_lo_kernel(
         cell_lists = [lists.tile([P, V // LIST_ROWS], U16, name=f"cells{s}") for s in range(2)]
         x_rows = xT.rearrange("(p j) c -> p j c", j=PACK)
         x_planes = [keep.tile([P, T], F32, name=f"x{j}") for j in range(PACK)]
-        w_raw = [keep.tile([P, PACK, H], F32, name=f"w_raw{i}") for i in range(3)]
+        w_raw = [keep.tile([P, PACK, H], F32, name=f"w_raw{i}", tag=f"w_raw{i}", align_bytes=64) for i in range(3)]
 
+        nc.sync.dma_start(x_planes[0][:], x_rows[:, 0, :])
         nc.sync.dma_start(offs_sb[:], offs)
-        for j in range(PACK):
+        for j in range(1, PACK):
             nc.sync.dma_start(x_planes[j][:], x_rows[:, j, :])
         nc.sync.dma_start(w_raw[0][:], w1.rearrange("(p j) c -> p j c", j=PACK))
         nc.sync.dma_start(cell_lists[0][:], near)
@@ -63,7 +66,7 @@ def tile_picked_bev_max_lo_kernel(
         def quantize(codes, scales, grouped):
             nc.vector.quantize_mx(out=codes.bitcast(FP8X4), scales=scales, in_=grouped)
 
-        picked = [keep.tile([P, PACK, V], BF16, name=f"picked{s}", align_bytes=64) for s in range(2)]
+        picked = {1: keep.tile([P, PACK + 1, V], BF16, name="picked1", align_bytes=64)}
         x_grouped = [keep.tile([P, V * PACK], BF16, name="x_grouped0", align_bytes=64)]
         x_codes = [keep.tile([P, V], U32, name=f"x_codes{s}", align_bytes=64) for s in range(2)]
         x_scales = [keep.tile([P, V], U8, name=f"x_scales{s}", align_bytes=64) for s in range(2)]
@@ -79,25 +82,27 @@ def tile_picked_bev_max_lo_kernel(
             nc.scalar.activation(picked[s][:, j, :], rounded[:].indirect(entries), COPY)
 
         def x_views(s, lo, hi):
-            return weave_views(x_grouped[s][:, lo * PACK : hi * PACK], picked[s][:, :, lo:hi])
+            return weave_views(x_grouped[s][:, lo * PACK : hi * PACK], picked[s][:, :PACK, lo:hi])
+
+        def gather_in_place(j, lo, hi):
+            entries = offs_sb[:, lo // LIST_ROWS : hi // LIST_ROWS]
+            slots = x_grouped[0][:].rearrange("p (c j) -> p c j", j=PACK)
+            nc.vector.tensor_copy(slots[:, lo:hi, j], x_planes[j][:].indirect(entries))
 
         for j in range(PACK - 1):
-            gather(0, j, 0, V)
+            gather_in_place(j, 0, V)
             if j < 2:
                 gather_rounded(1, j)
             else:
                 gather(1, j, 0, V)
-        gather(0, PACK - 1, 0, V // 2)
-        nc.scalar.copy(*x_views(0, 0, V // 2))
-        gather(0, PACK - 1, V // 2, V)
-        nc.vector.tensor_copy(*x_views(0, V // 2, V))
-        quantize(x_codes[0][:], x_scales[0][:], x_grouped[0][:])
+        for lo in range(0, V, V // 2):
+            gather_in_place(PACK - 1, lo, lo + V // 2)
+        for lo in range(0, V, V // 2):
+            hi = lo + V // 2
+            quantize(x_codes[0][:, lo:hi], x_scales[0][:, lo:hi], x_grouped[0][:, lo * PACK : hi * PACK])
 
         banks = [psum.tile([P, V], F32, name=f"bank{b}", tag=f"bank{b}") for b in range(2 * PACK)]
-        acts = [
-            [keep.tile([P, V], F32, name=f"act{s}_{t}", tag=f"act{s}_{t}", align_bytes=64) for t in range(PACK)]
-            for s in range(2)
-        ]
+        acts = {}
 
         def product(s, bank, codes, scales, lo, hi):
             nc.tensor.matmul_mx(
@@ -105,79 +110,49 @@ def tile_picked_bev_max_lo_kernel(
                 rhs=x_codes[s][:, lo:hi].bitcast(FP8X4), rhs_scale=x_scales[s][:, lo:hi], start=True, stop=True,
             )
 
-        def activate(s, t, bank, lo, hi):
-            nc.scalar.activation(acts[s][t][:, lo:hi], bank[:, lo:hi], RELU)
+        def activate(s, t, bank, lo, hi, tag=None, into=None):
+            if into is None:
+                name = f"act{s}_{t}_{lo}"
+                into = keep.tile([P, hi - lo], F32, name=name, tag=tag or name, align_bytes=64)[:]
+            acts[s, t, lo] = into
+            nc.scalar.activation(into, bank[:, lo:hi], RELU)
 
         def scatter(s, t, lo, hi):
             entries = cell_lists[s][:, lo // LIST_ROWS : hi // LIST_ROWS]
-            nc.vector.tensor_copy(maps[s][t][:].indirect(entries), acts[s][t][:, lo:hi])
+            nc.vector.tensor_copy(maps[s][t][:].indirect(entries), acts[s, t, lo])
 
-        def first_weights(t0, n, grouped):
-            codes = keep.tile([P, n * P], U32, name=f"w1_codes{t0}", tag=f"w1_codes{t0}", align_bytes=64)
-            scales = keep.tile([P, n * P], U8, name=f"w1_scales{t0}", tag=f"w1_scales{t0}", align_bytes=64)
-            nc.scalar.copy(
+        def deal(i, t0, n, grouped, copy=nc.scalar.copy):
+            copy(
                 grouped.rearrange("p (t m j) -> p m j t", t=n, j=PACK),
-                w_raw[0][:].rearrange("p j (m t) -> p m j t", t=PACK)[:, :, :, t0 : t0 + n],
+                w_raw[i][:].rearrange("p j (m t) -> p m j t", t=PACK)[:, :, :, t0 : t0 + n],
             )
+
+        def deal_aside(i, grouped):
+            nc.gpsimd.tensor_scalar(
+                grouped.rearrange("p (t m j) -> p t m j", t=PACK, j=PACK),
+                w_raw[i][:].rearrange("p j (m t) -> p t m j", t=PACK),
+                1.0, 0.0, MULT, ADD,
+            )
+
+        def quantized(name, grouped, width, tag=None):
+            codes = keep.tile([P, width], U32, name=f"{name}_codes", tag=tag or f"{name}_codes", align_bytes=64)
+            scales = keep.tile([P, width], U8, name=f"{name}_scales", tag=f"{name}_scales", align_bytes=64)
             quantize(codes[:], scales[:], grouped)
             return codes, scales
 
-        halves = [(banks[0], 0, V // 2), (banks[PACK], V // 2, V)]
-        codes, scales = first_weights(0, 1, picked[1][:, PACK - 1, :])
-        for bank, lo, hi in halves:
-            product(0, bank, codes[:], scales[:], lo, hi)
-        gather(1, PACK - 1, 0, V)
-        for bank, lo, hi in halves:
-            activate(0, 0, bank, lo, hi)
-        codes, scales = first_weights(1, 1, keep.tile([P, P * PACK], BF16, name="w1_grouped1", align_bytes=64)[:])
-        product(0, banks[1], codes[:], scales[:], 0, V)
-        activate(0, 1, banks[1], 0, V)
-        for bank, lo, hi in halves:
-            scatter(0, 0, lo, hi)
-        scatter(0, 1, 0, V)
+        def buffer(name, width, tag=None):
+            return keep.tile([P, width * PACK], BF16, name=name, tag=tag or name, align_bytes=64)
 
-        w3_grouped = keep.tile([P, H * PACK], BF16, name="w3_grouped", align_bytes=64)
-        nc.gpsimd.tensor_scalar(
-            w3_grouped[:].rearrange("p (t m j) -> p t m j", t=PACK, j=PACK),
-            w_raw[2][:].rearrange("p j (m t) -> p t m j", t=PACK),
-            1.0, 0.0, MULT, ADD,
-        )
+        z_parts = [
+            keep.tile([P, groups, 2, P], F32, name=f"z_words{i}", tag=f"z_words{i}", align_bytes=64)
+            for i, groups in enumerate((EARLY, S // P - EARLY))
+        ]
 
-        x_grouped.append(keep.tile([P, V * PACK], BF16, name="x_grouped1", tag="w1_codes1", align_bytes=64))
-        nc.scalar.copy(*x_views(1, 0, V))
-        quantize(x_codes[1][:], x_scales[1][:], x_grouped[1][:])
-        w2_grouped = keep.tile([P, H * PACK], BF16, name="w2_grouped", tag="w1_scales1", align_bytes=64)
-        w2_codes = keep.tile([P, H], U32, name="w2_codes", align_bytes=64)
-        w2_scales = keep.tile([P, H], U8, name="w2_scales", align_bytes=64)
-        nc.scalar.copy(
-            w2_grouped[:].rearrange("p (t m j) -> p m j t", t=PACK, j=PACK),
-            w_raw[1][:].rearrange("p j (m t) -> p m j t", t=PACK),
-        )
-        for lo in range(0, H, H // 2):
-            hi = lo + H // 2
-            quantize(w2_codes[:, lo:hi], w2_scales[:, lo:hi], w2_grouped[:, lo * PACK : hi * PACK])
-        for t in range(PACK):
-            cols = slice(t * P, (t + 1) * P)
-            product(1, banks[PACK + t], w2_codes[:, cols], w2_scales[:, cols], 0, V)
-        w3_codes = keep.tile([P, H], U32, name="w3_codes", tag="w1_scales1", align_bytes=64)
-        w3_scales = keep.tile([P, H], U8, name="w3_scales", align_bytes=64)
-        quantize(w3_codes[:], w3_scales[:], w3_grouped[:])
-        codes, scales = first_weights(
-            2, 2, keep.tile([P, 2 * P * PACK], BF16, name="w1_grouped2", tag="act0_0", align_bytes=64)[:]
-        )
-        for u in range(2):
-            cols = slice(u * P, (u + 1) * P)
-            product(0, banks[2 + u], codes[:, cols], scales[:, cols], 0, V)
-        remaining = [(1, 0), (1, 1), (0, 2), (1, 2), (0, 3), (1, 3)]
-        for s, t in remaining:
-            activate(s, t, banks[s * PACK + t], 0, V)
-        for s, t in remaining:
-            scatter(s, t, 0, V)
-
-        z_words = keep.tile([P, S // P, 2, P], F32, name="z_words")
+        def z_words(lo, hi):
+            return z_parts[0][:, lo:hi] if lo < EARLY else z_parts[1][:, lo - EARLY : hi - EARLY]
 
         def slot(t, lo, hi):
-            pairs = z_words[:, lo:hi, t // 2, :].bitcast(BF16)
+            pairs = z_words(lo, hi)[:, :, t // 2, :].bitcast(BF16)
             return pairs.rearrange("p g (r e) -> p g r e", e=2)[:, :, :, t % 2]
 
         def by_group(ap):
@@ -187,37 +162,99 @@ def tile_picked_bev_max_lo_kernel(
             a_map, e_map = (by_group(maps[s][t][:, lo * P : hi * P]) for s in range(2))
             nc.vector.tensor_tensor(slot(t, lo, hi), a_map, e_map, MAX)
 
-        def fuse_aside(t, lo, hi):
+        def fuse_aside(t, lo, hi, gap):
             cells = slice(lo * P, hi * P)
-            gap = keep.tile([P, (hi - lo) * P], F32, name="gap", bufs=2)
-            excess = z_words[:, lo:hi, (t + 1) // 2, :]
-            nc.gpsimd.tensor_tensor(gap[:], maps[1][t][:, cells], maps[0][t][:, cells], SUBTRACT)
-            nc.scalar.activation(excess, by_group(gap[:]), RELU)
+            excess = z_words(lo, hi)[:, :, (t + 1) // 2, :]
+            nc.gpsimd.tensor_tensor(gap[:, cells], maps[1][t][:, cells], maps[0][t][:, cells], SUBTRACT)
+            nc.scalar.activation(excess, by_group(gap[:, cells]), RELU)
             return lambda: nc.gpsimd.tensor_tensor(slot(t, lo, hi), by_group(maps[0][t][:, cells]), excess, ADD)
 
-        half = S // P // 2
-        for t in range(PACK - 1):
-            for finish in [fuse_aside(t, 0, half), fuse_aside(t, half, 2 * half)]:
+
+        def fuse_slot(t, lo, mid):
+            gap = keep.tile([P, S], F32, name=f"gap{t}", tag="aside", align_bytes=64)
+            for finish in [fuse_aside(t, lo, mid, gap), fuse_aside(t, mid, S // P, gap)]:
                 finish()
+
+        def tile_of(pair, u):
+            return [operand[:, u * P : (u + 1) * P] for operand in pair]
+
+        half = V // 2
+        grouped = picked[1][:, PACK - 1 :, :].rearrange("p a c -> p (a c)")
+        deal(0, 0, 2, grouped, nc.vector.tensor_copy)
+        first = quantized("w1_first", grouped, 2 * P)
+        halves = [(banks[0], 0, half), (banks[2 * PACK - 1], half, V)]
+        for bank, lo, hi in halves:
+            product(0, bank, *tile_of(first, 0), lo, hi)
+        gather(1, PACK - 1, 0, V)
+        product(0, banks[1], *tile_of(first, 1), 0, V)
+        grouped = buffer("w1_grouped_last", 2 * P, "aside")
+        deal(0, 2, 2, grouped[:])
+        last = quantized("w1_last", grouped[:], 2 * P)
+        first_acts = keep.tile([P, V], F32, name="first_acts", align_bytes=64)
+        for bank, lo, hi in halves:
+            activate(0, 0, bank, lo, hi, into=first_acts[:, lo:hi])
+        acts[0, 0, 0] = first_acts[:]
+        scatter(0, 0, 0, V)
+
+        x_grouped.append(buffer("x_grouped1", V, "w1_first_codes"))
+        nc.scalar.copy(*x_views(1, 0, V))
+        quantize(x_codes[1][:], x_scales[1][:], x_grouped[1][:])
+        grouped = buffer("w2_grouped", H, "aside")
+        deal_aside(1, grouped[:])
+        second = quantized("w2", grouped[:], H)
+        for t in range(PACK - 1):
+            product(1, banks[PACK + t], *tile_of(second, t), 0, V)
+        activate(0, 1, banks[1], 0, FILL, "w_raw1")
+        scatter(0, 1, 0, FILL)
+        grouped = buffer("w3_grouped", H, "aside")
+        deal_aside(2, grouped[:])
+        activate(1, 0, banks[PACK], 0, V)
+        scatter(1, 0, 0, V)
+        w3_codes, w3_scales = quantized("w3", grouped[:], H)
+        late = keep.tile([P, PACK, V], F32, name="late_acts", tag="w_raw2", align_bytes=64)
+        activate(0, 1, banks[1], FILL, V, into=late[:, 0, FILL:])
+        scatter(0, 1, FILL, V)
+        activate(1, 1, banks[PACK + 1], 0, V, into=late[:, 1, :])
+        scatter(1, 1, 0, V)
+        product(0, banks[PACK + 1], *tile_of(last, 0), 0, V)
+        activate(0, 2, banks[PACK + 1], 0, V)
+        activate(1, 2, banks[PACK + 2], 0, V, into=late[:, 2, :])
+        product(0, banks[PACK + 2], *tile_of(last, 1), 0, V)
+        activate(0, 3, banks[PACK + 2], 0, V)
+        product(1, banks[PACK + 1], *tile_of(second, 3), 0, V)
+        activate(1, 3, banks[PACK + 1], 0, V, into=late[:, 3, :])
+        fuse_slot(0, 0, EARLY)
+        fuse_slot(1, 0, EARLY)
+        first_grouped = buffer("z_grouped0", P)
+        first_slots = first_grouped[:].rearrange("p (c t) -> p c t", t=PACK)
+        nc.scalar.copy(first_grouped[:].bitcast(F32).rearrange("p (r u) -> p r u", u=2)[:, :, 0], z_parts[0][:, 0, 0, :])
+        for t in range(2, PACK):
+            for s in range(2):
+                scatter(s, t, 0, V)
+            nc.vector.tensor_tensor(first_slots[:, :, t], maps[0][t][:, :P], maps[1][t][:, :P], MAX)
+            if t < PACK - 1:
+                fuse_slot(t, 1, EARLY)
 
         out_rows = out_0.rearrange("(p t) c -> p t c", t=PACK)
         out_words = out_1[0].rearrange("p c r -> p (c r)").bitcast(I32)
         out_codes = keep.tile([P, S], U32, name="out_codes", align_bytes=64)
         out_scales = keep.tile([P, S], U8, name="out_scales", align_bytes=64)
         spans = [(sum(CHUNKS[:c]), sum(CHUNKS[: c + 1])) for c in range(len(CHUNKS))]
-        out_banks = []
-        for c, (lo, hi) in enumerate(spans):
-            width = (hi - lo) * P
+
+        def regroup(lo, hi, copy):
+            grouped = buffer(f"z_grouped{lo}", (hi - lo) * P)
             fuse(PACK - 1, lo, hi)
-            z_grouped = keep.tile([P, width * PACK], BF16, name=f"z_grouped{c}", align_bytes=64)
-            z_codes = keep.tile([P, width], U32, name=f"z_codes{c}", align_bytes=64)
-            z_scales = keep.tile([P, width], U8, name=f"z_scales{c}", align_bytes=64)
-            weave = nc.scalar.copy if c else nc.vector.tensor_copy
-            weave(
-                z_grouped[:].bitcast(F32).rearrange("p (g r u) -> p g r u", u=2, r=P),
-                z_words[:, lo:hi].rearrange("p g u r -> p g r u"),
+            copy(
+                grouped[:].bitcast(F32).rearrange("p (g r u) -> p g r u", u=2, r=P),
+                z_words(lo, hi).rearrange("p g u r -> p g r u"),
             )
-            quantize(z_codes[:], z_scales[:], z_grouped[:])
+            return grouped
+
+        out_banks = []
+
+        def last_product(lo, hi, grouped):
+            width = (hi - lo) * P
+            z_codes, z_scales = quantized(f"z{lo}", grouped, width)
             per_bank = PACK // (hi - lo)
             for b in range(lo, hi):
                 bank = psum.tile([P, per_bank, width], F32, name=f"out_bank{b}", tag=f"bank{b}")
@@ -229,18 +266,33 @@ def tile_picked_bev_max_lo_kernel(
                         rhs=z_codes[:].bitcast(FP8X4), rhs_scale=z_scales[:], start=True, stop=True,
                     )
                 out_banks.append(bank)
+
+        last_product(0, 1, first_grouped[:])
+        for lo, hi in spans[1:3]:
+            last_product(lo, hi, regroup(lo, hi, nc.vector.tensor_copy)[:])
+        grouped = regroup(EARLY, S // P, nc.vector.tensor_copy)
+        for lo, hi in spans[3:]:
+            last_product(lo, hi, grouped[:, (lo - EARLY) * P * PACK : (hi - EARLY) * P * PACK])
+
+        results = []
         for lo, hi in spans:
             cells = slice(lo * P, hi * P)
             per_bank = PACK // (hi - lo)
-            result = keep.tile([P, PACK, (hi - lo) * P], F32, name=f"result{lo}")
+            result = keep.tile([P, PACK, (hi - lo) * P], F32, name=f"result{lo}", align_bytes=64)
             for b in range(lo, hi):
                 first = (b - lo) * per_bank
                 nc.scalar.copy(result[:, first : first + per_bank, :], out_banks[b][:])
             nc.sync.dma_start(out_rows[:, :, cells], result[:])
-            out_grouped = keep.tile([P, (hi - lo) * P * PACK], BF16, name=f"out_grouped{lo}", align_bytes=64)
-            nc.vector.tensor_copy(*weave_views(out_grouped[:], result[:]))
-            quantize(out_codes[:, cells], out_scales[:, cells], out_grouped[:])
-            nc.sync.dma_start(out_words[:, cells], out_codes[:, cells].bitcast(I32))
+            results.append(result)
+        out_grouped = buffer("out_grouped", S, f"z_grouped{EARLY}")
+        done = 0
+        for (lo, hi), result, upto in zip(spans, results, (0, 0, 4, 6, 8)):
+            nc.vector.tensor_copy(*weave_views(out_grouped[:, lo * P * PACK : hi * P * PACK], result[:]))
+            if upto > done:
+                cells = slice(done * P, upto * P)
+                quantize(out_codes[:, cells], out_scales[:, cells], out_grouped[:, done * P * PACK : upto * P * PACK])
+                nc.sync.dma_start(out_words[:, cells], out_codes[:, cells].bitcast(I32))
+                done = upto
         for q in range(P // 32):
             queue = nc.scalar if q % 2 else nc.sync
             queue.dma_start(

@@ -66,7 +66,7 @@ def tile_picked_bev_max_lo_kernel(
         def quantize(codes, scales, grouped):
             nc.vector.quantize_mx(out=codes.bitcast(FP8X4), scales=scales, in_=grouped)
 
-        picked = {1: keep.tile([P, PACK + 1, V], BF16, name="picked1", align_bytes=64)}
+        picked = [keep.tile([P, PACK + s, V], BF16, name=f"picked{s}", align_bytes=64) for s in range(2)]
         x_grouped = [keep.tile([P, V * PACK], BF16, name="x_grouped0", align_bytes=64)]
         x_codes = [keep.tile([P, V], U32, name=f"x_codes{s}", align_bytes=64) for s in range(2)]
         x_scales = [keep.tile([P, V], U8, name=f"x_scales{s}", align_bytes=64) for s in range(2)]
@@ -84,19 +84,16 @@ def tile_picked_bev_max_lo_kernel(
         def x_views(s, lo, hi):
             return weave_views(x_grouped[s][:, lo * PACK : hi * PACK], picked[s][:, :PACK, lo:hi])
 
-        def gather_in_place(j, lo, hi):
-            entries = offs_sb[:, lo // LIST_ROWS : hi // LIST_ROWS]
-            slots = x_grouped[0][:].rearrange("p (c j) -> p c j", j=PACK)
-            nc.vector.tensor_copy(slots[:, lo:hi, j], x_planes[j][:].indirect(entries))
-
         for j in range(PACK - 1):
-            gather_in_place(j, 0, V)
+            gather(0, j, 0, V)
             if j < 2:
                 gather_rounded(1, j)
             else:
                 gather(1, j, 0, V)
-        for lo in range(0, V, V // 2):
-            gather_in_place(PACK - 1, lo, lo + V // 2)
+        gather(0, PACK - 1, 0, V // 2)
+        nc.scalar.copy(*x_views(0, 0, V // 2))
+        gather(0, PACK - 1, V // 2, V)
+        nc.vector.tensor_copy(*x_views(0, V // 2, V))
         for lo in range(0, V, V // 2):
             hi = lo + V // 2
             quantize(x_codes[0][:, lo:hi], x_scales[0][:, lo:hi], x_grouped[0][:, lo * PACK : hi * PACK])
@@ -167,37 +164,42 @@ def tile_picked_bev_max_lo_kernel(
             excess = z_words(lo, hi)[:, :, (t + 1) // 2, :]
             nc.gpsimd.tensor_tensor(gap[:, cells], maps[1][t][:, cells], maps[0][t][:, cells], SUBTRACT)
             nc.scalar.activation(excess, by_group(gap[:, cells]), RELU)
-            return lambda: nc.gpsimd.tensor_tensor(slot(t, lo, hi), by_group(maps[0][t][:, cells]), excess, ADD)
+
+        def finish_aside(t, lo, hi):
+            excess = z_words(lo, hi)[:, :, (t + 1) // 2, :]
+            nc.gpsimd.tensor_tensor(slot(t, lo, hi), by_group(maps[0][t][:, lo * P : hi * P]), excess, ADD)
 
 
-        def fuse_slot(t, lo, mid):
+        def fuse_slot(t, *cuts):
             gap = keep.tile([P, S], F32, name=f"gap{t}", tag="aside", align_bytes=64)
-            for finish in [fuse_aside(t, lo, mid, gap), fuse_aside(t, mid, S // P, gap)]:
-                finish()
+            fuse_aside(t, 0, EARLY, gap)
+            fuse_aside(t, EARLY, S // P, gap)
+            for lo, hi in zip(cuts, cuts[1:]):
+                finish_aside(t, lo, hi)
 
         def tile_of(pair, u):
             return [operand[:, u * P : (u + 1) * P] for operand in pair]
 
         half = V // 2
         grouped = picked[1][:, PACK - 1 :, :].rearrange("p a c -> p (a c)")
-        deal(0, 0, 2, grouped, nc.vector.tensor_copy)
-        first = quantized("w1_first", grouped, 2 * P)
+        deal(0, 0, 2, grouped)
+        first = quantized("w1_first", grouped[:, : P * PACK], P)
         halves = [(banks[0], 0, half), (banks[2 * PACK - 1], half, V)]
         for bank, lo, hi in halves:
             product(0, bank, *tile_of(first, 0), lo, hi)
         gather(1, PACK - 1, 0, V)
-        product(0, banks[1], *tile_of(first, 1), 0, V)
-        grouped = buffer("w1_grouped_last", 2 * P, "aside")
-        deal(0, 2, 2, grouped[:])
-        last = quantized("w1_last", grouped[:], 2 * P)
-        first_acts = keep.tile([P, V], F32, name="first_acts", align_bytes=64)
         for bank, lo, hi in halves:
-            activate(0, 0, bank, lo, hi, into=first_acts[:, lo:hi])
-        acts[0, 0, 0] = first_acts[:]
-        scatter(0, 0, 0, V)
+            activate(0, 0, bank, lo, hi)
+        scatter(0, 0, 0, half)
+        following = quantized("w1_next", grouped[:, P * PACK :], P, "act0_0_0")
+        product(0, banks[1], *tile_of(following, 0), 0, V)
+        scatter(0, 0, half, V)
 
         x_grouped.append(buffer("x_grouped1", V, "w1_first_codes"))
         nc.scalar.copy(*x_views(1, 0, V))
+        grouped = buffer("w1_grouped_last", 2 * P, "w1_first_scales")
+        deal(0, 2, 2, grouped[:])
+        last = quantized("w1_last", grouped[:], 2 * P)
         quantize(x_codes[1][:], x_scales[1][:], x_grouped[1][:])
         grouped = buffer("w2_grouped", H, "aside")
         deal_aside(1, grouped[:])
@@ -223,17 +225,21 @@ def tile_picked_bev_max_lo_kernel(
         activate(0, 3, banks[PACK + 2], 0, V)
         product(1, banks[PACK + 1], *tile_of(second, 3), 0, V)
         activate(1, 3, banks[PACK + 1], 0, V, into=late[:, 3, :])
-        fuse_slot(0, 0, EARLY)
-        fuse_slot(1, 0, EARLY)
+        fuse_slot(0, 0, EARLY, S // P)
+        fuse_slot(1, 0, EARLY, S // P)
         first_grouped = buffer("z_grouped0", P)
         first_slots = first_grouped[:].rearrange("p (c t) -> p c t", t=PACK)
-        nc.scalar.copy(first_grouped[:].bitcast(F32).rearrange("p (r u) -> p r u", u=2)[:, :, 0], z_parts[0][:, 0, 0, :])
         for t in range(2, PACK):
             for s in range(2):
                 scatter(s, t, 0, V)
-            nc.vector.tensor_tensor(first_slots[:, :, t], maps[0][t][:, :P], maps[1][t][:, :P], MAX)
             if t < PACK - 1:
-                fuse_slot(t, 1, EARLY)
+                fuse_slot(t, 0, 1, EARLY, S // P)
+        nc.scalar.copy(
+            first_grouped[:].bitcast(F32).rearrange("p (r u) -> p r u", u=2),
+            z_parts[0][:, 0].rearrange("p u r -> p r u"),
+        )
+        last_maps = [maps[s][PACK - 1][:, :P] for s in range(2)]
+        nc.vector.tensor_tensor(first_slots[:, :, PACK - 1], *last_maps, MAX)
 
         out_rows = out_0.rearrange("(p t) c -> p t c", t=PACK)
         out_words = out_1[0].rearrange("p c r -> p (c r)").bitcast(I32)
@@ -269,7 +275,7 @@ def tile_picked_bev_max_lo_kernel(
 
         last_product(0, 1, first_grouped[:])
         for lo, hi in spans[1:3]:
-            last_product(lo, hi, regroup(lo, hi, nc.vector.tensor_copy)[:])
+            last_product(lo, hi, regroup(lo, hi, nc.scalar.copy if lo == 1 else nc.vector.tensor_copy)[:])
         grouped = regroup(EARLY, S // P, nc.vector.tensor_copy)
         for lo, hi in spans[3:]:
             last_product(lo, hi, grouped[:, (lo - EARLY) * P * PACK : (hi - EARLY) * P * PACK])
@@ -287,7 +293,8 @@ def tile_picked_bev_max_lo_kernel(
         out_grouped = buffer("out_grouped", S, f"z_grouped{EARLY}")
         done = 0
         for (lo, hi), result, upto in zip(spans, results, (0, 0, 4, 6, 8)):
-            nc.vector.tensor_copy(*weave_views(out_grouped[:, lo * P * PACK : hi * P * PACK], result[:]))
+            copy = nc.scalar.copy if hi == S // P else nc.vector.tensor_copy
+            copy(*weave_views(out_grouped[:, lo * P * PACK : hi * P * PACK], result[:]))
             if upto > done:
                 cells = slice(done * P, upto * P)
                 quantize(out_codes[:, cells], out_scales[:, cells], out_grouped[:, done * P * PACK : upto * P * PACK])

@@ -126,8 +126,8 @@ def tile_picked_bev_max_lo_kernel(
 
         def deal_aside(i, grouped):
             nc.gpsimd.tensor_scalar(
-                grouped.rearrange("p (t m j) -> p t m j", t=PACK, j=PACK),
-                w_raw[i][:].rearrange("p j (m t) -> p t m j", t=PACK),
+                grouped.rearrange("p (t m j) -> p m j t", t=PACK, j=PACK),
+                w_raw[i][:].rearrange("p j (m t) -> p m j t", t=PACK),
                 1.0, 0.0, MULT, ADD,
             )
 

@@ -23,7 +23,6 @@ P = 128
 PACK = 4
 CHUNKS = (1, 2, 2, 2, 1)
 LIST_ROWS = 16
-FILL = 320
 EARLY = 5
 
 
@@ -66,7 +65,7 @@ def tile_picked_bev_max_lo_kernel(
         def quantize(codes, scales, grouped):
             nc.vector.quantize_mx(out=codes.bitcast(FP8X4), scales=scales, in_=grouped)
 
-        picked = [keep.tile([P, PACK + s, V], BF16, name=f"picked{s}", align_bytes=64) for s in range(2)]
+        picked = {1: keep.tile([P, PACK + 1, V], BF16, name="picked1", align_bytes=64)}
         x_grouped = [keep.tile([P, V * PACK], BF16, name="x_grouped0", align_bytes=64)]
         x_codes = [keep.tile([P, V], U32, name=f"x_codes{s}", align_bytes=64) for s in range(2)]
         x_scales = [keep.tile([P, V], U8, name=f"x_scales{s}", align_bytes=64) for s in range(2)]
@@ -84,16 +83,19 @@ def tile_picked_bev_max_lo_kernel(
         def x_views(s, lo, hi):
             return weave_views(x_grouped[s][:, lo * PACK : hi * PACK], picked[s][:, :PACK, lo:hi])
 
+        def gather_in_place(j, lo, hi):
+            entries = offs_sb[:, lo // LIST_ROWS : hi // LIST_ROWS]
+            slots = x_grouped[0][:].rearrange("p (c j) -> p c j", j=PACK)
+            nc.vector.tensor_copy(slots[:, lo:hi, j], x_planes[j][:].indirect(entries))
+
         for j in range(PACK - 1):
-            gather(0, j, 0, V)
+            gather_in_place(j, 0, V)
             if j < 2:
                 gather_rounded(1, j)
             else:
                 gather(1, j, 0, V)
-        gather(0, PACK - 1, 0, V // 2)
-        nc.scalar.copy(*x_views(0, 0, V // 2))
-        gather(0, PACK - 1, V // 2, V)
-        nc.vector.tensor_copy(*x_views(0, V // 2, V))
+        for lo in range(0, V, V // 2):
+            gather_in_place(PACK - 1, lo, lo + V // 2)
         for lo in range(0, V, V // 2):
             hi = lo + V // 2
             quantize(x_codes[0][:, lo:hi], x_scales[0][:, lo:hi], x_grouped[0][:, lo * PACK : hi * PACK])
@@ -126,8 +128,8 @@ def tile_picked_bev_max_lo_kernel(
 
         def deal_aside(i, grouped):
             nc.gpsimd.tensor_scalar(
-                grouped.rearrange("p (t m j) -> p m j t", t=PACK, j=PACK),
-                w_raw[i][:].rearrange("p j (m t) -> p m j t", t=PACK),
+                grouped.rearrange("p (t m j) -> p m t j", t=PACK, j=PACK),
+                w_raw[i][:].rearrange("p j (m t) -> p m t j", t=PACK),
                 1.0, 0.0, MULT, ADD,
             )
 
@@ -171,7 +173,7 @@ def tile_picked_bev_max_lo_kernel(
 
 
         def fuse_slot(t, *cuts):
-            gap = keep.tile([P, S], F32, name=f"gap{t}", tag="aside", align_bytes=64)
+            gap = keep.tile([P, S], F32, name=f"gap{t}", tag="w1_first_scales", align_bytes=64)
             fuse_aside(t, 0, EARLY, gap)
             fuse_aside(t, EARLY, S // P, gap)
             for lo, hi in zip(cuts, cuts[1:]):
@@ -180,42 +182,41 @@ def tile_picked_bev_max_lo_kernel(
         def tile_of(pair, u):
             return [operand[:, u * P : (u + 1) * P] for operand in pair]
 
-        half = V // 2
+        half, quarter = V // 2, V // 4
         grouped = picked[1][:, PACK - 1 :, :].rearrange("p a c -> p (a c)")
-        deal(0, 0, 2, grouped)
-        first = quantized("w1_first", grouped[:, : P * PACK], P)
-        halves = [(banks[0], 0, half), (banks[2 * PACK - 1], half, V)]
-        for bank, lo, hi in halves:
-            product(0, bank, *tile_of(first, 0), lo, hi)
+        deal(0, 0, 2, grouped, nc.vector.tensor_copy)
+        first = quantized("w1_first", grouped, 2 * P)
+        product(0, banks[0], *tile_of(first, 0), 0, half)
+        product(0, banks[1], *tile_of(first, 1), 0, quarter)
+        product(0, banks[2], *tile_of(first, 0), half, V)
+        product(0, banks[3], *tile_of(first, 1), quarter, 3 * quarter)
+        product(0, banks[3], *tile_of(first, 1), 3 * quarter, V)
         gather(1, PACK - 1, 0, V)
-        for bank, lo, hi in halves:
-            activate(0, 0, bank, lo, hi)
-        scatter(0, 0, 0, half)
-        following = quantized("w1_next", grouped[:, P * PACK :], P, "act0_0_0")
-        product(0, banks[1], *tile_of(following, 0), 0, V)
-        scatter(0, 0, half, V)
+        last_grouped = buffer("w1_grouped_last", 2 * P)
+        deal(0, 2, 2, last_grouped[:])
+        for t, bank, lo, hi in ((0, 0, 0, half), (1, 1, 0, quarter), (0, 2, half, V)):
+            activate(0, t, banks[bank], lo, hi)
+            scatter(0, t, lo, hi)
 
         x_grouped.append(buffer("x_grouped1", V, "w1_first_codes"))
         nc.scalar.copy(*x_views(1, 0, V))
-        grouped = buffer("w1_grouped_last", 2 * P, "w1_first_scales")
-        deal(0, 2, 2, grouped[:])
-        last = quantized("w1_last", grouped[:], 2 * P)
+        last = quantized("w1_last", last_grouped[:], 2 * P, f"act0_0_{half}")
         quantize(x_codes[1][:], x_scales[1][:], x_grouped[1][:])
-        grouped = buffer("w2_grouped", H, "aside")
+        grouped = buffer("w2_grouped", H, "w1_first_scales")
         deal_aside(1, grouped[:])
         second = quantized("w2", grouped[:], H)
         for t in range(PACK - 1):
             product(1, banks[PACK + t], *tile_of(second, t), 0, V)
-        activate(0, 1, banks[1], 0, FILL, "w_raw1")
-        scatter(0, 1, 0, FILL)
-        grouped = buffer("w3_grouped", H, "aside")
+        activate(0, 1, banks[3], quarter, 3 * quarter, "w_raw1")
+        scatter(0, 1, quarter, 3 * quarter)
+        grouped = buffer("w3_grouped", H, "w1_first_scales")
         deal_aside(2, grouped[:])
         activate(1, 0, banks[PACK], 0, V)
         scatter(1, 0, 0, V)
         w3_codes, w3_scales = quantized("w3", grouped[:], H)
         late = keep.tile([P, PACK, V], F32, name="late_acts", tag="w_raw2", align_bytes=64)
-        activate(0, 1, banks[1], FILL, V, into=late[:, 0, FILL:])
-        scatter(0, 1, FILL, V)
+        activate(0, 1, banks[3], 3 * quarter, V, into=late[:, 0, :quarter])
+        scatter(0, 1, 3 * quarter, V)
         activate(1, 1, banks[PACK + 1], 0, V, into=late[:, 1, :])
         scatter(1, 1, 0, V)
         product(0, banks[PACK + 1], *tile_of(last, 0), 0, V)

@@ -161,23 +161,27 @@ def tile_picked_bev_max_lo_kernel(
             a_map, e_map = (by_group(maps[s][t][:, lo * P : hi * P]) for s in range(2))
             nc.vector.tensor_tensor(slot(t, lo, hi), a_map, e_map, MAX)
 
-        def fuse_aside(t, lo, hi, gap):
-            cells = slice(lo * P, hi * P)
-            excess = z_words(lo, hi)[:, :, (t + 1) // 2, :]
-            nc.gpsimd.tensor_tensor(gap[:, cells], maps[1][t][:, cells], maps[0][t][:, cells], SUBTRACT)
-            nc.scalar.activation(excess, by_group(gap[:, cells]), RELU)
-
-        def finish_aside(t, lo, hi):
-            excess = z_words(lo, hi)[:, :, (t + 1) // 2, :]
-            nc.gpsimd.tensor_tensor(slot(t, lo, hi), by_group(maps[0][t][:, lo * P : hi * P]), excess, ADD)
-
+        z_planes = keep.tile([P, 2, S], BF16, name="z_planes", align_bytes=64)
 
         def fuse_slot(t, *cuts):
             gap = keep.tile([P, S], F32, name=f"gap{t}", tag="w1_first_scales", align_bytes=64)
-            fuse_aside(t, 0, EARLY, gap)
-            fuse_aside(t, EARLY, S // P, gap)
+            for lo, hi in ((0, EARLY), (EARLY, S // P)):
+                cells = slice(lo * P, hi * P)
+                nc.gpsimd.tensor_tensor(gap[:, cells], maps[1][t][:, cells], maps[0][t][:, cells], SUBTRACT)
+                excess = by_group(gap[:, cells]) if t < 2 else z_words(lo, hi)[:, :, 1, :]
+                nc.scalar.activation(excess, by_group(gap[:, cells]), RELU)
             for lo, hi in zip(cuts, cuts[1:]):
-                finish_aside(t, lo, hi)
+                cells = slice(lo * P, hi * P)
+                if t < 2:
+                    nc.gpsimd.tensor_tensor(z_planes[:, t, cells], maps[0][t][:, cells], gap[:, cells], ADD)
+                else:
+                    excess = z_words(lo, hi)[:, :, 1, :]
+                    nc.gpsimd.tensor_tensor(slot(t, lo, hi), by_group(maps[0][t][:, cells]), excess, ADD)
+                if t == 1:
+                    nc.scalar.copy(
+                        z_words(lo, hi)[:, :, 0, :].bitcast(BF16).rearrange("p g (r e) -> p g r e", e=2),
+                        z_planes[:, :, cells].rearrange("p e (g r) -> p g r e", r=P),
+                    )
 
         def tile_of(pair, u):
             return [operand[:, u * P : (u + 1) * P] for operand in pair]

@@ -30,28 +30,38 @@ def tile_picked_bev_max_lo_kernel(
     tc, xT, w1, w2, w3, offs, near, far, out_0, out_1, out_2
 ):
     nc = tc.nc
+    half = V // 2
     with ExitStack() as ctx:
         lists = ctx.enter_context(tc.tile_pool(name="lists", bufs=1))
         keep = ctx.enter_context(tc.tile_pool(name="keep", bufs=1))
         psum = ctx.enter_context(tc.psum_pool(name="psum", bufs=1))
 
+        def tile(name, shape, dtype, tag=None):
+            return keep.tile([P, *shape], dtype, name=name, tag=tag or name, align_bytes=64)
+
+        def buffer(name, width, tag=None):
+            return tile(name, [width * PACK], BF16, tag)
+
         offs_sb = lists.tile([P, S // LIST_ROWS], U16, name="offs_sb")
         cell_lists = [lists.tile([P, V // LIST_ROWS], U16, name=f"cells{s}") for s in range(2)]
         x_rows = xT.rearrange("(p j) c -> p j c", j=PACK)
-        x_planes = [keep.tile([P, T], F32, name=f"x{j}") for j in range(PACK)]
-        w_raw = [keep.tile([P, PACK, H], F32, name=f"w_raw{i}", tag=f"w_raw{i}", align_bytes=64) for i in range(3)]
+        x_planes = [tile(f"x{j}", [T], F32) for j in range(PACK)]
+        w1_rows = w1.rearrange("(p j) c -> p j c", j=PACK)
+        w1_raw = [tile(f"w1_raw{g}", [PACK, H // 2], F32) for g in range(2)]
+        w2_raw = tile("w2_raw", [PACK, H], F32)
+        w3_raw = tile("w3_raw", [PACK, H], F32)
 
         nc.sync.dma_start(x_planes[0][:], x_rows[:, 0, :])
         nc.sync.dma_start(offs_sb[:], offs)
         for j in range(1, PACK):
             nc.sync.dma_start(x_planes[j][:], x_rows[:, j, :])
-        nc.sync.dma_start(w_raw[0][:], w1.rearrange("(p j) c -> p j c", j=PACK))
-        nc.sync.dma_start(cell_lists[0][:], near)
-        nc.sync.dma_start(cell_lists[1][:], far)
-        nc.sync.dma_start(w_raw[1][:], w2.rearrange("(p j) c -> p j c", j=PACK))
-        nc.sync.dma_start(w_raw[2][:], w3.rearrange("(p j) c -> p j c", j=PACK))
+        for g in range(2):
+            nc.sync.dma_start(w1_raw[g][:], w1_rows[:, :, g * H // 2 : (g + 1) * H // 2])
+            nc.sync.dma_start(cell_lists[g][:], (near, far)[g])
+        nc.sync.dma_start(w2_raw[:], w2.rearrange("(p j) c -> p j c", j=PACK))
+        nc.sync.dma_start(w3_raw[:], w3.rearrange("(p j) c -> p j c", j=PACK))
 
-        maps = [[keep.tile([P, S], F32, name=f"map{s}_{t}") for t in range(PACK)] for s in range(2)]
+        maps = [[tile(f"map{s}_{t}", [S], F32) for t in range(PACK)] for s in range(2)]
         for s in range(2):
             for t in range(PACK):
                 nc.gpsimd.memset(maps[s][t][:].bitcast(I32), 0)
@@ -62,90 +72,131 @@ def tile_picked_bev_max_lo_kernel(
                 planes.rearrange("p j (c i) -> p c j i", i=PACK),
             )
 
-        def quantize(codes, scales, grouped):
-            nc.vector.quantize_mx(out=codes.bitcast(FP8X4), scales=scales, in_=grouped)
+        def quantized(name, grouped, tag=None):
+            width = grouped.shape[1] // PACK
+            codes, scales = tile(f"{name}_codes", [width], U32, tag), tile(f"{name}_scales", [width], U8)
+            nc.vector.quantize_mx(out=codes[:].bitcast(FP8X4), scales=scales[:], in_=grouped)
+            return codes, scales
 
-        picked = {1: keep.tile([P, PACK + 1, V], BF16, name="picked1", align_bytes=64)}
-        x_grouped = [keep.tile([P, V * PACK], BF16, name="x_grouped0", align_bytes=64)]
-        x_codes = [keep.tile([P, V], U32, name=f"x_codes{s}", align_bytes=64) for s in range(2)]
-        x_scales = [keep.tile([P, V], U8, name=f"x_scales{s}", align_bytes=64) for s in range(2)]
+        def columns(pair, lo, hi):
+            return [operand[:, lo:hi] for operand in pair]
 
-        def gather(s, j, lo, hi):
-            entries = offs_sb[:, (s * V + lo) // LIST_ROWS : (s * V + hi) // LIST_ROWS]
-            nc.vector.tensor_copy(picked[s][:, j, lo:hi], x_planes[j][:].indirect(entries))
+        def multiply(out, stationary, moving):
+            nc.tensor.matmul_mx(
+                out=out, lhsT=stationary[0].bitcast(FP8X4), lhsT_scale=stationary[1],
+                rhs=moving[0].bitcast(FP8X4), rhs_scale=moving[1], start=True, stop=True,
+            )
 
-        def gather_rounded(s, j):
-            rounded = keep.tile([P, T], BF16, name=f"x_rounded{j}")
-            nc.scalar.copy(rounded[:], x_planes[j][:])
-            entries = offs_sb[:, s * V // LIST_ROWS : (s + 1) * V // LIST_ROWS]
-            nc.scalar.activation(picked[s][:, j, :], rounded[:].indirect(entries), COPY)
+        x0_grouped = buffer("x0_grouped", V)
+        picked = tile("picked", [PACK, V], BF16)
 
-        def x_views(s, lo, hi):
-            return weave_views(x_grouped[s][:, lo * PACK : hi * PACK], picked[s][:, :PACK, lo:hi])
+        def entries(s, lo, hi):
+            return offs_sb[:, (s * V + lo) // LIST_ROWS : (s * V + hi) // LIST_ROWS]
 
         def gather_in_place(j, lo, hi):
-            entries = offs_sb[:, lo // LIST_ROWS : hi // LIST_ROWS]
-            slots = x_grouped[0][:].rearrange("p (c j) -> p c j", j=PACK)
-            nc.vector.tensor_copy(slots[:, lo:hi, j], x_planes[j][:].indirect(entries))
+            slots = x0_grouped[:].rearrange("p (c j) -> p c j", j=PACK)
+            nc.vector.tensor_copy(slots[:, lo:hi, j], x_planes[j][:].indirect(entries(0, lo, hi)))
+
+        def gather(j):
+            nc.vector.tensor_copy(picked[:, j, :], x_planes[j][:].indirect(entries(1, 0, V)))
+
+        def gather_rounded(j):
+            rounded = tile(f"x_rounded{j}", [T], BF16)
+            nc.scalar.copy(rounded[:], x_planes[j][:])
+            nc.scalar.activation(picked[:, j, :], rounded[:].indirect(entries(1, 0, V)), COPY)
 
         for j in range(PACK - 1):
             gather_in_place(j, 0, V)
-            if j < 2:
-                gather_rounded(1, j)
-            else:
-                gather(1, j, 0, V)
-        for lo in range(0, V, V // 2):
-            gather_in_place(PACK - 1, lo, lo + V // 2)
-        for lo in range(0, V, V // 2):
-            hi = lo + V // 2
-            quantize(x_codes[0][:, lo:hi], x_scales[0][:, lo:hi], x_grouped[0][:, lo * PACK : hi * PACK])
+            (gather if j % 2 else gather_rounded)(j)
+        for lo in (0, half):
+            gather_in_place(PACK - 1, lo, lo + half)
+
+        def pair_views(grouped, raw):
+            return (
+                grouped.rearrange("p (m u j) -> p m u j", u=2, j=PACK),
+                raw.rearrange("p j (m t) -> p m t j", t=PACK)[:, :, :2, :],
+            )
+
+        def slot_views(grouped, raw, first):
+            count = PACK - first
+            return (
+                grouped.rearrange("p t (m j) -> p m t j", j=PACK),
+                raw.rearrange("p j (m t) -> p m t j", t=PACK)[:, :, first : first + count, :],
+            )
+
+        def deal_aside(views):
+            nc.gpsimd.tensor_scalar(*views, 1.0, 0.0, MULT, ADD)
 
         banks = [psum.tile([P, V], F32, name=f"bank{b}", tag=f"bank{b}") for b in range(2 * PACK)]
         acts = {}
 
-        def product(s, bank, codes, scales, lo, hi):
-            nc.tensor.matmul_mx(
-                out=bank[:, lo:hi], lhsT=codes.bitcast(FP8X4), lhsT_scale=scales,
-                rhs=x_codes[s][:, lo:hi].bitcast(FP8X4), rhs_scale=x_scales[s][:, lo:hi], start=True, stop=True,
-            )
-
         def activate(s, t, bank, lo, hi, tag=None, into=None):
             if into is None:
-                name = f"act{s}_{t}_{lo}"
-                into = keep.tile([P, hi - lo], F32, name=name, tag=tag or name, align_bytes=64)[:]
+                into = tile(f"act{s}_{t}_{lo}", [hi - lo], F32, tag)[:]
             acts[s, t, lo] = into
             nc.scalar.activation(into, bank[:, lo:hi], RELU)
 
         def scatter(s, t, lo, hi):
-            entries = cell_lists[s][:, lo // LIST_ROWS : hi // LIST_ROWS]
-            nc.vector.tensor_copy(maps[s][t][:].indirect(entries), acts[s, t, lo])
+            cells = cell_lists[s][:, lo // LIST_ROWS : hi // LIST_ROWS]
+            nc.vector.tensor_copy(maps[s][t][:].indirect(cells), acts[s, t, lo])
 
-        def deal(i, t0, n, grouped, copy=nc.scalar.copy):
-            copy(
-                grouped.rearrange("p (t m j) -> p m j t", t=n, j=PACK),
-                w_raw[i][:].rearrange("p j (m t) -> p m j t", t=PACK)[:, :, :, t0 : t0 + n],
-            )
+        nc.scalar.copy(*pair_views(picked[:, PACK - 1, :], w1_raw[0][:]))
+        x0 = [quantized("x0_0", x0_grouped[:, : half * PACK])]
+        first = quantized("w1_first", picked[:, PACK - 1, :])
+        x0.append(quantized("x0_1", x0_grouped[:, half * PACK :]))
+        for u in range(2):
+            multiply(banks[u][:, u * half : (u + 1) * half], columns(first, 0, P), columns(x0[u], 0, half))
+        gather(PACK - 1)
+        next_grouped = buffer("w1_next_grouped", P)
+        nc.scalar.copy(*pair_views(next_grouped[:], w1_raw[1][:]))
+        following = quantized("w1_next", next_grouped[:])
+        last_grouped = tile("w1_last_grouped", [2, P * PACK], BF16, "aside")
+        for g in range(2):
+            part = last_grouped[:, :, g * P * PACK // 2 : (g + 1) * P * PACK // 2]
+            nc.scalar.copy(*slot_views(part, w1_raw[g][:], 2))
+        last = quantized("w1_last", last_grouped[:].rearrange("p t c -> p (t c)"))
+        for u in range(2):
+            multiply(banks[2 + u][:, u * half : (u + 1) * half], columns(following, 0, P), columns(x0[u], 0, half))
+        activate(0, 0, banks[0], 0, half)
+        scatter(0, 0, 0, half)
+        activate(0, 0, banks[1], half, V, "w1_raw1")
+        scatter(0, 0, half, V)
 
-        def deal_aside(i, grouped):
-            nc.gpsimd.tensor_scalar(
-                grouped.rearrange("p (t m j) -> p m t j", t=PACK, j=PACK),
-                w_raw[i][:].rearrange("p j (m t) -> p m t j", t=PACK),
-                1.0, 0.0, MULT, ADD,
-            )
+        activate(0, 1, banks[2], 0, half)
+        scatter(0, 1, 0, half)
+        x1_grouped = buffer("x1_grouped", V, "w1_next_codes")
+        nc.scalar.copy(*weave_views(x1_grouped[:], picked[:]))
+        x1 = quantized("x1", x1_grouped[:])
+        w2_grouped = tile("w2_grouped", [2, 2, P * PACK], BF16, "aside")
+        deal_aside(pair_views(w2_grouped[:, 0].rearrange("p t c -> p (t c)"), w2_raw[:]))
+        deal_aside(slot_views(w2_grouped[:, 1], w2_raw[:], 2))
+        second = quantized("w2", w2_grouped[:].rearrange("p a t c -> p (a t c)"))
+        for t in range(PACK - 1):
+            multiply(banks[PACK + t][:], columns(second, t * P, (t + 1) * P), columns(x1, 0, V))
+        activate(0, 1, banks[3], half, V, "w2_raw")
+        scatter(0, 1, half, V)
+        w3_grouped = tile("w3_grouped", [PACK, P * PACK], BF16, "aside")
+        deal_aside(slot_views(w3_grouped[:], w3_raw[:], 0))
+        activate(1, 0, banks[PACK], 0, V)
+        scatter(1, 0, 0, V)
+        third = quantized("w3", w3_grouped[:].rearrange("p t c -> p (t c)"))
+        late = tile("late_acts", [PACK - 1, V], F32, "w3_raw")
 
-        def quantized(name, grouped, width, tag=None):
-            codes = keep.tile([P, width], U32, name=f"{name}_codes", tag=tag or f"{name}_codes", align_bytes=64)
-            scales = keep.tile([P, width], U8, name=f"{name}_scales", tag=f"{name}_scales", align_bytes=64)
-            quantize(codes[:], scales[:], grouped)
-            return codes, scales
+        def first_sensor(t, bank):
+            for u in range(2):
+                multiply(bank[:, u * half : (u + 1) * half], columns(last, (t - 2) * P, (t - 1) * P), columns(x0[u], 0, half))
+            activate(0, t, bank, 0, V)
 
-        def buffer(name, width, tag=None):
-            return keep.tile([P, width * PACK], BF16, name=name, tag=tag or name, align_bytes=64)
+        activate(1, 1, banks[PACK + 1], 0, V, into=late[:, 0, :])
+        scatter(1, 1, 0, V)
+        first_sensor(2, banks[PACK + 1])
+        activate(1, 2, banks[PACK + 2], 0, V, into=late[:, 1, :])
+        first_sensor(3, banks[PACK + 2])
+        multiply(banks[PACK + 1][:], columns(second, 3 * P, 4 * P), columns(x1, 0, V))
+        activate(1, 3, banks[PACK + 1], 0, V, into=late[:, 2, :])
 
-        z_parts = [
-            keep.tile([P, groups, 2, P], F32, name=f"z_words{i}", tag=f"z_words{i}", align_bytes=64)
-            for i, groups in enumerate((EARLY, S // P - EARLY))
-        ]
+        parts = ((0, EARLY), (EARLY, S // P))
+        z_parts = [tile(f"z_words{lo}", [hi - lo, 2, P], F32) for lo, hi in parts]
 
         def z_words(lo, hi):
             return z_parts[0][:, lo:hi] if lo < EARLY else z_parts[1][:, lo - EARLY : hi - EARLY]
@@ -157,104 +208,61 @@ def tile_picked_bev_max_lo_kernel(
         def by_group(ap):
             return ap.rearrange("p (g r) -> p g r", r=P)
 
-        def fuse(t, lo, hi):
-            a_map, e_map = (by_group(maps[s][t][:, lo * P : hi * P]) for s in range(2))
-            nc.vector.tensor_tensor(slot(t, lo, hi), a_map, e_map, MAX)
+        z_planes = tile("z_planes", [2, S], BF16)
 
-        z_planes = keep.tile([P, 2, S], BF16, name="z_planes", align_bytes=64)
+        def excess(t, gap, lo, hi):
+            return by_group(gap[:, lo * P : hi * P]) if t < 2 else z_words(lo, hi)[:, :, 1, :]
 
-        def fuse_slot(t, *cuts):
-            gap = keep.tile([P, S], F32, name=f"gap{t}", tag="w1_first_scales", align_bytes=64)
-            for lo, hi in ((0, EARLY), (EARLY, S // P)):
+        def fuse_aside(t, *cuts):
+            gap = tile(f"gap{t}", [S], F32, "aside")
+            for lo, hi in parts:
                 cells = slice(lo * P, hi * P)
                 nc.gpsimd.tensor_tensor(gap[:, cells], maps[1][t][:, cells], maps[0][t][:, cells], SUBTRACT)
-                excess = by_group(gap[:, cells]) if t < 2 else z_words(lo, hi)[:, :, 1, :]
-                nc.scalar.activation(excess, by_group(gap[:, cells]), RELU)
+                nc.scalar.activation(excess(t, gap, lo, hi), by_group(gap[:, cells]), RELU)
+            rows = tile(f"z_rows{t}", [S], BF16) if t < 2 else None
             for lo, hi in zip(cuts, cuts[1:]):
                 cells = slice(lo * P, hi * P)
+                into = by_group(rows[:, cells]) if t < 2 else slot(t, lo, hi)
+                nc.gpsimd.tensor_tensor(into, by_group(maps[0][t][:, cells]), excess(t, gap, lo, hi), ADD)
                 if t < 2:
-                    nc.gpsimd.tensor_tensor(z_planes[:, t, cells], maps[0][t][:, cells], gap[:, cells], ADD)
-                else:
-                    excess = z_words(lo, hi)[:, :, 1, :]
-                    nc.gpsimd.tensor_tensor(slot(t, lo, hi), by_group(maps[0][t][:, cells]), excess, ADD)
-                if t == 1:
-                    nc.scalar.copy(
-                        z_words(lo, hi)[:, :, 0, :].bitcast(BF16).rearrange("p g (r e) -> p g r e", e=2),
-                        z_planes[:, :, cells].rearrange("p e (g r) -> p g r e", r=P),
-                    )
+                    for u in range(2):
+                        nc.sync.dma_start(z_planes[t * P // 2 : (t + 1) * P // 2, u, cells], rows[u:P:2, cells])
 
-        def tile_of(pair, u):
-            return [operand[:, u * P : (u + 1) * P] for operand in pair]
+        for t in range(2):
+            fuse_aside(t, 0, EARLY, S // P)
 
-        half, quarter = V // 2, V // 4
-        grouped = picked[1][:, PACK - 1 :, :].rearrange("p a c -> p (a c)")
-        deal(0, 0, 2, grouped, nc.vector.tensor_copy)
-        first = quantized("w1_first", grouped, 2 * P)
-        product(0, banks[0], *tile_of(first, 0), 0, half)
-        product(0, banks[1], *tile_of(first, 1), 0, quarter)
-        product(0, banks[2], *tile_of(first, 0), half, V)
-        product(0, banks[3], *tile_of(first, 1), quarter, 3 * quarter)
-        product(0, banks[3], *tile_of(first, 1), 3 * quarter, V)
-        gather(1, PACK - 1, 0, V)
-        last_grouped = buffer("w1_grouped_last", 2 * P)
-        deal(0, 2, 2, last_grouped[:])
-        for t, bank, lo, hi in ((0, 0, 0, half), (1, 1, 0, quarter), (0, 2, half, V)):
-            activate(0, t, banks[bank], lo, hi)
-            scatter(0, t, lo, hi)
+        def pair_up(lo, hi):
+            nc.scalar.copy(
+                z_words(lo, hi)[:, :, 0, :].bitcast(BF16).rearrange("p g (r e) -> p g r e", e=2),
+                z_planes[:, :, lo * P : hi * P].rearrange("p e (g r) -> p g r e", r=P),
+            )
 
-        x_grouped.append(buffer("x_grouped1", V, "w1_first_codes"))
-        nc.scalar.copy(*x_views(1, 0, V))
-        last = quantized("w1_last", last_grouped[:], 2 * P, f"act0_0_{half}")
-        quantize(x_codes[1][:], x_scales[1][:], x_grouped[1][:])
-        grouped = buffer("w2_grouped", H, "w1_first_scales")
-        deal_aside(1, grouped[:])
-        second = quantized("w2", grouped[:], H)
-        for t in range(PACK - 1):
-            product(1, banks[PACK + t], *tile_of(second, t), 0, V)
-        activate(0, 1, banks[3], quarter, 3 * quarter, "w_raw1")
-        scatter(0, 1, quarter, 3 * quarter)
-        grouped = buffer("w3_grouped", H, "w1_first_scales")
-        deal_aside(2, grouped[:])
-        activate(1, 0, banks[PACK], 0, V)
-        scatter(1, 0, 0, V)
-        w3_codes, w3_scales = quantized("w3", grouped[:], H)
-        late = keep.tile([P, PACK, V], F32, name="late_acts", tag="w_raw2", align_bytes=64)
-        activate(0, 1, banks[3], 3 * quarter, V, into=late[:, 0, :quarter])
-        scatter(0, 1, 3 * quarter, V)
-        activate(1, 1, banks[PACK + 1], 0, V, into=late[:, 1, :])
-        scatter(1, 1, 0, V)
-        product(0, banks[PACK + 1], *tile_of(last, 0), 0, V)
-        activate(0, 2, banks[PACK + 1], 0, V)
-        activate(1, 2, banks[PACK + 2], 0, V, into=late[:, 2, :])
-        product(0, banks[PACK + 2], *tile_of(last, 1), 0, V)
-        activate(0, 3, banks[PACK + 2], 0, V)
-        product(1, banks[PACK + 1], *tile_of(second, 3), 0, V)
-        activate(1, 3, banks[PACK + 1], 0, V, into=late[:, 3, :])
-        fuse_slot(0, 0, EARLY, S // P)
-        fuse_slot(1, 0, EARLY, S // P)
-        first_grouped = buffer("z_grouped0", P)
-        first_slots = first_grouped[:].rearrange("p (c t) -> p c t", t=PACK)
+        pair_up(0, 1)
         for t in range(2, PACK):
             for s in range(2):
                 scatter(s, t, 0, V)
             if t < PACK - 1:
-                fuse_slot(t, 0, 1, EARLY, S // P)
+                fuse_aside(t, 0, 1, EARLY, S // P)
+        first_grouped = buffer("z_grouped0", P)
         nc.scalar.copy(
             first_grouped[:].bitcast(F32).rearrange("p (r u) -> p r u", u=2),
             z_parts[0][:, 0].rearrange("p u r -> p r u"),
         )
-        last_maps = [maps[s][PACK - 1][:, :P] for s in range(2)]
-        nc.vector.tensor_tensor(first_slots[:, :, PACK - 1], *last_maps, MAX)
+        pair_up(1, EARLY)
+        pair_up(EARLY, S // P)
+        last_maps = [maps[s][PACK - 1] for s in range(2)]
+        first_slots = first_grouped[:].rearrange("p (c t) -> p c t", t=PACK)
+        nc.vector.tensor_tensor(first_slots[:, :, PACK - 1], last_maps[0][:, :P], last_maps[1][:, :P], MAX)
 
         out_rows = out_0.rearrange("(p t) c -> p t c", t=PACK)
         out_words = out_1[0].rearrange("p c r -> p (c r)").bitcast(I32)
-        out_codes = keep.tile([P, S], U32, name="out_codes", align_bytes=64)
-        out_scales = keep.tile([P, S], U8, name="out_scales", align_bytes=64)
+        out_codes, out_scales = tile("out_codes", [S], U32), tile("out_scales", [S], U8)
         spans = [(sum(CHUNKS[:c]), sum(CHUNKS[: c + 1])) for c in range(len(CHUNKS))]
 
         def regroup(lo, hi, copy):
             grouped = buffer(f"z_grouped{lo}", (hi - lo) * P)
-            fuse(PACK - 1, lo, hi)
+            both = [by_group(last_map[:, lo * P : hi * P]) for last_map in last_maps]
+            nc.vector.tensor_tensor(slot(PACK - 1, lo, hi), *both, MAX)
             copy(
                 grouped[:].bitcast(F32).rearrange("p (g r u) -> p g r u", u=2, r=P),
                 z_words(lo, hi).rearrange("p g u r -> p g r u"),
@@ -265,17 +273,13 @@ def tile_picked_bev_max_lo_kernel(
 
         def last_product(lo, hi, grouped):
             width = (hi - lo) * P
-            z_codes, z_scales = quantized(f"z{lo}", grouped, width)
+            z = quantized(f"z{lo}", grouped)
             per_bank = PACK // (hi - lo)
             for b in range(lo, hi):
                 bank = psum.tile([P, per_bank, width], F32, name=f"out_bank{b}", tag=f"bank{b}")
                 for u in range(per_bank):
                     t = (b - lo) * per_bank + u
-                    cols = slice(t * P, (t + 1) * P)
-                    nc.tensor.matmul_mx(
-                        out=bank[:, u, :], lhsT=w3_codes[:, cols].bitcast(FP8X4), lhsT_scale=w3_scales[:, cols],
-                        rhs=z_codes[:].bitcast(FP8X4), rhs_scale=z_scales[:], start=True, stop=True,
-                    )
+                    multiply(bank[:, u, :], columns(third, t * P, (t + 1) * P), columns(z, 0, width))
                 out_banks.append(bank)
 
         last_product(0, 1, first_grouped[:])
@@ -287,13 +291,12 @@ def tile_picked_bev_max_lo_kernel(
 
         results = []
         for lo, hi in spans:
-            cells = slice(lo * P, hi * P)
             per_bank = PACK // (hi - lo)
-            result = keep.tile([P, PACK, (hi - lo) * P], F32, name=f"result{lo}", align_bytes=64)
+            result = tile(f"result{lo}", [PACK, (hi - lo) * P], F32)
             for b in range(lo, hi):
-                first = (b - lo) * per_bank
-                nc.scalar.copy(result[:, first : first + per_bank, :], out_banks[b][:])
-            nc.sync.dma_start(out_rows[:, :, cells], result[:])
+                first_row = (b - lo) * per_bank
+                nc.scalar.copy(result[:, first_row : first_row + per_bank, :], out_banks[b][:])
+            nc.sync.dma_start(out_rows[:, :, lo * P : hi * P], result[:])
             results.append(result)
         out_grouped = buffer("out_grouped", S, f"z_grouped{EARLY}")
         done = 0
@@ -302,7 +305,10 @@ def tile_picked_bev_max_lo_kernel(
             copy(*weave_views(out_grouped[:, lo * P * PACK : hi * P * PACK], result[:]))
             if upto > done:
                 cells = slice(done * P, upto * P)
-                quantize(out_codes[:, cells], out_scales[:, cells], out_grouped[:, done * P * PACK : upto * P * PACK])
+                nc.vector.quantize_mx(
+                    out=out_codes[:, cells].bitcast(FP8X4), scales=out_scales[:, cells],
+                    in_=out_grouped[:, done * P * PACK : upto * P * PACK],
+                )
                 nc.sync.dma_start(out_words[:, cells], out_codes[:, cells].bitcast(I32))
                 done = upto
         for q in range(P // 32):

@@ -1,6 +1,7 @@
 from contextlib import ExitStack
 
 import concourse.mybir as mybir
+from concourse.masks import make_identity
 
 K, T, S, H, V = 512, 2048, 1024, 512, 512
 FLOPS = 2 * K * H * 2 * V + 2 * H * H * S
@@ -24,6 +25,8 @@ PACK = 4
 CHUNKS = (1, 2, 2, 2, 1)
 LIST_ROWS = 16
 EARLY = 5
+MOST = 384
+WARM = 4
 
 
 def tile_picked_bev_max_lo_kernel(
@@ -179,7 +182,6 @@ def tile_picked_bev_max_lo_kernel(
         deal_aside(slot_views(w3_grouped[:], w3_raw[:], 0))
         activate(1, 0, banks[PACK], 0, V)
         scatter(1, 0, 0, V)
-        third = quantized("w3", w3_grouped[:].rearrange("p t c -> p (t c)"))
         late = tile("late_acts", [PACK - 1, V], F32, "w3_raw")
 
         def first_sensor(t, bank):
@@ -193,13 +195,14 @@ def tile_picked_bev_max_lo_kernel(
         activate(1, 2, banks[PACK + 2], 0, V, into=late[:, 1, :])
         first_sensor(3, banks[PACK + 2])
         multiply(banks[PACK + 1][:], columns(second, 3 * P, 4 * P), columns(x1, 0, V))
-        activate(1, 3, banks[PACK + 1], 0, V, into=late[:, 2, :])
+        activate(1, 3, banks[PACK + 1], 0, MOST, into=late[:, 2, :MOST])
 
-        parts = ((0, EARLY), (EARLY, S // P))
+        parts = ((0, 1), (1, EARLY), (EARLY, S // P))
         z_parts = [tile(f"z_words{lo}", [hi - lo, 2, P], F32) for lo, hi in parts]
 
         def z_words(lo, hi):
-            return z_parts[0][:, lo:hi] if lo < EARLY else z_parts[1][:, lo - EARLY : hi - EARLY]
+            (start, part), = [(a, part) for (a, b), part in zip(parts, z_parts) if a <= lo < b]
+            return part[:, lo - start : hi - start]
 
         def slot(t, lo, hi):
             pairs = z_words(lo, hi)[:, :, t // 2, :].bitcast(BF16)
@@ -208,48 +211,57 @@ def tile_picked_bev_max_lo_kernel(
         def by_group(ap):
             return ap.rearrange("p (g r) -> p g r", r=P)
 
-        z_planes = tile("z_planes", [2, S], BF16)
+        identity = tile("identity", [P], F32)
+        make_identity(nc, identity[:])
+        turned = tile("turned", [S // P, 2, P], BF16)
 
-        def excess(t, gap, lo, hi):
-            return by_group(gap[:, lo * P : hi * P]) if t < 2 else z_words(lo, hi)[:, :, 1, :]
+        def turn(out, block, start, stop):
+            nc.tensor.matmul(out, lhsT=block, rhs=identity[:], is_transpose=True, start=start, stop=stop)
 
-        def fuse_aside(t, *cuts):
-            gap = tile(f"gap{t}", [S], F32, "aside")
-            for lo, hi in parts:
-                cells = slice(lo * P, hi * P)
-                nc.gpsimd.tensor_tensor(gap[:, cells], maps[1][t][:, cells], maps[0][t][:, cells], SUBTRACT)
-                nc.scalar.activation(excess(t, gap, lo, hi), by_group(gap[:, cells]), RELU)
-            rows = tile(f"z_rows{t}", [S], BF16) if t < 2 else None
-            for lo, hi in zip(cuts, cuts[1:]):
-                cells = slice(lo * P, hi * P)
-                into = by_group(rows[:, cells]) if t < 2 else slot(t, lo, hi)
-                nc.gpsimd.tensor_tensor(into, by_group(maps[0][t][:, cells]), excess(t, gap, lo, hi), ADD)
-                if t < 2:
-                    for u in range(2):
-                        nc.sync.dma_start(z_planes[t * P // 2 : (t + 1) * P // 2, u, cells], rows[u:P:2, cells])
+        def difference(t, gap, lo, hi, excess):
+            cells = slice(lo * P, hi * P)
+            nc.gpsimd.tensor_tensor(gap[:, cells], maps[1][t][:, cells], maps[0][t][:, cells], SUBTRACT)
+            nc.scalar.activation(excess, by_group(gap[:, cells]), RELU)
 
         for t in range(2):
-            fuse_aside(t, 0, EARLY, S // P)
+            gap = tile(f"gap{t}", [S], F32)
+            for lo in (0, PACK):
+                difference(t, gap, lo, lo + PACK, by_group(gap[:, lo * P : (lo + PACK) * P]))
+            for lo in (0, PACK):
+                bank = psum.tile([P, PACK, P], F32, name=f"sum{t}_{lo}", tag=f"bank{2 * t + lo // PACK}")
+                for b in range(PACK):
+                    cells = slice((lo + b) * P, (lo + b + 1) * P)
+                    turn(bank[:, b, :], gap[:, cells], True, False)
+                    turn(bank[:, b, :], maps[0][t][:, cells], False, True)
+                nc.scalar.copy(turned[:, lo : lo + PACK, t, :], bank[:])
+        for lo in (0, PACK):
+            bank = psum.tile([P, PACK, P], F32, name=f"pairs{lo}", tag=f"bank{2 * PACK - 2 + lo // PACK}")
+            for b in range(PACK):
+                turn(bank[:, b, :], turned[:, lo + b].rearrange("p t c -> p (t c)").bitcast(F32), True, True)
+            for first_group, last_group in ((0, 1), (1, PACK)) if lo == 0 else ((PACK, EARLY), (EARLY, S // P)):
+                nc.scalar.copy(z_words(first_group, last_group)[:, :, 0, :], bank[:, first_group - lo : last_group - lo, :])
 
-        def pair_up(lo, hi):
-            nc.scalar.copy(
-                z_words(lo, hi)[:, :, 0, :].bitcast(BF16).rearrange("p g (r e) -> p g r e", e=2),
-                z_planes[:, :, lo * P : hi * P].rearrange("p e (g r) -> p g r e", r=P),
-            )
-
-        pair_up(0, 1)
-        for t in range(2, PACK):
-            for s in range(2):
-                scatter(s, t, 0, V)
-            if t < PACK - 1:
-                fuse_aside(t, 0, 1, EARLY, S // P)
+        for s in range(2):
+            scatter(s, 2, 0, V)
+        gap = tile("gap2", [S], F32)
+        for lo, hi in parts:
+            difference(2, gap, lo, hi, z_words(lo, hi)[:, :, 1, :])
+        for lo, hi in parts:
+            a_map = by_group(maps[0][2][:, lo * P : hi * P])
+            nc.gpsimd.tensor_tensor(slot(2, lo, hi), a_map, z_words(lo, hi)[:, :, 1, :], ADD)
+        scatter(0, 3, 0, V)
+        scatter(1, 3, 0, MOST)
+        third = quantized("w3", w3_grouped[:].rearrange("p t c -> p (t c)"), "w3_raw")
+        spare = psum.tile([P, V], F32, name="spare", tag=f"bank{2 * PACK - 1}")
+        for t in range(WARM):
+            multiply(spare[:], columns(third, t * P, (t + 1) * P), columns(x1, 0, V))
         first_grouped = buffer("z_grouped0", P)
         nc.scalar.copy(
             first_grouped[:].bitcast(F32).rearrange("p (r u) -> p r u", u=2),
             z_parts[0][:, 0].rearrange("p u r -> p r u"),
         )
-        pair_up(1, EARLY)
-        pair_up(EARLY, S // P)
+        activate(1, 3, banks[PACK + 1], MOST, V, "z_words0")
+        scatter(1, 3, MOST, V)
         last_maps = [maps[s][PACK - 1] for s in range(2)]
         first_slots = first_grouped[:].rearrange("p (c t) -> p c t", t=PACK)
         nc.vector.tensor_tensor(first_slots[:, :, PACK - 1], last_maps[0][:, :P], last_maps[1][:, :P], MAX)

@@ -159,14 +159,14 @@ def tile_picked_bev_max_lo_kernel(
             nc.scalar.copy(*slot_views(part, w1_raw[g][:], 2))
         last = quantized("w1_last", last_grouped[:].rearrange("p t c -> p (t c)"))
         for u in range(2):
-            multiply(banks[2 + u][:, u * half : (u + 1) * half], columns(following, 0, P), columns(x0[u], 0, half))
+            multiply(banks[2][:, u * half : (u + 1) * half], columns(following, 0, P), columns(x0[u], 0, half))
         activate(0, 0, banks[0], 0, half)
         scatter(0, 0, 0, half)
         activate(0, 0, banks[1], half, V, "w1_raw1")
         scatter(0, 0, half, V)
 
-        activate(0, 1, banks[2], 0, half)
-        scatter(0, 1, 0, half)
+        activate(0, 1, banks[2], 0, V)
+        scatter(0, 1, 0, V)
         x1_grouped = buffer("x1_grouped", V, "w1_next_codes")
         nc.scalar.copy(*weave_views(x1_grouped[:], picked[:]))
         x1 = quantized("x1", x1_grouped[:])
@@ -176,26 +176,30 @@ def tile_picked_bev_max_lo_kernel(
         second = quantized("w2", w2_grouped[:].rearrange("p a t c -> p (a t c)"))
         for t in range(PACK - 1):
             multiply(banks[PACK + t][:], columns(second, t * P, (t + 1) * P), columns(x1, 0, V))
-        activate(0, 1, banks[3], half, V, "w2_raw")
-        scatter(0, 1, half, V)
-        w3_grouped = tile("w3_grouped", [PACK, P * PACK], BF16, "aside")
-        deal_aside(slot_views(w3_grouped[:], w3_raw[:], 0))
-        activate(1, 0, banks[PACK], 0, V)
-        scatter(1, 0, 0, V)
-        late = tile("late_acts", [PACK - 1, V], F32, "w3_raw")
 
         def first_sensor(t, bank):
             for u in range(2):
                 multiply(bank[:, u * half : (u + 1) * half], columns(last, (t - 2) * P, (t - 1) * P), columns(x0[u], 0, half))
-            activate(0, t, bank, 0, V)
+
+        first_sensor(2, banks[3])
+        activate(0, 2, banks[3], 0, half, "w2_raw")
+        scatter(0, 2, 0, half)
+        w3_grouped = tile("w3_grouped", [PACK, P * PACK], BF16, "aside")
+        deal_aside(slot_views(w3_grouped[:], w3_raw[:], 0))
+        activate(1, 0, banks[PACK], 0, V)
+        scatter(1, 0, 0, V)
+        third = quantized("w3", w3_grouped[:].rearrange("p t c -> p (t c)"))
+        late = tile("late_acts", [PACK - 1, V], F32, "w3_raw")
 
         activate(1, 1, banks[PACK + 1], 0, V, into=late[:, 0, :])
         scatter(1, 1, 0, V)
-        first_sensor(2, banks[PACK + 1])
+        activate(0, 2, banks[3], half, V, into=late[:, 2, half:])
+        scatter(0, 2, half, V)
         activate(1, 2, banks[PACK + 2], 0, V, into=late[:, 1, :])
         first_sensor(3, banks[PACK + 2])
+        activate(0, 3, banks[PACK + 2], 0, V)
         multiply(banks[PACK + 1][:], columns(second, 3 * P, 4 * P), columns(x1, 0, V))
-        activate(1, 3, banks[PACK + 1], 0, MOST, into=late[:, 2, :MOST])
+        activate(1, 3, banks[PACK + 1], 0, MOST, "act1_0_0")
 
         parts = ((0, 1), (1, EARLY), (EARLY, S // P))
         z_parts = [tile(f"z_words{lo}", [hi - lo, 2, P], F32) for lo, hi in parts]
@@ -223,8 +227,9 @@ def tile_picked_bev_max_lo_kernel(
             nc.gpsimd.tensor_tensor(gap[:, cells], maps[1][t][:, cells], maps[0][t][:, cells], SUBTRACT)
             nc.scalar.activation(excess, by_group(gap[:, cells]), RELU)
 
+        gaps = tile("gaps", [2, S], F32, "aside")
         for t in range(2):
-            gap = tile(f"gap{t}", [S], F32)
+            gap = gaps[:, t, :]
             for lo in (0, PACK):
                 difference(t, gap, lo, lo + PACK, by_group(gap[:, lo * P : (lo + PACK) * P]))
             for lo in (0, PACK):
@@ -241,9 +246,8 @@ def tile_picked_bev_max_lo_kernel(
             for first_group, last_group in ((0, 1), (1, PACK)) if lo == 0 else ((PACK, EARLY), (EARLY, S // P)):
                 nc.scalar.copy(z_words(first_group, last_group)[:, :, 0, :], bank[:, first_group - lo : last_group - lo, :])
 
-        for s in range(2):
-            scatter(s, 2, 0, V)
-        gap = tile("gap2", [S], F32)
+        scatter(1, 2, 0, V)
+        gap = tile("gap2", [S], F32, "aside")
         for lo, hi in parts:
             difference(2, gap, lo, hi, z_words(lo, hi)[:, :, 1, :])
         for lo, hi in parts:
@@ -251,10 +255,6 @@ def tile_picked_bev_max_lo_kernel(
             nc.gpsimd.tensor_tensor(slot(2, lo, hi), a_map, z_words(lo, hi)[:, :, 1, :], ADD)
         scatter(0, 3, 0, V)
         scatter(1, 3, 0, MOST)
-        third = quantized("w3", w3_grouped[:].rearrange("p t c -> p (t c)"), "w3_raw")
-        spare = psum.tile([P, V], F32, name="spare", tag=f"bank{2 * PACK - 1}")
-        for t in range(WARM):
-            multiply(spare[:], columns(third, t * P, (t + 1) * P), columns(x1, 0, V))
         first_grouped = buffer("z_grouped0", P)
         nc.scalar.copy(
             first_grouped[:].bitcast(F32).rearrange("p (r u) -> p r u", u=2),
@@ -262,6 +262,9 @@ def tile_picked_bev_max_lo_kernel(
         )
         activate(1, 3, banks[PACK + 1], MOST, V, "z_words0")
         scatter(1, 3, MOST, V)
+        spare = psum.tile([P, V], F32, name="spare", tag=f"bank{PACK + 1}")
+        for t in range(WARM):
+            multiply(spare[:], columns(third, t * P, (t + 1) * P), columns(x1, 0, V))
         last_maps = [maps[s][PACK - 1] for s in range(2)]
         first_slots = first_grouped[:].rearrange("p (c t) -> p c t", t=PACK)
         nc.vector.tensor_tensor(first_slots[:, :, PACK - 1], last_maps[0][:, :P], last_maps[1][:, :P], MAX)
@@ -296,7 +299,7 @@ def tile_picked_bev_max_lo_kernel(
 
         last_product(0, 1, first_grouped[:])
         for lo, hi in spans[1:3]:
-            last_product(lo, hi, regroup(lo, hi, nc.scalar.copy if lo == 1 else nc.vector.tensor_copy)[:])
+            last_product(lo, hi, regroup(lo, hi, nc.scalar.copy)[:])
         grouped = regroup(EARLY, S // P, nc.vector.tensor_copy)
         for lo, hi in spans[3:]:
             last_product(lo, hi, grouped[:, (lo - EARLY) * P * PACK : (hi - EARLY) * P * PACK])

@@ -227,16 +227,15 @@ def tile_picked_bev_max_lo_kernel(
             nc.gpsimd.tensor_tensor(gap[:, cells], maps[1][t][:, cells], maps[0][t][:, cells], SUBTRACT)
             nc.scalar.activation(excess, by_group(gap[:, cells]), RELU)
 
-        gaps = tile("gaps", [2, S], F32, "aside")
         for t in range(2):
-            gap = gaps[:, t, :]
+            gap, excess = tile(f"gap{t}", [S], F32, "aside"), tile(f"excess{t}", [S], F32)
             for lo in (0, PACK):
-                difference(t, gap, lo, lo + PACK, by_group(gap[:, lo * P : (lo + PACK) * P]))
+                difference(t, gap, lo, lo + PACK, by_group(excess[:, lo * P : (lo + PACK) * P]))
             for lo in (0, PACK):
                 bank = psum.tile([P, PACK, P], F32, name=f"sum{t}_{lo}", tag=f"bank{2 * t + lo // PACK}")
                 for b in range(PACK):
                     cells = slice((lo + b) * P, (lo + b + 1) * P)
-                    turn(bank[:, b, :], gap[:, cells], True, False)
+                    turn(bank[:, b, :], excess[:, cells], True, False)
                     turn(bank[:, b, :], maps[0][t][:, cells], False, True)
                 nc.scalar.copy(turned[:, lo : lo + PACK, t, :], bank[:])
         for lo in (0, PACK):
@@ -248,8 +247,11 @@ def tile_picked_bev_max_lo_kernel(
 
         scatter(1, 2, 0, V)
         gap = tile("gap2", [S], F32, "aside")
-        for lo, hi in parts:
-            difference(2, gap, lo, hi, z_words(lo, hi)[:, :, 1, :])
+        for group in (parts[:2], parts[2:]):
+            cells = slice(group[0][0] * P, group[-1][1] * P)
+            nc.gpsimd.tensor_tensor(gap[:, cells], maps[1][2][:, cells], maps[0][2][:, cells], SUBTRACT)
+            for lo, hi in group:
+                nc.scalar.activation(z_words(lo, hi)[:, :, 1, :], by_group(gap[:, lo * P : hi * P]), RELU)
         for lo, hi in parts:
             a_map = by_group(maps[0][2][:, lo * P : hi * P])
             nc.gpsimd.tensor_tensor(slot(2, lo, hi), a_map, z_words(lo, hi)[:, :, 1, :], ADD)

@@ -105,7 +105,10 @@ def tile_picked_bev_max_lo_kernel(
 
         def gather_rounded(j):
             rounded = tile(f"x_rounded{j}", [T], BF16)
-            nc.scalar.copy(rounded[:], x_planes[j][:])
+            if j:
+                nc.gpsimd.tensor_scalar(rounded[:], x_planes[j][:], 1.0, 0.0, MULT, ADD)
+            else:
+                nc.scalar.copy(rounded[:], x_planes[j][:])
             nc.scalar.activation(picked[:, j, :], rounded[:].indirect(entries(1, 0, V)), COPY)
 
         for j in range(PACK - 1):

@@ -105,7 +105,7 @@ def tile_picked_bev_max_lo_kernel(
 
         def gather_rounded(j):
             rounded = tile(f"x_rounded{j}", [T], BF16)
-            if j:
+            if j == 2:
                 nc.gpsimd.tensor_scalar(rounded[:], x_planes[j][:], 1.0, 0.0, MULT, ADD)
             else:
                 nc.scalar.copy(rounded[:], x_planes[j][:])
@@ -113,7 +113,7 @@ def tile_picked_bev_max_lo_kernel(
 
         for j in range(PACK - 1):
             gather_in_place(j, 0, V)
-            (gather if j % 2 else gather_rounded)(j)
+            gather_rounded(j)
         for lo in (0, half):
             gather_in_place(PACK - 1, lo, lo + half)
 
@@ -162,13 +162,16 @@ def tile_picked_bev_max_lo_kernel(
             nc.scalar.copy(*slot_views(part, w1_raw[g][:], 2))
         last = quantized("w1_last", last_grouped[:].rearrange("p t c -> p (t c)"))
         for u in range(2):
-            multiply(banks[2][:, u * half : (u + 1) * half], columns(following, 0, P), columns(x0[u], 0, half))
+            multiply(banks[2 + u][:, u * half : (u + 1) * half], columns(following, 0, P), columns(x0[u], 0, half))
         activate(0, 0, banks[0], 0, half)
         scatter(0, 0, 0, half)
         activate(0, 0, banks[1], half, V, "w1_raw1")
         scatter(0, 0, half, V)
 
-        activate(0, 1, banks[2], 0, V)
+        a1_acts = tile("act0_1_0", [V], F32)
+        for u in range(2):
+            activate(0, 1, banks[2 + u], u * half, (u + 1) * half, into=a1_acts[:, u * half : (u + 1) * half])
+        acts[0, 1, 0] = a1_acts[:]
         scatter(0, 1, 0, V)
         x1_grouped = buffer("x1_grouped", V, "w1_next_codes")
         nc.scalar.copy(*weave_views(x1_grouped[:], picked[:]))
@@ -177,7 +180,10 @@ def tile_picked_bev_max_lo_kernel(
         deal_aside(pair_views(w2_grouped[:, 0].rearrange("p t c -> p (t c)"), w2_raw[:]))
         deal_aside(slot_views(w2_grouped[:, 1], w2_raw[:], 2))
         second = quantized("w2", w2_grouped[:].rearrange("p a t c -> p (a t c)"))
-        for t in range(PACK - 1):
+        e0_banks = ((banks[PACK], 0, half), (banks[2 * PACK - 1], half, V))
+        for bank, lo, hi in e0_banks:
+            multiply(bank[:, lo:hi], columns(second, 0, P), columns(x1, lo, hi))
+        for t in range(1, PACK - 1):
             multiply(banks[PACK + t][:], columns(second, t * P, (t + 1) * P), columns(x1, 0, V))
 
         def first_sensor(t, bank):
@@ -189,7 +195,10 @@ def tile_picked_bev_max_lo_kernel(
         scatter(0, 2, 0, half)
         w3_grouped = tile("w3_grouped", [PACK, P * PACK], BF16, "aside")
         deal_aside(slot_views(w3_grouped[:], w3_raw[:], 0))
-        activate(1, 0, banks[PACK], 0, V)
+        e0_acts = tile("act1_0_0", [V], F32)
+        for bank, lo, hi in e0_banks:
+            activate(1, 0, bank, lo, hi, into=e0_acts[:, lo:hi])
+        acts[1, 0, 0] = e0_acts[:]
         scatter(1, 0, 0, V)
         third = quantized("w3", w3_grouped[:].rearrange("p t c -> p (t c)"))
         late = tile("late_acts", [PACK - 1, V], F32, "w3_raw")
@@ -319,20 +328,33 @@ def tile_picked_bev_max_lo_kernel(
             nc.sync.dma_start(out_rows[:, :, lo * P : hi * P], result[:])
             results.append(result)
         out_grouped = buffer("out_grouped", S, f"z_grouped{EARLY}")
-        done = 0
-        for (lo, hi), result, upto in zip(spans, results, (0, 0, 4, 6, 8)):
+        def store_scales(cells):
+            for q in range(P // 32):
+                queue = nc.scalar if q % 2 else nc.sync
+                queue.dma_start(
+                    out_2[0, 4 * q : 4 * q + 4, cells].bitcast(I32), out_scales[32 * q : 32 * q + 4, cells].bitcast(I32)
+                )
+
+        def planes(lo, hi):
+            cells = slice(lo * P, hi * P)
+            nc.vector.quantize_mx(
+                out=out_codes[:, cells].bitcast(FP8X4), scales=out_scales[:, cells],
+                in_=out_grouped[:, lo * P * PACK : hi * P * PACK],
+            )
+
+        def store_words(lo, hi):
+            nc.sync.dma_start(out_words[:, lo * P : hi * P], out_codes[:, lo * P : hi * P].bitcast(I32))
+
+        for (lo, hi), result in zip(spans, results):
             copy = nc.scalar.copy if hi == S // P else nc.vector.tensor_copy
             copy(*weave_views(out_grouped[:, lo * P * PACK : hi * P * PACK], result[:]))
-            if upto > done:
-                cells = slice(done * P, upto * P)
-                nc.vector.quantize_mx(
-                    out=out_codes[:, cells].bitcast(FP8X4), scales=out_scales[:, cells],
-                    in_=out_grouped[:, done * P * PACK : upto * P * PACK],
-                )
-                nc.sync.dma_start(out_words[:, cells], out_codes[:, cells].bitcast(I32))
-                done = upto
-        for q in range(P // 32):
-            queue = nc.scalar if q % 2 else nc.sync
-            queue.dma_start(
-                out_2[0, 4 * q : 4 * q + 4, :].bitcast(I32), out_scales[32 * q : 32 * q + 4, :].bitcast(I32)
-            )
+            if hi == EARLY:
+                planes(0, 4)
+                store_words(0, 4)
+            if hi == 7:
+                planes(4, 6)
+                planes(6, 7)
+                store_words(4, 7)
+        planes(7, 8)
+        store_words(7, 8)
+        store_scales(slice(0, S))

@@ -67,7 +67,9 @@ def tile_picked_bev_max_lo_kernel(
         maps = [[tile(f"map{s}_{t}", [S], F32) for t in range(PACK)] for s in range(2)]
         for s in range(2):
             for t in range(PACK):
-                nc.gpsimd.memset(maps[s][t][:].bitcast(I32), 0)
+                (nc.gpsimd if s else nc.vector).memset(maps[s][t][:].bitcast(I32), 0)
+        identity = tile("identity", [P], F32)
+        make_identity(nc, identity[:])
 
         def weave_views(grouped, planes):
             return (
@@ -100,34 +102,35 @@ def tile_picked_bev_max_lo_kernel(
             slots = x0_grouped[:].rearrange("p (c j) -> p c j", j=PACK)
             nc.vector.tensor_copy(slots[:, lo:hi, j], x_planes[j][:].indirect(entries(0, lo, hi)))
 
-        def gather(j):
-            nc.vector.tensor_copy(picked[:, j, :], x_planes[j][:].indirect(entries(1, 0, V)))
+        def gather(j, lo, hi):
+            nc.vector.tensor_copy(picked[:, j, lo:hi], x_planes[j][:].indirect(entries(1, lo, hi)))
 
-        def gather_rounded(j):
-            rounded = tile(f"x_rounded{j}", [T], BF16)
-            if j == 2:
-                nc.gpsimd.tensor_scalar(rounded[:], x_planes[j][:], 1.0, 0.0, MULT, ADD)
-            else:
-                nc.scalar.copy(rounded[:], x_planes[j][:])
-            nc.scalar.activation(picked[:, j, :], rounded[:].indirect(entries(1, 0, V)), COPY)
+        rounded = [tile(f"x_rounded{j}", [T], BF16) for j in range(PACK - 1)]
 
-        for j in range(PACK - 1):
+        def gather_rounded(j, lo, hi):
+            nc.scalar.activation(picked[:, j, lo:hi], rounded[j][:].indirect(entries(1, lo, hi)), COPY)
+
+        for j in range(2):
             gather_in_place(j, 0, V)
-            gather_rounded(j)
+            nc.scalar.copy(rounded[j][:], x_planes[j][:])
+            gather_rounded(j, 0, V)
+        gather_in_place(2, 0, V)
+        nc.gpsimd.tensor_scalar(rounded[2][:], x_planes[2][:], 1.0, 0.0, MULT, ADD)
+        gather_rounded(2, 0, half)
+        gather(2, half, V)
         for lo in (0, half):
             gather_in_place(PACK - 1, lo, lo + half)
 
-        def pair_views(grouped, raw):
+        def pair_views(grouped, raw, order):
             return (
-                grouped.rearrange("p (m u j) -> p m u j", u=2, j=PACK),
-                raw.rearrange("p j (m t) -> p m t j", t=PACK)[:, :, :2, :],
+                grouped.rearrange(f"p (m t j) -> p m {order}", t=2, j=PACK),
+                raw.rearrange("p j (m t) -> p j m t", t=PACK)[:, :, :, :2].rearrange(f"p j m t -> p m {order}"),
             )
 
-        def slot_views(grouped, raw, first):
-            count = PACK - first
+        def slot_views(grouped, raw, first, order):
             return (
-                grouped.rearrange("p t (m j) -> p m t j", j=PACK),
-                raw.rearrange("p j (m t) -> p m t j", t=PACK)[:, :, first : first + count, :],
+                grouped.rearrange(f"p t (m j) -> p m {order}", j=PACK),
+                raw.rearrange("p j (m t) -> p j m t", t=PACK)[:, :, :, first:].rearrange(f"p j m t -> p m {order}"),
             )
 
         def deal_aside(views):
@@ -146,20 +149,21 @@ def tile_picked_bev_max_lo_kernel(
             cells = cell_lists[s][:, lo // LIST_ROWS : hi // LIST_ROWS]
             nc.vector.tensor_copy(maps[s][t][:].indirect(cells), acts[s, t, lo])
 
-        nc.scalar.copy(*pair_views(picked[:, PACK - 1, :], w1_raw[0][:]))
+        first_w1 = picked[:, PACK - 1, :]
+        nc.scalar.copy(*pair_views(first_w1, w1_raw[0][:], "j t"))
         x0 = [quantized("x0_0", x0_grouped[:, : half * PACK])]
-        first = quantized("w1_first", picked[:, PACK - 1, :])
+        first = quantized("w1_first", first_w1)
         x0.append(quantized("x0_1", x0_grouped[:, half * PACK :]))
         for u in range(2):
             multiply(banks[u][:, u * half : (u + 1) * half], columns(first, 0, P), columns(x0[u], 0, half))
-        gather(PACK - 1)
+        gather(PACK - 1, 0, V)
         next_grouped = buffer("w1_next_grouped", P)
-        nc.scalar.copy(*pair_views(next_grouped[:], w1_raw[1][:]))
+        nc.scalar.copy(*pair_views(next_grouped[:], w1_raw[1][:], "j t"))
         following = quantized("w1_next", next_grouped[:])
         last_grouped = tile("w1_last_grouped", [2, P * PACK], BF16, "aside")
         for g in range(2):
             part = last_grouped[:, :, g * P * PACK // 2 : (g + 1) * P * PACK // 2]
-            nc.scalar.copy(*slot_views(part, w1_raw[g][:], 2))
+            nc.scalar.copy(*slot_views(part, w1_raw[g][:], 2, "j t"))
         last = quantized("w1_last", last_grouped[:].rearrange("p t c -> p (t c)"))
         for u in range(2):
             multiply(banks[2 + u][:, u * half : (u + 1) * half], columns(following, 0, P), columns(x0[u], 0, half))
@@ -177,8 +181,8 @@ def tile_picked_bev_max_lo_kernel(
         nc.scalar.copy(*weave_views(x1_grouped[:], picked[:]))
         x1 = quantized("x1", x1_grouped[:])
         w2_grouped = tile("w2_grouped", [2, 2, P * PACK], BF16, "aside")
-        deal_aside(pair_views(w2_grouped[:, 0].rearrange("p t c -> p (t c)"), w2_raw[:]))
-        deal_aside(slot_views(w2_grouped[:, 1], w2_raw[:], 2))
+        deal_aside(pair_views(w2_grouped[:, 0].rearrange("p t c -> p (t c)"), w2_raw[:], "t j"))
+        deal_aside(slot_views(w2_grouped[:, 1], w2_raw[:], 2, "t j"))
         second = quantized("w2", w2_grouped[:].rearrange("p a t c -> p (a t c)"))
         e0_banks = ((banks[PACK], 0, half), (banks[2 * PACK - 1], half, V))
         for bank, lo, hi in e0_banks:
@@ -194,7 +198,7 @@ def tile_picked_bev_max_lo_kernel(
         activate(0, 2, banks[3], 0, half, "w2_raw")
         scatter(0, 2, 0, half)
         w3_grouped = tile("w3_grouped", [PACK, P * PACK], BF16, "aside")
-        deal_aside(slot_views(w3_grouped[:], w3_raw[:], 0))
+        deal_aside(slot_views(w3_grouped[:], w3_raw[:], 0, "t j"))
         e0_acts = tile("act1_0_0", [V], F32)
         for bank, lo, hi in e0_banks:
             activate(1, 0, bank, lo, hi, into=e0_acts[:, lo:hi])
@@ -227,8 +231,6 @@ def tile_picked_bev_max_lo_kernel(
         def by_group(ap):
             return ap.rearrange("p (g r) -> p g r", r=P)
 
-        identity = tile("identity", [P], F32)
-        make_identity(nc, identity[:])
         turned = tile("turned", [S // P, 2, P], BF16)
 
         def turn(out, block, start, stop):

@@ -64,12 +64,17 @@ def tile_picked_bev_max_lo_kernel(
         nc.sync.dma_start(w2_raw[:], w2.rearrange("(p j) c -> p j c", j=PACK))
         nc.sync.dma_start(w3_raw[:], w3.rearrange("(p j) c -> p j c", j=PACK))
 
-        maps = [[tile(f"map{s}_{t}", [S], F32) for t in range(PACK)] for s in range(2)]
-        for s in range(2):
-            for t in range(PACK):
-                (nc.gpsimd if s else nc.vector).memset(maps[s][t][:].bitcast(I32), 0)
         identity = tile("identity", [P], F32)
         make_identity(nc, identity[:])
+        maps = [[], []]
+
+        def clear(s, t, tag=None):
+            maps[s].append(tile(f"map{s}_{t}", [S], F32, tag))
+            nc.gpsimd.memset(maps[s][t][:].bitcast(I32), 0)
+
+        for s in range(2):
+            for t in range(PACK - s):
+                clear(s, t)
 
         def weave_views(grouped, planes):
             return (
@@ -157,6 +162,7 @@ def tile_picked_bev_max_lo_kernel(
         for u in range(2):
             multiply(banks[u][:, u * half : (u + 1) * half], columns(first, 0, P), columns(x0[u], 0, half))
         gather(PACK - 1, 0, V)
+        clear(1, PACK - 1, "x0_grouped")
         next_grouped = buffer("w1_next_grouped", P)
         nc.scalar.copy(*pair_views(next_grouped[:], w1_raw[1][:], "j t"))
         following = quantized("w1_next", next_grouped[:])

@@ -332,8 +332,9 @@ def tile_picked_bev_max_lo_kernel(
             result = tile(f"result{lo}", [PACK, (hi - lo) * P], F32)
             for b in range(lo, hi):
                 first_row = (b - lo) * per_bank
-                nc.scalar.copy(result[:, first_row : first_row + per_bank, :], out_banks[b][:])
-            nc.sync.dma_start(out_rows[:, :, lo * P : hi * P], result[:])
+                rows = slice(first_row, first_row + per_bank)
+                nc.scalar.copy(result[:, rows, :], out_banks[b][:])
+                nc.sync.dma_start(out_rows[:, rows, lo * P : hi * P], result[:, rows, :])
             results.append(result)
         out_grouped = buffer("out_grouped", S, f"z_grouped{EARLY}")
         def store_scales(cells):

@@ -201,8 +201,8 @@ def tile_picked_bev_max_lo_kernel(
                 multiply(bank[:, u * half : (u + 1) * half], columns(last, (t - 2) * P, (t - 1) * P), columns(x0[u], 0, half))
 
         first_sensor(2, banks[3])
-        activate(0, 2, banks[3], 0, half, "w2_raw")
-        scatter(0, 2, 0, half)
+        activate(0, 2, banks[3], 0, MOST, "w2_raw")
+        scatter(0, 2, 0, MOST)
         w3_grouped = tile("w3_grouped", [PACK, P * PACK], BF16, "aside")
         deal_aside(slot_views(w3_grouped[:], w3_raw[:], 0, "t j"))
         e0_acts = tile("act1_0_0", [V], F32)
@@ -215,8 +215,8 @@ def tile_picked_bev_max_lo_kernel(
 
         activate(1, 1, banks[PACK + 1], 0, V, into=late[:, 0, :])
         scatter(1, 1, 0, V)
-        activate(0, 2, banks[3], half, V, into=late[:, 2, half:])
-        scatter(0, 2, half, V)
+        activate(0, 2, banks[3], MOST, V, into=late[:, 2, MOST:])
+        scatter(0, 2, MOST, V)
         activate(1, 2, banks[PACK + 2], 0, V, into=late[:, 1, :])
         first_sensor(3, banks[PACK + 2])
         activate(0, 3, banks[PACK + 2], 0, V)
@@ -354,16 +354,21 @@ def tile_picked_bev_max_lo_kernel(
         def store_words(lo, hi):
             nc.sync.dma_start(out_words[:, lo * P : hi * P], out_codes[:, lo * P : hi * P].bitcast(I32))
 
-        for (lo, hi), result in zip(spans, results):
-            copy = nc.scalar.copy if hi == S // P else nc.vector.tensor_copy
-            copy(*weave_views(out_grouped[:, lo * P * PACK : hi * P * PACK], result[:]))
-            if hi == EARLY:
-                planes(0, 4)
-                store_words(0, 4)
-            if hi == 7:
-                planes(4, 6)
-                planes(6, 7)
-                store_words(4, 7)
+        def weave(chunk, first_group, last_group, copy):
+            lo = spans[chunk][0]
+            part = results[chunk][:, :, (first_group - lo) * P : (last_group - lo) * P]
+            copy(*weave_views(out_grouped[:, first_group * P * PACK : last_group * P * PACK], part))
+
+        for chunk in range(3):
+            weave(chunk, *spans[chunk], nc.vector.tensor_copy)
+        weave(3, 6, 7, nc.scalar.copy)
+        weave(4, 7, 8, nc.scalar.copy)
+        planes(0, 4)
+        store_words(0, 4)
+        weave(3, 5, 6, nc.vector.tensor_copy)
+        planes(4, 6)
+        planes(6, 7)
+        store_words(4, 7)
         planes(7, 8)
         store_words(7, 8)
         store_scales(slice(0, S))

@@ -27,6 +27,7 @@ LIST_ROWS = 16
 EARLY = 5
 MOST = 384
 WARM = 4
+TAIL = 32
 
 
 def tile_picked_bev_max_lo_kernel(
@@ -203,14 +204,18 @@ def tile_picked_bev_max_lo_kernel(
         first_sensor(2, banks[3])
         activate(0, 2, banks[3], 0, MOST, "w2_raw")
         scatter(0, 2, 0, MOST)
-        w3_grouped = tile("w3_grouped", [PACK, P * PACK], BF16, "aside")
-        deal_aside(slot_views(w3_grouped[:], w3_raw[:], 0, "t j"))
+        w3_space = tile("w3_grouped", [(H - TAIL) * PACK + PACK * P], BF16, "aside")
+        w3_grouped = w3_space[:, : H * PACK]
+        w3_views = slot_views(w3_grouped.rearrange("p (t c) -> p t c", t=PACK), w3_raw[:], 0, "t j")
+        deal_aside([view[:, :, : PACK - 1] for view in w3_views])
+        deal_aside([view[:, : P - TAIL, PACK - 1] for view in w3_views])
+        w3_rest = tile("w3_rest", [TAIL, PACK], F32)
+        deal_aside([w3_rest[:], w3_views[1][:, P - TAIL :, PACK - 1]])
         e0_acts = tile("act1_0_0", [V], F32)
         for bank, lo, hi in e0_banks:
             activate(1, 0, bank, lo, hi, into=e0_acts[:, lo:hi])
         acts[1, 0, 0] = e0_acts[:]
         scatter(1, 0, 0, V)
-        third = quantized("w3", w3_grouped[:].rearrange("p t c -> p (t c)"))
         late = tile("late_acts", [PACK - 1, V], F32, "w3_raw")
 
         activate(1, 1, banks[PACK + 1], 0, V, into=late[:, 0, :])
@@ -224,7 +229,9 @@ def tile_picked_bev_max_lo_kernel(
         activate(1, 3, banks[PACK + 1], 0, MOST, "act1_0_0")
 
         parts = ((0, 1), (1, EARLY), (EARLY, S // P))
-        z_parts = [tile(f"z_words{lo}", [hi - lo, 2, P], F32) for lo, hi in parts]
+        first_words = w3_space[:, (H - TAIL) * PACK :].bitcast(F32)
+        z_parts = [first_words.rearrange("p (g u r) -> p g u r", g=1, u=2)]
+        z_parts += [tile(f"z_words{lo}", [hi - lo, 2, P], F32) for lo, hi in parts[1:]]
 
         def z_words(lo, hi):
             (start, part), = [(a, part) for (a, b), part in zip(parts, z_parts) if a <= lo < b]
@@ -248,7 +255,7 @@ def tile_picked_bev_max_lo_kernel(
             nc.scalar.activation(excess, by_group(gap[:, cells]), RELU)
 
         for t in range(2):
-            gap, excess = tile(f"gap{t}", [S], F32, "aside"), tile(f"excess{t}", [S], F32)
+            gap, excess = tile(f"gap{t}", [S], F32, "gap"), tile(f"excess{t}", [S], F32)
             for lo in (0, PACK):
                 difference(t, gap, lo, lo + PACK, by_group(excess[:, lo * P : (lo + PACK) * P]))
             for lo in (0, PACK):
@@ -266,7 +273,7 @@ def tile_picked_bev_max_lo_kernel(
                 nc.scalar.copy(z_words(first_group, last_group)[:, :, 0, :], bank[:, first_group - lo : last_group - lo, :])
 
         scatter(1, 2, 0, V)
-        gap = tile("gap2", [S], F32, "aside")
+        gap = tile("gap2", [S], F32, "gap")
         for group in (parts[:2], parts[2:]):
             cells = slice(group[0][0] * P, group[-1][1] * P)
             nc.gpsimd.tensor_tensor(gap[:, cells], maps[1][2][:, cells], maps[0][2][:, cells], SUBTRACT)
@@ -282,11 +289,13 @@ def tile_picked_bev_max_lo_kernel(
             first_grouped[:].bitcast(F32).rearrange("p (r u) -> p r u", u=2),
             z_parts[0][:, 0].rearrange("p u r -> p r u"),
         )
-        activate(1, 3, banks[PACK + 1], MOST, V, "z_words0")
+        activate(1, 3, banks[PACK + 1], MOST, V, into=first_words[:, P:])
         scatter(1, 3, MOST, V)
+        nc.scalar.copy(w3_grouped[:, H * PACK - TAIL * PACK :], w3_rest[:].rearrange("p m j -> p (m j)"))
+        third = quantized("w3", w3_grouped)
         spare = psum.tile([P, V], F32, name="spare", tag=f"bank{PACK + 1}")
         for t in range(WARM):
-            multiply(spare[:], columns(third, t * P, (t + 1) * P), columns(x1, 0, V))
+            multiply(spare[:], columns(second, t * P, (t + 1) * P), columns(x1, 0, V))
         last_maps = [maps[s][PACK - 1] for s in range(2)]
         first_slots = first_grouped[:].rearrange("p (c t) -> p c t", t=PACK)
         nc.vector.tensor_tensor(first_slots[:, :, PACK - 1], last_maps[0][:, :P], last_maps[1][:, :P], MAX)

@@ -51,7 +51,8 @@ def tile_picked_bev_max_lo_kernel(
         x_rows = xT.rearrange("(p j) c -> p j c", j=PACK)
         x_planes = [tile(f"x{j}", [T], F32) for j in range(PACK)]
         w1_rows = w1.rearrange("(p j) c -> p j c", j=PACK)
-        w1_raw = [tile(f"w1_raw{g}", [PACK, H // 2], F32) for g in range(2)]
+        w1_runs = ((0, P), (P, 2 * P), (2 * P, H))
+        w1_raw = [tile(f"w1_raw{g}", [PACK, hi - lo], F32) for g, (lo, hi) in enumerate(w1_runs)]
         w2_raw = tile("w2_raw", [PACK, H], F32)
         w3_raw = tile("w3_raw", [PACK, H], F32)
 
@@ -59,9 +60,10 @@ def tile_picked_bev_max_lo_kernel(
         nc.sync.dma_start(offs_sb[:], offs)
         for j in range(1, PACK):
             nc.sync.dma_start(x_planes[j][:], x_rows[:, j, :])
-        for g in range(2):
-            nc.sync.dma_start(w1_raw[g][:], w1_rows[:, :, g * H // 2 : (g + 1) * H // 2])
-            nc.sync.dma_start(cell_lists[g][:], (near, far)[g])
+        for raw, (lo, hi) in zip(w1_raw, w1_runs):
+            nc.sync.dma_start(raw[:], w1_rows[:, :, lo:hi])
+        for cell_list, source in zip(cell_lists, (near, far)):
+            nc.sync.dma_start(cell_list[:], source)
         nc.sync.dma_start(w2_raw[:], w2.rearrange("(p j) c -> p j c", j=PACK))
         nc.sync.dma_start(w3_raw[:], w3.rearrange("(p j) c -> p j c", j=PACK))
 
@@ -99,7 +101,7 @@ def tile_picked_bev_max_lo_kernel(
             )
 
         x0_grouped = buffer("x0_grouped", V)
-        picked = tile("picked", [PACK, V], BF16)
+        picked = tile("picked", [PACK, V + half], BF16)
 
         def entries(s, lo, hi):
             return offs_sb[:, (s * V + lo) // LIST_ROWS : (s * V + hi) // LIST_ROWS]
@@ -122,8 +124,7 @@ def tile_picked_bev_max_lo_kernel(
             gather_rounded(j, 0, V)
         gather_in_place(2, 0, V)
         nc.gpsimd.tensor_scalar(rounded[2][:], x_planes[2][:], 1.0, 0.0, MULT, ADD)
-        gather_rounded(2, 0, half)
-        gather(2, half, V)
+        gather(2, 0, half)
         for lo in (0, half):
             gather_in_place(PACK - 1, lo, lo + half)
 
@@ -155,8 +156,9 @@ def tile_picked_bev_max_lo_kernel(
             cells = cell_lists[s][:, lo // LIST_ROWS : hi // LIST_ROWS]
             nc.vector.tensor_copy(maps[s][t][:].indirect(cells), acts[s, t, lo])
 
-        first_w1 = picked[:, PACK - 1, :]
-        nc.scalar.copy(*pair_views(first_w1, w1_raw[0][:], "j t"))
+        first_w1 = picked[:, PACK - 1, :V]
+        for g in range(2):
+            nc.scalar.copy(*pair_views(first_w1[:, g * 2 * P : (g + 1) * 2 * P], w1_raw[g][:], "j t"))
         x0 = [quantized("x0_0", x0_grouped[:, : half * PACK])]
         first = quantized("w1_first", first_w1)
         x0.append(quantized("x0_1", x0_grouped[:, half * PACK :]))
@@ -164,19 +166,18 @@ def tile_picked_bev_max_lo_kernel(
             multiply(banks[u][:, u * half : (u + 1) * half], columns(first, 0, P), columns(x0[u], 0, half))
         gather(PACK - 1, 0, V)
         clear(1, PACK - 1, "x0_grouped")
-        next_grouped = buffer("w1_next_grouped", P)
-        nc.scalar.copy(*pair_views(next_grouped[:], w1_raw[1][:], "j t"))
-        following = quantized("w1_next", next_grouped[:])
+        next_grouped = picked[:, 2, half:]
+        nc.scalar.copy(*pair_views(next_grouped, w1_raw[2][:], "j t"))
+        following = quantized("w1_next", next_grouped)
         last_grouped = tile("w1_last_grouped", [2, P * PACK], BF16, "aside")
-        for g in range(2):
-            part = last_grouped[:, :, g * P * PACK // 2 : (g + 1) * P * PACK // 2]
-            nc.scalar.copy(*slot_views(part, w1_raw[g][:], 2, "j t"))
+        for raw, (lo, hi) in zip(w1_raw, w1_runs):
+            nc.scalar.copy(*slot_views(last_grouped[:, :, lo:hi], raw[:], 2, "j t"))
         last = quantized("w1_last", last_grouped[:].rearrange("p t c -> p (t c)"))
         for u in range(2):
             multiply(banks[2 + u][:, u * half : (u + 1) * half], columns(following, 0, P), columns(x0[u], 0, half))
         activate(0, 0, banks[0], 0, half)
         scatter(0, 0, 0, half)
-        activate(0, 0, banks[1], half, V, "w1_raw1")
+        activate(0, 0, banks[1], half, V, "w1_raw2")
         scatter(0, 0, half, V)
 
         a1_acts = tile("act0_1_0", [V], F32)
@@ -184,8 +185,9 @@ def tile_picked_bev_max_lo_kernel(
             activate(0, 1, banks[2 + u], u * half, (u + 1) * half, into=a1_acts[:, u * half : (u + 1) * half])
         acts[0, 1, 0] = a1_acts[:]
         scatter(0, 1, 0, V)
+        gather_rounded(2, half, V)
         x1_grouped = buffer("x1_grouped", V, "w1_next_codes")
-        nc.scalar.copy(*weave_views(x1_grouped[:], picked[:]))
+        nc.scalar.copy(*weave_views(x1_grouped[:], picked[:, :, :V]))
         x1 = quantized("x1", x1_grouped[:])
         w2_grouped = tile("w2_grouped", [2, 2, P * PACK], BF16, "aside")
         deal_aside(pair_views(w2_grouped[:, 0].rearrange("p t c -> p (t c)"), w2_raw[:], "t j"))

@@ -162,8 +162,9 @@ def tile_picked_bev_max_lo_kernel(
         x0 = [quantized("x0_0", x0_grouped[:, : half * PACK])]
         first = quantized("w1_first", first_w1)
         x0.append(quantized("x0_1", x0_grouped[:, half * PACK :]))
-        for u in range(2):
-            multiply(banks[u][:, u * half : (u + 1) * half], columns(first, 0, P), columns(x0[u], 0, half))
+        for bank, lo in ((banks[0], 0), (banks[PACK], P)):
+            multiply(bank[:, lo : lo + P], columns(first, 0, P), columns(x0[0], lo, lo + P))
+        multiply(banks[1][:, half:], columns(first, 0, P), columns(x0[1], 0, half))
         gather(PACK - 1, 0, V)
         clear(1, PACK - 1, "x0_grouped")
         next_grouped = picked[:, 2, half:]
@@ -175,7 +176,10 @@ def tile_picked_bev_max_lo_kernel(
         last = quantized("w1_last", last_grouped[:].rearrange("p t c -> p (t c)"))
         for u in range(2):
             multiply(banks[2 + u][:, u * half : (u + 1) * half], columns(following, 0, P), columns(x0[u], 0, half))
-        activate(0, 0, banks[0], 0, half)
+        a0_acts = tile("act0_0_0", [half], F32)
+        for bank, lo in ((banks[0], 0), (banks[PACK], P)):
+            activate(0, 0, bank, lo, lo + P, into=a0_acts[:, lo : lo + P])
+        acts[0, 0, 0] = a0_acts[:]
         scatter(0, 0, 0, half)
         activate(0, 0, banks[1], half, V, "w1_raw2")
         scatter(0, 0, half, V)

@@ -1,7 +1,6 @@
 from contextlib import ExitStack
 
 import concourse.mybir as mybir
-from concourse.masks import make_identity
 
 K, T, S, H, V = 512, 2048, 1024, 512, 512
 FLOPS = 2 * K * H * 2 * V + 2 * H * H * S
@@ -18,16 +17,14 @@ COPY = mybir.ActivationFunctionType.Copy
 MAX = mybir.AluOpType.max
 ADD = mybir.AluOpType.add
 MULT = mybir.AluOpType.mult
-SUBTRACT = mybir.AluOpType.subtract
 
 P = 128
 PACK = 4
 CHUNKS = (1, 2, 2, 2, 1)
 LIST_ROWS = 16
 EARLY = 5
-MOST = 384
-WARM = 4
-TAIL = 32
+SHARE = 256
+FEW = 128
 
 
 def tile_picked_bev_max_lo_kernel(
@@ -50,34 +47,26 @@ def tile_picked_bev_max_lo_kernel(
         cell_lists = [lists.tile([P, V // LIST_ROWS], U16, name=f"cells{s}") for s in range(2)]
         x_rows = xT.rearrange("(p j) c -> p j c", j=PACK)
         x_planes = [tile(f"x{j}", [T], F32) for j in range(PACK)]
-        w1_rows = w1.rearrange("(p j) c -> p j c", j=PACK)
-        w1_runs = ((0, P), (P, 2 * P), (2 * P, H))
-        w1_raw = [tile(f"w1_raw{g}", [PACK, hi - lo], F32) for g, (lo, hi) in enumerate(w1_runs)]
-        w2_raw = tile("w2_raw", [PACK, H], F32)
-        w3_raw = tile("w3_raw", [PACK, H], F32)
+        raws = [tile(f"w{n}_raw", [PACK, H], F32) for n in range(3)]
 
-        nc.sync.dma_start(x_planes[0][:], x_rows[:, 0, :])
+        def load_weights(n, w):
+            nc.sync.dma_start(raws[n][:], w.rearrange("(p j) c -> p j c", j=PACK))
+
+        load_weights(0, w1)
         nc.sync.dma_start(offs_sb[:], offs)
-        for j in range(1, PACK):
+        for j in range(PACK):
             nc.sync.dma_start(x_planes[j][:], x_rows[:, j, :])
-        for raw, (lo, hi) in zip(w1_raw, w1_runs):
-            nc.sync.dma_start(raw[:], w1_rows[:, :, lo:hi])
         for cell_list, source in zip(cell_lists, (near, far)):
             nc.sync.dma_start(cell_list[:], source)
-        nc.sync.dma_start(w2_raw[:], w2.rearrange("(p j) c -> p j c", j=PACK))
-        nc.sync.dma_start(w3_raw[:], w3.rearrange("(p j) c -> p j c", j=PACK))
+        load_weights(1, w2)
+        load_weights(2, w3)
 
-        identity = tile("identity", [P], F32)
-        make_identity(nc, identity[:])
-        maps = [[], []]
-
-        def clear(s, t, tag=None):
-            maps[s].append(tile(f"map{s}_{t}", [S], F32, tag))
-            nc.gpsimd.memset(maps[s][t][:].bitcast(I32), 0)
-
+        maps = [[tile(f"map{s}_{t}", [S], F32) for t in range(PACK)] for s in range(2)]
+        ones = tile("ones", [1], F32)
+        nc.gpsimd.memset(ones[:], 1.0)
         for s in range(2):
-            for t in range(PACK - s):
-                clear(s, t)
+            for t in range(PACK):
+                nc.gpsimd.memset(maps[s][t][:].bitcast(I32), 0)
 
         def weave_views(grouped, planes):
             return (
@@ -85,14 +74,28 @@ def tile_picked_bev_max_lo_kernel(
                 planes.rearrange("p j (c i) -> p c j i", i=PACK),
             )
 
-        def quantized(name, grouped, tag=None):
-            width = grouped.shape[1] // PACK
-            codes, scales = tile(f"{name}_codes", [width], U32, tag), tile(f"{name}_scales", [width], U8)
-            nc.vector.quantize_mx(out=codes[:].bitcast(FP8X4), scales=scales[:], in_=grouped)
-            return codes, scales
+        def deal_views(grouped, raw):
+            return (
+                grouped.rearrange("p (t m j) -> p m t j", t=PACK, j=PACK),
+                raw.rearrange("p j (m t) -> p m t j", t=PACK),
+            )
+
+        def deal_aside(views):
+            nc.gpsimd.tensor_scalar(*views, 1.0, 0.0, MULT, ADD)
+
+        def operand(name, width):
+            return tile(f"{name}_codes", [width], U32), tile(f"{name}_scales", [width], U8)
 
         def columns(pair, lo, hi):
-            return [operand[:, lo:hi] for operand in pair]
+            return [part[:, lo:hi] for part in pair]
+
+        def quantize(target, grouped):
+            nc.vector.quantize_mx(out=target[0].bitcast(FP8X4), scales=target[1], in_=grouped)
+
+        def quantized(name, grouped):
+            pair = operand(name, grouped.shape[1] // PACK)
+            quantize([part[:] for part in pair], grouped)
+            return pair
 
         def multiply(out, stationary, moving):
             nc.tensor.matmul_mx(
@@ -100,211 +103,107 @@ def tile_picked_bev_max_lo_kernel(
                 rhs=moving[0].bitcast(FP8X4), rhs_scale=moving[1], start=True, stop=True,
             )
 
-        x0_grouped = buffer("x0_grouped", V)
-        picked = tile("picked", [PACK, V + half], BF16)
+        w1_grouped = buffer("w1_grouped", H)
+        nc.scalar.copy(*deal_views(w1_grouped[:], raws[0][:]))
+        first = quantized("w1", w1_grouped[:])
 
-        def entries(s, lo, hi):
-            return offs_sb[:, (s * V + lo) // LIST_ROWS : (s * V + hi) // LIST_ROWS]
+        picked = buffer("picked", S)
 
-        def gather_in_place(j, lo, hi):
-            slots = x0_grouped[:].rearrange("p (c j) -> p c j", j=PACK)
-            nc.vector.tensor_copy(slots[:, lo:hi, j], x_planes[j][:].indirect(entries(0, lo, hi)))
-
-        def gather(j, lo, hi):
-            nc.vector.tensor_copy(picked[:, j, lo:hi], x_planes[j][:].indirect(entries(1, lo, hi)))
-
-        rounded = [tile(f"x_rounded{j}", [T], BF16) for j in range(PACK - 1)]
-
-        def gather_rounded(j, lo, hi):
-            nc.scalar.activation(picked[:, j, lo:hi], rounded[j][:].indirect(entries(1, lo, hi)), COPY)
+        def gather(engine, j, lo, hi):
+            slots = picked[:].rearrange("p (c j) -> p c j", j=PACK)[:, lo:hi, j]
+            window = x_planes[j][:].indirect(offs_sb[:, lo // LIST_ROWS : hi // LIST_ROWS])
+            if engine == "vector":
+                nc.vector.tensor_copy(slots, window)
+            else:
+                nc.scalar.activation(slots, window, COPY)
 
         for j in range(2):
-            gather_in_place(j, 0, V)
-            nc.scalar.copy(rounded[j][:], x_planes[j][:])
-            gather_rounded(j, 0, V)
-        gather_in_place(2, 0, V)
-        nc.gpsimd.tensor_scalar(rounded[2][:], x_planes[2][:], 1.0, 0.0, MULT, ADD)
-        gather(2, 0, half)
-        for lo in (0, half):
-            gather_in_place(PACK - 1, lo, lo + half)
+            gather("vector", j, 0, V)
+            gather("scalar", j, V, S)
+        for j in range(2, PACK):
+            gather("scalar", j, 0, half)
+            gather("vector", j, half, V + FEW)
+            gather("scalar", j, V + FEW, S)
+        xs = [operand(f"x{s}", V) for s in range(2)]
+        for u in range(2):
+            quantize(columns(xs[0], u * half, (u + 1) * half), picked[:, u * half * PACK : (u + 1) * half * PACK])
+        quantize(columns(xs[1], 0, V), picked[:, V * PACK :])
 
-        def pair_views(grouped, raw, order):
-            return (
-                grouped.rearrange(f"p (m t j) -> p m {order}", t=2, j=PACK),
-                raw.rearrange("p j (m t) -> p j m t", t=PACK)[:, :, :, :2].rearrange(f"p j m t -> p m {order}"),
-            )
-
-        def slot_views(grouped, raw, first, order):
-            return (
-                grouped.rearrange(f"p t (m j) -> p m {order}", j=PACK),
-                raw.rearrange("p j (m t) -> p j m t", t=PACK)[:, :, :, first:].rearrange(f"p j m t -> p m {order}"),
-            )
-
-        def deal_aside(views):
-            nc.gpsimd.tensor_scalar(*views, 1.0, 0.0, MULT, ADD)
-
-        banks = [psum.tile([P, V], F32, name=f"bank{b}", tag=f"bank{b}") for b in range(2 * PACK)]
+        banks = [[psum.tile([P, V], F32, name=f"bank{s}_{t}", tag=f"bank{s * PACK + t}") for t in range(PACK - s)] + [None] * s for s in range(2)]
         acts = {}
 
-        def activate(s, t, bank, lo, hi, tag=None, into=None):
-            if into is None:
-                into = tile(f"act{s}_{t}_{lo}", [hi - lo], F32, tag)[:]
-            acts[s, t, lo] = into
-            nc.scalar.activation(into, bank[:, lo:hi], RELU)
+        def activate(s, t, into, engine="scalar", lo=0, hi=V):
+            acts[s, t] = into
+            if engine == "scalar":
+                nc.scalar.activation(into[:, lo:hi], banks[s][t][:, lo:hi], RELU)
+            else:
+                nc.vector.tensor_scalar_max(into[:, lo:hi], banks[s][t][:, lo:hi], 0.0)
 
-        def scatter(s, t, lo, hi):
-            cells = cell_lists[s][:, lo // LIST_ROWS : hi // LIST_ROWS]
-            nc.vector.tensor_copy(maps[s][t][:].indirect(cells), acts[s, t, lo])
+        def scatter(s, t, engine, lo=0, hi=V):
+            window = maps[s][t][:].indirect(cell_lists[s][:, lo // LIST_ROWS : hi // LIST_ROWS])
+            if engine == "scalar":
+                nc.scalar.activation(window, acts[s, t][:, lo:hi], COPY, scale=ones[:])
+            else:
+                nc.vector.tensor_copy(window, acts[s, t][:, lo:hi])
 
-        first_w1 = picked[:, PACK - 1, :V]
-        for g in range(2):
-            nc.scalar.copy(*pair_views(first_w1[:, g * 2 * P : (g + 1) * 2 * P], w1_raw[g][:], "j t"))
-        x0 = [quantized("x0_0", x0_grouped[:, : half * PACK])]
-        first = quantized("w1_first", first_w1)
-        x0.append(quantized("x0_1", x0_grouped[:, half * PACK :]))
-        for bank, lo in ((banks[0], 0), (banks[PACK], P)):
-            multiply(bank[:, lo : lo + P], columns(first, 0, P), columns(x0[0], lo, lo + P))
-        multiply(banks[1][:, half:], columns(first, 0, P), columns(x0[1], 0, half))
-        gather(PACK - 1, 0, V)
-        clear(1, PACK - 1, "x0_grouped")
-        next_grouped = picked[:, 2, half:]
-        nc.scalar.copy(*pair_views(next_grouped, w1_raw[2][:], "j t"))
-        following = quantized("w1_next", next_grouped)
-        last_grouped = tile("w1_last_grouped", [2, P * PACK], BF16, "aside")
-        for raw, (lo, hi) in zip(w1_raw, w1_runs):
-            nc.scalar.copy(*slot_views(last_grouped[:, :, lo:hi], raw[:], 2, "j t"))
-        last = quantized("w1_last", last_grouped[:].rearrange("p t c -> p (t c)"))
-        for u in range(2):
-            multiply(banks[2 + u][:, u * half : (u + 1) * half], columns(following, 0, P), columns(x0[u], 0, half))
-        a0_acts = tile("act0_0_0", [half], F32)
-        for bank, lo in ((banks[0], 0), (banks[PACK], P)):
-            activate(0, 0, bank, lo, lo + P, into=a0_acts[:, lo : lo + P])
-        acts[0, 0, 0] = a0_acts[:]
-        scatter(0, 0, 0, half)
-        activate(0, 0, banks[1], half, V, "w1_raw2")
-        scatter(0, 0, half, V)
+        early = [tile(f"act0_{t}", [V], F32)[:] for t in (0, 1, 3)]
+        split = psum.tile([P, V], F32, name="split", tag=f"bank{2 * PACK - 1}")
+        multiply(split[:, :half], columns(first, 0, P), columns(xs[0], 0, half))
+        multiply(banks[0][0][:, half:], columns(first, 0, P), columns(xs[0], half, V))
+        for t in (1, 2, 3):
+            multiply(banks[0][t][:], columns(first, t * P, (t + 1) * P), columns(xs[0], 0, V))
+        nc.scalar.activation(early[0][:, :half], split[:, :half], RELU)
+        activate(0, 0, early[0], lo=half)
+        activate(0, 1, early[1])
+        scatter(0, 0, "vector")
+        scatter(0, 1, "scalar")
+        w2_grouped = buffer("w2_grouped", H, "picked")
+        deal_aside(deal_views(w2_grouped[:], raws[1][:]))
+        w3_grouped = buffer("w3_grouped", H)
+        deal_aside(deal_views(w3_grouped[:], raws[2][:]))
+        activate(0, 2, tile("act0_2", [V], F32, "w1_raw")[:], "vector")
+        second = quantized("w2", w2_grouped[:])
+        activate(0, 3, early[2])
+        scatter(0, 2, "vector")
+        scatter(0, 3, "scalar")
+        third = quantized("w3", w3_grouped[:])
+        banks[1][PACK - 1] = psum.tile([P, V], F32, name="bank_last", tag=f"bank{2 * PACK - 1}")
+        for t in (0, 2, 1, 3):
+            multiply(banks[1][t][:], columns(second, t * P, (t + 1) * P), columns(xs[1], 0, V))
+        late = tile("late_acts", [PACK, V], F32, "w2_raw")
 
-        a1_acts = tile("act0_1_0", [V], F32)
-        for u in range(2):
-            activate(0, 1, banks[2 + u], u * half, (u + 1) * half, into=a1_acts[:, u * half : (u + 1) * half])
-        acts[0, 1, 0] = a1_acts[:]
-        scatter(0, 1, 0, V)
-        gather_rounded(2, half, V)
-        x1_grouped = buffer("x1_grouped", V, "w1_next_codes")
-        nc.scalar.copy(*weave_views(x1_grouped[:], picked[:, :, :V]))
-        x1 = quantized("x1", x1_grouped[:])
-        w2_grouped = tile("w2_grouped", [2, 2, P * PACK], BF16, "aside")
-        deal_aside(pair_views(w2_grouped[:, 0].rearrange("p t c -> p (t c)"), w2_raw[:], "t j"))
-        deal_aside(slot_views(w2_grouped[:, 1], w2_raw[:], 2, "t j"))
-        second = quantized("w2", w2_grouped[:].rearrange("p a t c -> p (a t c)"))
-        e0_banks = ((banks[PACK], 0, half), (banks[2 * PACK - 1], half, V))
-        for bank, lo, hi in e0_banks:
-            multiply(bank[:, lo:hi], columns(second, 0, P), columns(x1, lo, hi))
-        for t in range(1, PACK - 1):
-            multiply(banks[PACK + t][:], columns(second, t * P, (t + 1) * P), columns(x1, 0, V))
-
-        def first_sensor(t, bank):
-            for u in range(2):
-                multiply(bank[:, u * half : (u + 1) * half], columns(last, (t - 2) * P, (t - 1) * P), columns(x0[u], 0, half))
-
-        first_sensor(2, banks[3])
-        activate(0, 2, banks[3], 0, MOST, "w2_raw")
-        scatter(0, 2, 0, MOST)
-        w3_space = tile("w3_grouped", [(H - TAIL) * PACK + PACK * P], BF16, "aside")
-        w3_grouped = w3_space[:, : H * PACK]
-        w3_views = slot_views(w3_grouped.rearrange("p (t c) -> p t c", t=PACK), w3_raw[:], 0, "t j")
-        deal_aside([view[:, :, : PACK - 1] for view in w3_views])
-        deal_aside([view[:, : P - TAIL, PACK - 1] for view in w3_views])
-        w3_rest = tile("w3_rest", [TAIL, PACK], F32)
-        deal_aside([w3_rest[:], w3_views[1][:, P - TAIL :, PACK - 1]])
-        e0_acts = tile("act1_0_0", [V], F32)
-        for bank, lo, hi in e0_banks:
-            activate(1, 0, bank, lo, hi, into=e0_acts[:, lo:hi])
-        acts[1, 0, 0] = e0_acts[:]
-        scatter(1, 0, 0, V)
-        late = tile("late_acts", [PACK - 1, V], F32, "w3_raw")
-
-        activate(1, 1, banks[PACK + 1], 0, V, into=late[:, 0, :])
-        scatter(1, 1, 0, V)
-        activate(0, 2, banks[3], MOST, V, into=late[:, 2, MOST:])
-        scatter(0, 2, MOST, V)
-        activate(1, 2, banks[PACK + 2], 0, V, into=late[:, 1, :])
-        first_sensor(3, banks[PACK + 2])
-        activate(0, 3, banks[PACK + 2], 0, V)
-        multiply(banks[PACK + 1][:], columns(second, 3 * P, 4 * P), columns(x1, 0, V))
-        activate(1, 3, banks[PACK + 1], 0, MOST, "act1_0_0")
-
-        parts = ((0, 1), (1, EARLY), (EARLY, S // P))
-        first_words = w3_space[:, (H - TAIL) * PACK :].bitcast(F32)
-        z_parts = [first_words.rearrange("p (g u r) -> p g u r", g=1, u=2)]
-        z_parts += [tile(f"z_words{lo}", [hi - lo, 2, P], F32) for lo, hi in parts[1:]]
+        parts = ((1, EARLY), (EARLY, S // P))
+        first_grouped = buffer("z_grouped0", P)
+        z_parts = [tile(f"z_words{lo}", [2, (hi - lo) * P], F32) for lo, hi in parts]
 
         def z_words(lo, hi):
             (start, part), = [(a, part) for (a, b), part in zip(parts, z_parts) if a <= lo < b]
-            return part[:, lo - start : hi - start]
+            return part[:, :, (lo - start) * P : (hi - start) * P]
 
         def slot(t, lo, hi):
-            pairs = z_words(lo, hi)[:, :, t // 2, :].bitcast(BF16)
-            return pairs.rearrange("p g (r e) -> p g r e", e=2)[:, :, :, t % 2]
+            if lo == 0:
+                return first_grouped[:].rearrange("p (c t) -> p c t", t=PACK)[:, :, t]
+            return z_words(lo, hi)[:, t // 2, :].bitcast(BF16).rearrange("p (c e) -> p c e", e=2)[:, :, t % 2]
 
-        def by_group(ap):
-            return ap.rearrange("p (g r) -> p g r", r=P)
+        def larger(t, lo, hi):
+            nc.vector.tensor_tensor(slot(t, lo, hi), maps[0][t][:, lo * P : hi * P], maps[1][t][:, lo * P : hi * P], MAX)
 
-        turned = tile("turned", [S // P, 2, P], BF16)
+        def join(t):
+            for lo, hi in ((0, 1), *parts):
+                larger(t, lo, hi)
 
-        def turn(out, block, start, stop):
-            nc.tensor.matmul(out, lhsT=block, rhs=identity[:], is_transpose=True, start=start, stop=stop)
-
-        def difference(t, gap, lo, hi, excess):
-            cells = slice(lo * P, hi * P)
-            nc.gpsimd.tensor_tensor(gap[:, cells], maps[1][t][:, cells], maps[0][t][:, cells], SUBTRACT)
-            nc.scalar.activation(excess, by_group(gap[:, cells]), RELU)
-
-        for t in range(2):
-            gap, excess = tile(f"gap{t}", [S], F32, "gap"), tile(f"excess{t}", [S], F32)
-            for lo in (0, PACK):
-                difference(t, gap, lo, lo + PACK, by_group(excess[:, lo * P : (lo + PACK) * P]))
-            for lo in (0, PACK):
-                bank = psum.tile([P, PACK, P], F32, name=f"sum{t}_{lo}", tag=f"bank{2 * t + lo // PACK}")
-                for b in range(PACK):
-                    cells = slice((lo + b) * P, (lo + b + 1) * P)
-                    turn(bank[:, b, :], excess[:, cells], True, False)
-                    turn(bank[:, b, :], maps[0][t][:, cells], False, True)
-                nc.scalar.copy(turned[:, lo : lo + PACK, t, :], bank[:])
-        for lo in (0, PACK):
-            bank = psum.tile([P, PACK, P], F32, name=f"pairs{lo}", tag=f"bank{2 * PACK - 2 + lo // PACK}")
-            for b in range(PACK):
-                turn(bank[:, b, :], turned[:, lo + b].rearrange("p t c -> p (t c)").bitcast(F32), True, True)
-            for first_group, last_group in ((0, 1), (1, PACK)) if lo == 0 else ((PACK, EARLY), (EARLY, S // P)):
-                nc.scalar.copy(z_words(first_group, last_group)[:, :, 0, :], bank[:, first_group - lo : last_group - lo, :])
-
-        scatter(1, 2, 0, V)
-        gap = tile("gap2", [S], F32, "gap")
-        for group in (parts[:2], parts[2:]):
-            cells = slice(group[0][0] * P, group[-1][1] * P)
-            nc.gpsimd.tensor_tensor(gap[:, cells], maps[1][2][:, cells], maps[0][2][:, cells], SUBTRACT)
-            for lo, hi in group:
-                nc.scalar.activation(z_words(lo, hi)[:, :, 1, :], by_group(gap[:, lo * P : hi * P]), RELU)
-        for lo, hi in parts:
-            a_map = by_group(maps[0][2][:, lo * P : hi * P])
-            nc.gpsimd.tensor_tensor(slot(2, lo, hi), a_map, z_words(lo, hi)[:, :, 1, :], ADD)
-        scatter(0, 3, 0, V)
-        scatter(1, 3, 0, MOST)
-        first_grouped = buffer("z_grouped0", P)
-        nc.scalar.copy(
-            first_grouped[:].bitcast(F32).rearrange("p (r u) -> p r u", u=2),
-            z_parts[0][:, 0].rearrange("p u r -> p r u"),
-        )
-        activate(1, 3, banks[PACK + 1], MOST, V, into=first_words[:, P:])
-        scatter(1, 3, MOST, V)
-        nc.scalar.copy(w3_grouped[:, H * PACK - TAIL * PACK :], w3_rest[:].rearrange("p m j -> p (m j)"))
-        third = quantized("w3", w3_grouped)
-        spare = psum.tile([P, V], F32, name="spare", tag=f"bank{PACK + 1}")
-        for t in range(WARM):
-            multiply(spare[:], columns(second, t * P, (t + 1) * P), columns(x1, 0, V))
-        last_maps = [maps[s][PACK - 1] for s in range(2)]
-        first_slots = first_grouped[:].rearrange("p (c t) -> p c t", t=PACK)
-        nc.vector.tensor_tensor(first_slots[:, :, PACK - 1], last_maps[0][:, :P], last_maps[1][:, :P], MAX)
+        for t in (0, 2, 1):
+            activate(1, t, late[:, t, :])
+        scatter(1, 0, "vector")
+        scatter(1, 2, "scalar", 0, SHARE)
+        scatter(1, 1, "scalar")
+        activate(1, 3, late[:, 3, :])
+        join(0)
+        scatter(1, 2, "vector", SHARE, V)
+        scatter(1, 3, "scalar")
+        join(1)
+        join(2)
+        larger(PACK - 1, 0, 1)
 
         out_rows = out_0.rearrange("(p t) c -> p t c", t=PACK)
         out_words = out_1[0].rearrange("p c r -> p (c r)").bitcast(I32)
@@ -313,11 +212,10 @@ def tile_picked_bev_max_lo_kernel(
 
         def regroup(lo, hi, copy):
             grouped = buffer(f"z_grouped{lo}", (hi - lo) * P)
-            both = [by_group(last_map[:, lo * P : hi * P]) for last_map in last_maps]
-            nc.vector.tensor_tensor(slot(PACK - 1, lo, hi), *both, MAX)
+            larger(PACK - 1, lo, hi)
             copy(
-                grouped[:].bitcast(F32).rearrange("p (g r u) -> p g r u", u=2, r=P),
-                z_words(lo, hi).rearrange("p g u r -> p g r u"),
+                grouped[:].bitcast(F32).rearrange("p (c u) -> p c u", u=2),
+                z_words(lo, hi).rearrange("p u c -> p c u"),
             )
             return grouped
 
@@ -352,6 +250,7 @@ def tile_picked_bev_max_lo_kernel(
                 nc.sync.dma_start(out_rows[:, rows, lo * P : hi * P], result[:, rows, :])
             results.append(result)
         out_grouped = buffer("out_grouped", S, f"z_grouped{EARLY}")
+
         def store_scales(cells):
             for q in range(P // 32):
                 queue = nc.scalar if q % 2 else nc.sync

@@ -23,7 +23,7 @@ PACK = 4
 CHUNKS = (1, 2, 2, 2, 1)
 LIST_ROWS = 16
 EARLY = 5
-SHARE = 256
+FILL = 128
 FEW = 128
 
 
@@ -132,45 +132,45 @@ def tile_picked_bev_max_lo_kernel(
         banks = [[psum.tile([P, V], F32, name=f"bank{s}_{t}", tag=f"bank{s * PACK + t}") for t in range(PACK - s)] + [None] * s for s in range(2)]
         acts = {}
 
-        def activate(s, t, into, engine="scalar", lo=0, hi=V):
-            acts[s, t] = into
+        def activate(engine, s, t, into, lo=0, hi=V):
+            acts[s, t, lo] = into
             if engine == "scalar":
-                nc.scalar.activation(into[:, lo:hi], banks[s][t][:, lo:hi], RELU)
+                nc.scalar.activation(into, banks[s][t][:, lo:hi], RELU)
             else:
-                nc.vector.tensor_scalar_max(into[:, lo:hi], banks[s][t][:, lo:hi], 0.0)
+                nc.vector.tensor_scalar_max(into, banks[s][t][:, lo:hi], 0.0)
 
-        def scatter(s, t, engine, lo=0, hi=V):
+        def scatter(engine, s, t, lo=0, hi=V):
             window = maps[s][t][:].indirect(cell_lists[s][:, lo // LIST_ROWS : hi // LIST_ROWS])
             if engine == "scalar":
-                nc.scalar.activation(window, acts[s, t][:, lo:hi], COPY, scale=ones[:])
+                nc.scalar.activation(window, acts[s, t, lo], COPY, scale=ones[:])
             else:
-                nc.vector.tensor_copy(window, acts[s, t][:, lo:hi])
+                nc.vector.tensor_copy(window, acts[s, t, lo])
 
-        early = [tile(f"act0_{t}", [V], F32)[:] for t in (0, 1, 3)]
+        early = [tile(f"act0_{t}", [V], F32)[:] for t in range(2)]
         split = psum.tile([P, V], F32, name="split", tag=f"bank{2 * PACK - 1}")
         multiply(split[:, :half], columns(first, 0, P), columns(xs[0], 0, half))
         multiply(banks[0][0][:, half:], columns(first, 0, P), columns(xs[0], half, V))
         for t in (1, 2, 3):
             multiply(banks[0][t][:], columns(first, t * P, (t + 1) * P), columns(xs[0], 0, V))
         nc.scalar.activation(early[0][:, :half], split[:, :half], RELU)
-        activate(0, 0, early[0], lo=half)
-        activate(0, 1, early[1])
-        scatter(0, 0, "vector")
-        scatter(0, 1, "scalar")
+        activate("scalar", 0, 0, early[0][:, half:], half, V)
+        acts[0, 0, 0] = early[0]
+        activate("scalar", 0, 1, early[1])
+        scatter("vector", 0, 0)
+        scatter("scalar", 0, 1)
         w2_grouped = buffer("w2_grouped", H, "picked")
         deal_aside(deal_views(w2_grouped[:], raws[1][:]))
-        w3_grouped = buffer("w3_grouped", H)
+        second = operand("w2", H)
+        quantize(columns(second, 0, P), w2_grouped[:, : P * PACK])
+        quantize(columns(second, P, H), w2_grouped[:, P * PACK :])
+        activate("scalar", 0, 2, tile("act0_2", [FILL], F32, "w1_raw")[:], 0, FILL)
+        scatter("vector", 0, 2, 0, FILL)
+        w3_grouped = buffer("w3_grouped", H, "picked")
         deal_aside(deal_views(w3_grouped[:], raws[2][:]))
-        activate(0, 2, tile("act0_2", [V], F32, "w1_raw")[:], "vector")
-        second = quantized("w2", w2_grouped[:])
-        activate(0, 3, early[2])
-        scatter(0, 2, "vector")
-        scatter(0, 3, "scalar")
-        third = quantized("w3", w3_grouped[:])
         banks[1][PACK - 1] = psum.tile([P, V], F32, name="bank_last", tag=f"bank{2 * PACK - 1}")
-        for t in (0, 2, 1, 3):
+        for t in range(PACK):
             multiply(banks[1][t][:], columns(second, t * P, (t + 1) * P), columns(xs[1], 0, V))
-        late = tile("late_acts", [PACK, V], F32, "w2_raw")
+        late = tile("late_acts", [PACK * V], F32)
 
         parts = ((1, EARLY), (EARLY, S // P))
         first_grouped = buffer("z_grouped0", P)
@@ -188,21 +188,41 @@ def tile_picked_bev_max_lo_kernel(
         def larger(t, lo, hi):
             nc.vector.tensor_tensor(slot(t, lo, hi), maps[0][t][:, lo * P : hi * P], maps[1][t][:, lo * P : hi * P], MAX)
 
-        def join(t):
-            for lo, hi in ((0, 1), *parts):
-                larger(t, lo, hi)
+        flat = tile("z_flat", [PACK - 1, S], BF16)
 
-        for t in (0, 2, 1):
-            activate(1, t, late[:, t, :])
-        scatter(1, 0, "vector")
-        scatter(1, 2, "scalar", 0, SHARE)
-        scatter(1, 1, "scalar")
-        activate(1, 3, late[:, 3, :])
+        def join(t):
+            nc.vector.tensor_tensor(flat[:, t, :], maps[0][t][:], maps[1][t][:], MAX)
+
+        def pair_slots(u, lo, hi):
+            if lo == 0:
+                return first_grouped[:].rearrange("p (c t) -> p c t", t=PACK)[:, :, 2 * u : 2 * u + 2]
+            return z_words(lo, hi)[:, u, :].bitcast(BF16).rearrange("p (c e) -> p c e", e=2)
+
+        def late_acts(t, width=V):
+            return late[:, t * V : t * V + width]
+
+        for t in range(2):
+            activate("scalar", 1, t, late_acts(t))
+        scatter("vector", 1, 0)
+        scatter("scalar", 1, 1)
         join(0)
-        scatter(1, 2, "vector", SHARE, V)
-        scatter(1, 3, "scalar")
+        third = quantized("w3", w3_grouped[:])
         join(1)
+        for lo, hi in ((0, 1), *parts):
+            deal_aside((pair_slots(0, lo, hi), flat[:, :2, lo * P : hi * P].rearrange("p e c -> p c e")))
+        activate("scalar", 0, 2, late_acts(0, V - FILL), FILL, V)
+        activate("scalar", 1, 2, late_acts(2))
+        scatter("scalar", 1, 2)
+        scatter("vector", 0, 2, FILL, V)
+        activate("scalar", 0, 3, late_acts(1, FILL), 0, FILL)
+        activate("scalar", 1, 3, late_acts(3))
+        scatter("scalar", 0, 3, 0, FILL)
+        activate("vector", 0, 3, late_acts(1)[:, FILL:], FILL, V)
         join(2)
+        for lo, hi in ((0, 1), *parts):
+            deal_aside((pair_slots(1, lo, hi), flat[:, 2, lo * P : hi * P].unsqueeze(2).to_broadcast([P, (hi - lo) * P, 2])))
+        scatter("vector", 0, 3, FILL, V)
+        scatter("scalar", 1, 3)
         larger(PACK - 1, 0, 1)
 
         out_rows = out_0.rearrange("(p t) c -> p t c", t=PACK)
@@ -242,7 +262,7 @@ def tile_picked_bev_max_lo_kernel(
         results = []
         for lo, hi in spans:
             per_bank = PACK // (hi - lo)
-            result = tile(f"result{lo}", [PACK, (hi - lo) * P], F32)
+            result = tile(f"result{lo}", [PACK, (hi - lo) * P], F32, None if lo else "z_words1")
             for b in range(lo, hi):
                 first_row = (b - lo) * per_bank
                 rows = slice(first_row, first_row + per_bank)

@@ -170,10 +170,8 @@ def tile_picked_bev_max_lo_kernel(
         banks[1][PACK - 1] = psum.tile([P, V], F32, name="bank_last", tag=f"bank{2 * PACK - 1}")
         for t in range(PACK):
             multiply(banks[1][t][:], columns(second, t * P, (t + 1) * P), columns(xs[1], 0, V))
-        late = tile("late_acts", [PACK * V], F32)
 
-        parts = ((1, EARLY), (EARLY, S // P))
-        first_grouped = buffer("z_grouped0", P)
+        parts = ((0, EARLY), (EARLY, S // P))
         z_parts = [tile(f"z_words{lo}", [2, (hi - lo) * P], F32) for lo, hi in parts]
 
         def z_words(lo, hi):
@@ -181,8 +179,6 @@ def tile_picked_bev_max_lo_kernel(
             return part[:, :, (lo - start) * P : (hi - start) * P]
 
         def slot(t, lo, hi):
-            if lo == 0:
-                return first_grouped[:].rearrange("p (c t) -> p c t", t=PACK)[:, :, t]
             return z_words(lo, hi)[:, t // 2, :].bitcast(BF16).rearrange("p (c e) -> p c e", e=2)[:, :, t % 2]
 
         def larger(t, lo, hi):
@@ -194,36 +190,30 @@ def tile_picked_bev_max_lo_kernel(
             nc.vector.tensor_tensor(flat[:, t, :], maps[0][t][:], maps[1][t][:], MAX)
 
         def pair_slots(u, lo, hi):
-            if lo == 0:
-                return first_grouped[:].rearrange("p (c t) -> p c t", t=PACK)[:, :, 2 * u : 2 * u + 2]
             return z_words(lo, hi)[:, u, :].bitcast(BF16).rearrange("p (c e) -> p c e", e=2)
 
-        def late_acts(t, width=V):
-            return late[:, t * V : t * V + width]
-
-        for t in range(2):
-            activate("scalar", 1, t, late_acts(t))
+        for t in range(PACK - 1):
+            activate("scalar", 1, t, tile(f"act1_{t}", [V], F32)[:])
         scatter("vector", 1, 0)
         scatter("scalar", 1, 1)
         join(0)
         third = quantized("w3", w3_grouped[:])
         join(1)
-        for lo, hi in ((0, 1), *parts):
+        for lo, hi in parts:
             deal_aside((pair_slots(0, lo, hi), flat[:, :2, lo * P : hi * P].rearrange("p e c -> p c e")))
-        activate("scalar", 0, 2, late_acts(0, V - FILL), FILL, V)
-        activate("scalar", 1, 2, late_acts(2))
+        activate("scalar", 0, 2, tile("act0_2_rest", [V - FILL], F32, "act1_0")[:], FILL, V)
         scatter("scalar", 1, 2)
         scatter("vector", 0, 2, FILL, V)
-        activate("scalar", 0, 3, late_acts(1, FILL), 0, FILL)
-        activate("scalar", 1, 3, late_acts(3))
+        last_acts = tile("last_acts", [2 * V], F32, "act1_1")
+        activate("scalar", 0, 3, last_acts[:, :FILL], 0, FILL)
+        activate("scalar", 1, 3, last_acts[:, V:])
         scatter("scalar", 0, 3, 0, FILL)
-        activate("vector", 0, 3, late_acts(1)[:, FILL:], FILL, V)
+        activate("vector", 0, 3, last_acts[:, FILL:V], FILL, V)
         join(2)
-        for lo, hi in ((0, 1), *parts):
+        for lo, hi in parts:
             deal_aside((pair_slots(1, lo, hi), flat[:, 2, lo * P : hi * P].unsqueeze(2).to_broadcast([P, (hi - lo) * P, 2])))
         scatter("vector", 0, 3, FILL, V)
         scatter("scalar", 1, 3)
-        larger(PACK - 1, 0, 1)
 
         out_rows = out_0.rearrange("(p t) c -> p t c", t=PACK)
         out_words = out_1[0].rearrange("p c r -> p (c r)").bitcast(I32)
@@ -232,7 +222,6 @@ def tile_picked_bev_max_lo_kernel(
 
         def regroup(lo, hi, copy):
             grouped = buffer(f"z_grouped{lo}", (hi - lo) * P)
-            larger(PACK - 1, lo, hi)
             copy(
                 grouped[:].bitcast(F32).rearrange("p (c u) -> p c u", u=2),
                 z_words(lo, hi).rearrange("p u c -> p c u"),
@@ -252,17 +241,22 @@ def tile_picked_bev_max_lo_kernel(
                     multiply(bank[:, u, :], columns(third, t * P, (t + 1) * P), columns(z, 0, width))
                 out_banks.append(bank)
 
-        last_product(0, 1, first_grouped[:])
-        for lo, hi in spans[1:3]:
-            last_product(lo, hi, regroup(lo, hi, nc.scalar.copy)[:])
-        grouped = regroup(EARLY, S // P, nc.vector.tensor_copy)
+        for lo, hi in spans[:2]:
+            larger(PACK - 1, lo, hi)
+        groups = [regroup(*spans[0], nc.vector.tensor_copy), regroup(*spans[1], nc.scalar.copy)]
+        larger(PACK - 1, *spans[2])
+        groups.append(regroup(*spans[2], nc.scalar.copy))
+        for (lo, hi), group in zip(spans, groups):
+            last_product(lo, hi, group[:])
+        larger(PACK - 1, *parts[1])
+        grouped = regroup(*parts[1], nc.vector.tensor_copy)
         for lo, hi in spans[3:]:
             last_product(lo, hi, grouped[:, (lo - EARLY) * P * PACK : (hi - EARLY) * P * PACK])
 
         results = []
         for lo, hi in spans:
             per_bank = PACK // (hi - lo)
-            result = tile(f"result{lo}", [PACK, (hi - lo) * P], F32, None if lo else "z_words1")
+            result = tile(f"result{lo}", [PACK, (hi - lo) * P], F32)
             for b in range(lo, hi):
                 first_row = (b - lo) * per_bank
                 rows = slice(first_row, first_row + per_bank)

@@ -38,7 +38,7 @@ def tile_picked_bev_max_lo_kernel(
         psum = ctx.enter_context(tc.psum_pool(name="psum", bufs=1))
 
         def tile(name, shape, dtype, tag=None):
-            return keep.tile([P, *shape], dtype, name=name, tag=tag or name, align_bytes=64)
+            return keep.tile([P, *shape], dtype, name=name, tag=tag or name, align_bytes=256)
 
         def buffer(name, width, tag=None):
             return tile(name, [width * PACK], BF16, tag)

@@ -171,7 +171,7 @@ def tile_picked_bev_max_lo_kernel(
         for t in range(PACK):
             multiply(banks[1][t][:], columns(second, t * P, (t + 1) * P), columns(xs[1], 0, V))
 
-        parts = ((0, EARLY), (EARLY, S // P))
+        parts = ((0, 3), (3, S // P))
         z_parts = [tile(f"z_words{lo}", [2, (hi - lo) * P], F32) for lo, hi in parts]
 
         def z_words(lo, hi):
@@ -233,34 +233,35 @@ def tile_picked_bev_max_lo_kernel(
         def last_product(lo, hi, grouped):
             width = (hi - lo) * P
             z = quantized(f"z{lo}", grouped)
-            per_bank = PACK // (hi - lo)
-            for b in range(lo, hi):
-                bank = psum.tile([P, per_bank, width], F32, name=f"out_bank{b}", tag=f"bank{b}")
+            tags = (lo, S // P - 1) if lo == 0 else range(lo, hi)
+            per_bank = PACK // len(tags)
+            for n, b in enumerate(tags):
+                bank = psum.tile([P, per_bank, width], F32, name=f"out_bank{lo}_{n}", tag=f"bank{b}")
                 for u in range(per_bank):
-                    t = (b - lo) * per_bank + u
+                    t = n * per_bank + u
                     multiply(bank[:, u, :], columns(third, t * P, (t + 1) * P), columns(z, 0, width))
-                out_banks.append(bank)
+                out_banks.append((lo, slice(n * per_bank, (n + 1) * per_bank), bank))
 
+        groups = []
         for lo, hi in spans[:2]:
             larger(PACK - 1, lo, hi)
-        groups = [regroup(*spans[0], nc.vector.tensor_copy), regroup(*spans[1], nc.scalar.copy)]
+        for lo, hi in spans[:2]:
+            groups.append(regroup(lo, hi, nc.scalar.copy))
+        last_product(*spans[0], groups[0][:])
         larger(PACK - 1, *spans[2])
-        groups.append(regroup(*spans[2], nc.scalar.copy))
-        for (lo, hi), group in zip(spans, groups):
-            last_product(lo, hi, group[:])
-        larger(PACK - 1, *parts[1])
-        grouped = regroup(*parts[1], nc.vector.tensor_copy)
+        last_product(*spans[1], groups[1][:])
+        groups.append(regroup(*spans[2], nc.vector.tensor_copy))
+        larger(PACK - 1, EARLY, S // P)
+        last_product(*spans[2], groups[2][:])
+        grouped = regroup(EARLY, S // P, nc.vector.tensor_copy)
         for lo, hi in spans[3:]:
             last_product(lo, hi, grouped[:, (lo - EARLY) * P * PACK : (hi - EARLY) * P * PACK])
 
         results = []
         for lo, hi in spans:
-            per_bank = PACK // (hi - lo)
             result = tile(f"result{lo}", [PACK, (hi - lo) * P], F32)
-            for b in range(lo, hi):
-                first_row = (b - lo) * per_bank
-                rows = slice(first_row, first_row + per_bank)
-                nc.scalar.copy(result[:, rows, :], out_banks[b][:])
+            for rows, bank in [(rows, bank) for first_group, rows, bank in out_banks if first_group == lo]:
+                nc.scalar.copy(result[:, rows, :], bank[:])
                 nc.sync.dma_start(out_rows[:, rows, lo * P : hi * P], result[:, rows, :])
             results.append(result)
         out_grouped = buffer("out_grouped", S, f"z_grouped{EARLY}")

@@ -24,7 +24,6 @@ CHUNKS = (1, 2, 2, 2, 1)
 LIST_ROWS = 16
 EARLY = 5
 FILL = 128
-FEW = 128
 
 
 def tile_picked_bev_max_lo_kernel(
@@ -35,6 +34,7 @@ def tile_picked_bev_max_lo_kernel(
     with ExitStack() as ctx:
         lists = ctx.enter_context(tc.tile_pool(name="lists", bufs=1))
         keep = ctx.enter_context(tc.tile_pool(name="keep", bufs=1))
+        staging = ctx.enter_context(tc.tile_pool(name="staging", bufs=1))
         psum = ctx.enter_context(tc.psum_pool(name="psum", bufs=1))
 
         def tile(name, shape, dtype, tag=None):
@@ -52,10 +52,11 @@ def tile_picked_bev_max_lo_kernel(
         def load_weights(n, w):
             nc.sync.dma_start(raws[n][:], w.rearrange("(p j) c -> p j c", j=PACK))
 
-        load_weights(0, w1)
+        nc.sync.dma_start(x_planes[0][:], x_rows[:, 0, :])
         nc.sync.dma_start(offs_sb[:], offs)
-        for j in range(PACK):
+        for j in range(1, PACK):
             nc.sync.dma_start(x_planes[j][:], x_rows[:, j, :])
+        load_weights(0, w1)
         for cell_list, source in zip(cell_lists, (near, far)):
             nc.sync.dma_start(cell_list[:], source)
         load_weights(1, w2)
@@ -63,10 +64,10 @@ def tile_picked_bev_max_lo_kernel(
 
         maps = [[tile(f"map{s}_{t}", [S], F32) for t in range(PACK)] for s in range(2)]
         ones = tile("ones", [1], F32)
-        nc.gpsimd.memset(ones[:], 1.0)
         for s in range(2):
             for t in range(PACK):
                 nc.gpsimd.memset(maps[s][t][:].bitcast(I32), 0)
+        nc.scalar.activation(ones[:], maps[0][0][:, :1], RELU, bias=1.0)
 
         def weave_views(grouped, planes):
             return (
@@ -83,8 +84,8 @@ def tile_picked_bev_max_lo_kernel(
         def deal_aside(views):
             nc.gpsimd.tensor_scalar(*views, 1.0, 0.0, MULT, ADD)
 
-        def operand(name, width):
-            return tile(f"{name}_codes", [width], U32), tile(f"{name}_scales", [width], U8)
+        def operand(name, width, tag=None):
+            return tile(f"{name}_codes", [width], U32, tag), tile(f"{name}_scales", [width], U8)
 
         def columns(pair, lo, hi):
             return [part[:, lo:hi] for part in pair]
@@ -103,11 +104,10 @@ def tile_picked_bev_max_lo_kernel(
                 rhs=moving[0].bitcast(FP8X4), rhs_scale=moving[1], start=True, stop=True,
             )
 
-        w1_grouped = buffer("w1_grouped", H)
-        nc.scalar.copy(*deal_views(w1_grouped[:], raws[0][:]))
-        first = quantized("w1", w1_grouped[:])
+        def staged(name, first_word, width):
+            return staging.tile([P, width * PACK], BF16, name=name, offset=first_word * PACK * 2, align_bytes=256)
 
-        picked = buffer("picked", S)
+        picked = staged("picked", 0, S)
 
         def gather(engine, j, lo, hi):
             slots = picked[:].rearrange("p (c j) -> p c j", j=PACK)[:, lo:hi, j]
@@ -117,17 +117,29 @@ def tile_picked_bev_max_lo_kernel(
             else:
                 nc.scalar.activation(slots, window, COPY)
 
-        for j in range(2):
+        for j in range(PACK):
             gather("vector", j, 0, V)
             gather("scalar", j, V, S)
-        for j in range(2, PACK):
-            gather("scalar", j, 0, half)
-            gather("vector", j, half, V + FEW)
-            gather("scalar", j, V + FEW, S)
-        xs = [operand(f"x{s}", V) for s in range(2)]
+        xs = [operand("x0", V)]
+        quantize(columns(xs[0], 0, V), picked[:, : V * PACK])
+
+        def pair_views(grouped, first_tile, lo, hi):
+            return (
+                grouped.rearrange("p (t m j) -> p m j t", t=2, j=PACK)[:, lo:hi],
+                raws[0][:].rearrange("p j (m t) -> p m j t", t=PACK)[:, lo:hi, :, first_tile : first_tile + 2],
+            )
+
+        first = operand("w1", H)
+        w1_pairs = [buffer("w1_pair0", half), staged("w1_pair1", S, half)]
         for u in range(2):
-            quantize(columns(xs[0], u * half, (u + 1) * half), picked[:, u * half * PACK : (u + 1) * half * PACK])
+            nc.scalar.copy(*pair_views(w1_pairs[u][:], 2 * u, 0, P // 2))
+        nc.vector.tensor_copy(*pair_views(w1_pairs[0][:], 0, P // 2, P))
+        for t in range(2):
+            quantize(columns(first, t * P, (t + 1) * P), w1_pairs[0][:, t * P * PACK : (t + 1) * P * PACK])
+        nc.vector.tensor_copy(*pair_views(w1_pairs[1][:], 2, P // 2, P))
+        xs.append(operand("x1", V, "w1_pair0"))
         quantize(columns(xs[1], 0, V), picked[:, V * PACK :])
+        quantize(columns(first, half, H), w1_pairs[1][:])
 
         banks = [[psum.tile([P, V], F32, name=f"bank{s}_{t}", tag=f"bank{s * PACK + t}") for t in range(PACK - s)] + [None] * s for s in range(2)]
         acts = {}
@@ -158,14 +170,14 @@ def tile_picked_bev_max_lo_kernel(
         activate("scalar", 0, 1, early[1])
         scatter("vector", 0, 0)
         scatter("scalar", 0, 1)
-        w2_grouped = buffer("w2_grouped", H, "picked")
+        w2_grouped = staged("w2_grouped", S - half, H)
         deal_aside(deal_views(w2_grouped[:], raws[1][:]))
         second = operand("w2", H)
         quantize(columns(second, 0, P), w2_grouped[:, : P * PACK])
         quantize(columns(second, P, H), w2_grouped[:, P * PACK :])
         activate("scalar", 0, 2, tile("act0_2", [FILL], F32, "w1_raw")[:], 0, FILL)
         scatter("vector", 0, 2, 0, FILL)
-        w3_grouped = buffer("w3_grouped", H, "picked")
+        w3_grouped = staged("w3_grouped", S - half, H)
         deal_aside(deal_views(w3_grouped[:], raws[2][:]))
         banks[1][PACK - 1] = psum.tile([P, V], F32, name="bank_last", tag=f"bank{2 * PACK - 1}")
         for t in range(PACK):

from contextlib import ExitStack

import concourse.mybir as mybir

K, T, S, H, V = 512, 2048, 1024, 512, 512
FLOPS = 2 * K * H * 2 * V + 2 * H * H * S

F32 = mybir.dt.float32
BF16 = mybir.dt.bfloat16
U32 = mybir.dt.uint32
I32 = mybir.dt.int32
U16 = mybir.dt.uint16
U8 = mybir.dt.uint8
FP8X4 = mybir.dt.float8_e4m3fn_x4
RELU = mybir.ActivationFunctionType.Relu
COPY = mybir.ActivationFunctionType.Copy
MAX = mybir.AluOpType.max
ADD = mybir.AluOpType.add
MULT = mybir.AluOpType.mult

P = 128
PACK = 4
CHUNKS = (1, 2, 2, 2, 1)
LIST_ROWS = 16
EARLY = 5
FILL = 128


def tile_picked_bev_max_lo_kernel(
    tc, xT, w1, w2, w3, offs, near, far, out_0, out_1, out_2
):
    nc = tc.nc
    half = V // 2
    with ExitStack() as ctx:
        lists = ctx.enter_context(tc.tile_pool(name="lists", bufs=1))
        keep = ctx.enter_context(tc.tile_pool(name="keep", bufs=1))
        staging = ctx.enter_context(tc.tile_pool(name="staging", bufs=1))
        psum = ctx.enter_context(tc.psum_pool(name="psum", bufs=1))

        def tile(name, shape, dtype, tag=None):
            return keep.tile([P, *shape], dtype, name=name, tag=tag or name, align_bytes=256)

        def buffer(name, width, tag=None):
            return tile(name, [width * PACK], BF16, tag)

        offs_sb = lists.tile([P, S // LIST_ROWS], U16, name="offs_sb")
        cell_lists = [lists.tile([P, V // LIST_ROWS], U16, name=f"cells{s}") for s in range(2)]
        x_rows = xT.rearrange("(p j) c -> p j c", j=PACK)
        x_planes = [tile(f"x{j}", [T], F32) for j in range(PACK)]
        raws = [tile(f"w{n}_raw", [PACK, H], F32) for n in range(3)]

        def load_weights(n, w):
            nc.sync.dma_start(raws[n][:], w.rearrange("(p j) c -> p j c", j=PACK))

        nc.sync.dma_start(x_planes[0][:], x_rows[:, 0, :])
        nc.sync.dma_start(offs_sb[:], offs)
        for j in range(1, PACK):
            nc.sync.dma_start(x_planes[j][:], x_rows[:, j, :])
        load_weights(0, w1)
        for cell_list, source in zip(cell_lists, (near, far)):
            nc.sync.dma_start(cell_list[:], source)
        load_weights(1, w2)
        load_weights(2, w3)

        maps = [[tile(f"map{s}_{t}", [S], F32) for t in range(PACK)] for s in range(2)]
        ones = tile("ones", [1], F32)
        for s in range(2):
            for t in range(PACK):
                nc.gpsimd.memset(maps[s][t][:].bitcast(I32), 0)
        nc.scalar.activation(ones[:], maps[0][0][:, :1], RELU, bias=1.0)

        def weave_views(grouped, planes):
            return (
                grouped.rearrange("p (c i j) -> p c j i", i=PACK, j=PACK),
                planes.rearrange("p j (c i) -> p c j i", i=PACK),
            )

        def deal_views(grouped, raw):
            return (
                grouped.rearrange("p (t m j) -> p m t j", t=PACK, j=PACK),
                raw.rearrange("p j (m t) -> p m t j", t=PACK),
            )

        def deal_aside(views):
            nc.gpsimd.tensor_scalar(*views, 1.0, 0.0, MULT, ADD)

        def operand(name, width, tag=None):
            return tile(f"{name}_codes", [width], U32, tag), tile(f"{name}_scales", [width], U8)

        def columns(pair, lo, hi):
            return [part[:, lo:hi] for part in pair]

        def quantize(target, grouped):
            nc.vector.quantize_mx(out=target[0].bitcast(FP8X4), scales=target[1], in_=grouped)

        def quantized(name, grouped):
            pair = operand(name, grouped.shape[1] // PACK)
            quantize([part[:] for part in pair], grouped)
            return pair

        def multiply(out, stationary, moving):
            nc.tensor.matmul_mx(
                out=out, lhsT=stationary[0].bitcast(FP8X4), lhsT_scale=stationary[1],
                rhs=moving[0].bitcast(FP8X4), rhs_scale=moving[1], start=True, stop=True,
            )

        def staged(name, first_word, width):
            return staging.tile([P, width * PACK], BF16, name=name, offset=first_word * PACK * 2, align_bytes=256)

        picked = staged("picked", 0, S)

        def gather(engine, j, lo, hi):
            slots = picked[:].rearrange("p (c j) -> p c j", j=PACK)[:, lo:hi, j]
            window = x_planes[j][:].indirect(offs_sb[:, lo // LIST_ROWS : hi // LIST_ROWS])
            if engine == "vector":
                nc.vector.tensor_copy(slots, window)
            else:
                nc.scalar.activation(slots, window, COPY)

        for j in range(PACK):
            gather("vector", j, 0, V)
            gather("scalar", j, V, S)
        xs = [operand("x0", V)]
        quantize(columns(xs[0], 0, V), picked[:, : V * PACK])

        def pair_views(grouped, first_tile, lo, hi):
            return (
                grouped.rearrange("p (t m j) -> p m j t", t=2, j=PACK)[:, lo:hi],
                raws[0][:].rearrange("p j (m t) -> p m j t", t=PACK)[:, lo:hi, :, first_tile : first_tile + 2],
            )

        first = operand("w1", H)
        w1_pairs = [buffer("w1_pair0", half), staged("w1_pair1", S, half)]
        for u in range(2):
            nc.scalar.copy(*pair_views(w1_pairs[u][:], 2 * u, 0, P // 2))
        nc.vector.tensor_copy(*pair_views(w1_pairs[0][:], 0, P // 2, P))
        for t in range(2):
            quantize(columns(first, t * P, (t + 1) * P), w1_pairs[0][:, t * P * PACK : (t + 1) * P * PACK])
        nc.vector.tensor_copy(*pair_views(w1_pairs[1][:], 2, P // 2, P))
        xs.append(operand("x1", V, "w1_pair0"))
        quantize(columns(xs[1], 0, V), picked[:, V * PACK :])
        quantize(columns(first, half, H), w1_pairs[1][:])

        banks = [[psum.tile([P, V], F32, name=f"bank{s}_{t}", tag=f"bank{s * PACK + t}") for t in range(PACK - s)] + [None] * s for s in range(2)]
        acts = {}

        def activate(engine, s, t, into, lo=0, hi=V):
            acts[s, t, lo] = into
            if engine == "scalar":
                nc.scalar.activation(into, banks[s][t][:, lo:hi], RELU)
            else:
                nc.vector.tensor_scalar_max(into, banks[s][t][:, lo:hi], 0.0)

        def scatter(engine, s, t, lo=0, hi=V):
            window = maps[s][t][:].indirect(cell_lists[s][:, lo // LIST_ROWS : hi // LIST_ROWS])
            if engine == "scalar":
                nc.scalar.activation(window, acts[s, t, lo], COPY, scale=ones[:])
            else:
                nc.vector.tensor_copy(window, acts[s, t, lo])

        early = [tile(f"act0_{t}", [V], F32)[:] for t in range(2)]
        split = psum.tile([P, V], F32, name="split", tag=f"bank{2 * PACK - 1}")
        multiply(split[:, :half], columns(first, 0, P), columns(xs[0], 0, half))
        multiply(banks[0][0][:, half:], columns(first, 0, P), columns(xs[0], half, V))
        for t in (1, 2, 3):
            multiply(banks[0][t][:], columns(first, t * P, (t + 1) * P), columns(xs[0], 0, V))
        nc.scalar.activation(early[0][:, :half], split[:, :half], RELU)
        activate("scalar", 0, 0, early[0][:, half:], half, V)
        acts[0, 0, 0] = early[0]
        activate("scalar", 0, 1, early[1])
        scatter("vector", 0, 0)
        scatter("scalar", 0, 1)
        w2_grouped = staged("w2_grouped", S - half, H)
        deal_aside(deal_views(w2_grouped[:], raws[1][:]))
        second = operand("w2", H)
        quantize(columns(second, 0, P), w2_grouped[:, : P * PACK])
        quantize(columns(second, P, H), w2_grouped[:, P * PACK :])
        activate("scalar", 0, 2, tile("act0_2", [FILL], F32, "w1_raw")[:], 0, FILL)
        scatter("vector", 0, 2, 0, FILL)
        w3_grouped = staged("w3_grouped", S - half, H)
        deal_aside(deal_views(w3_grouped[:], raws[2][:]))
        banks[1][PACK - 1] = psum.tile([P, V], F32, name="bank_last", tag=f"bank{2 * PACK - 1}")
        for t in range(PACK):
            multiply(banks[1][t][:], columns(second, t * P, (t + 1) * P), columns(xs[1], 0, V))

        parts = ((0, 3), (3, S // P))
        z_parts = [tile(f"z_words{lo}", [2, (hi - lo) * P], F32) for lo, hi in parts]

        def z_words(lo, hi):
            (start, part), = [(a, part) for (a, b), part in zip(parts, z_parts) if a <= lo < b]
            return part[:, :, (lo - start) * P : (hi - start) * P]

        def slot(t, lo, hi):
            return z_words(lo, hi)[:, t // 2, :].bitcast(BF16).rearrange("p (c e) -> p c e", e=2)[:, :, t % 2]

        def larger(t, lo, hi):
            nc.vector.tensor_tensor(slot(t, lo, hi), maps[0][t][:, lo * P : hi * P], maps[1][t][:, lo * P : hi * P], MAX)

        flat = tile("z_flat", [PACK - 1, S], BF16)

        def join(t):
            nc.vector.tensor_tensor(flat[:, t, :], maps[0][t][:], maps[1][t][:], MAX)

        def pair_slots(u, lo, hi):
            return z_words(lo, hi)[:, u, :].bitcast(BF16).rearrange("p (c e) -> p c e", e=2)

        for t in range(PACK - 1):
            activate("scalar", 1, t, tile(f"act1_{t}", [V], F32)[:])
        scatter("vector", 1, 0)
        scatter("scalar", 1, 1)
        join(0)
        third = quantized("w3", w3_grouped[:])
        join(1)
        for lo, hi in parts:
            deal_aside((pair_slots(0, lo, hi), flat[:, :2, lo * P : hi * P].rearrange("p e c -> p c e")))
        activate("scalar", 0, 2, tile("act0_2_rest", [V - FILL], F32, "act1_0")[:], FILL, V)
        scatter("scalar", 1, 2)
        scatter("vector", 0, 2, FILL, V)
        last_acts = tile("last_acts", [2 * V], F32, "act1_1")
        activate("scalar", 0, 3, last_acts[:, :FILL], 0, FILL)
        activate("scalar", 1, 3, last_acts[:, V:])
        scatter("scalar", 0, 3, 0, FILL)
        activate("vector", 0, 3, last_acts[:, FILL:V], FILL, V)
        join(2)
        for lo, hi in parts:
            deal_aside((pair_slots(1, lo, hi), flat[:, 2, lo * P : hi * P].unsqueeze(2).to_broadcast([P, (hi - lo) * P, 2])))
        scatter("vector", 0, 3, FILL, V)
        scatter("scalar", 1, 3)

        out_rows = out_0.rearrange("(p t) c -> p t c", t=PACK)
        out_words = out_1[0].rearrange("p c r -> p (c r)").bitcast(I32)
        out_codes, out_scales = tile("out_codes", [S], U32), tile("out_scales", [S], U8)
        spans = [(sum(CHUNKS[:c]), sum(CHUNKS[: c + 1])) for c in range(len(CHUNKS))]

        def regroup(lo, hi, copy):
            grouped = buffer(f"z_grouped{lo}", (hi - lo) * P)
            copy(
                grouped[:].bitcast(F32).rearrange("p (c u) -> p c u", u=2),
                z_words(lo, hi).rearrange("p u c -> p c u"),
            )
            return grouped

        out_banks = []

        def last_product(lo, hi, grouped):
            width = (hi - lo) * P
            z = quantized(f"z{lo}", grouped)
            tags = (lo, S // P - 1) if lo == 0 else range(lo, hi)
            per_bank = PACK // len(tags)
            for n, b in enumerate(tags):
                bank = psum.tile([P, per_bank, width], F32, name=f"out_bank{lo}_{n}", tag=f"bank{b}")
                for u in range(per_bank):
                    t = n * per_bank + u
                    multiply(bank[:, u, :], columns(third, t * P, (t + 1) * P), columns(z, 0, width))
                out_banks.append((lo, slice(n * per_bank, (n + 1) * per_bank), bank))

        groups = []
        for lo, hi in spans[:2]:
            larger(PACK - 1, lo, hi)
        for lo, hi in spans[:2]:
            groups.append(regroup(lo, hi, nc.scalar.copy))
        last_product(*spans[0], groups[0][:])
        larger(PACK - 1, *spans[2])
        last_product(*spans[1], groups[1][:])
        groups.append(regroup(*spans[2], nc.vector.tensor_copy))
        larger(PACK - 1, EARLY, S // P)
        last_product(*spans[2], groups[2][:])
        grouped = regroup(EARLY, S // P, nc.vector.tensor_copy)
        for lo, hi in spans[3:]:
            last_product(lo, hi, grouped[:, (lo - EARLY) * P * PACK : (hi - EARLY) * P * PACK])

        results = []
        for lo, hi in spans:
            result = tile(f"result{lo}", [PACK, (hi - lo) * P], F32)
            for rows, bank in [(rows, bank) for first_group, rows, bank in out_banks if first_group == lo]:
                nc.scalar.copy(result[:, rows, :], bank[:])
                nc.sync.dma_start(out_rows[:, rows, lo * P : hi * P], result[:, rows, :])
            results.append(result)
        out_grouped = buffer("out_grouped", S, f"z_grouped{EARLY}")

        def store_scales(cells):
            for q in range(P // 32):
                queue = nc.scalar if q % 2 else nc.sync
                queue.dma_start(
                    out_2[0, 4 * q : 4 * q + 4, cells].bitcast(I32), out_scales[32 * q : 32 * q + 4, cells].bitcast(I32)
                )

        def planes(lo, hi):
            cells = slice(lo * P, hi * P)
            nc.vector.quantize_mx(
                out=out_codes[:, cells].bitcast(FP8X4), scales=out_scales[:, cells],
                in_=out_grouped[:, lo * P * PACK : hi * P * PACK],
            )

        def store_words(lo, hi):
            nc.sync.dma_start(out_words[:, lo * P : hi * P], out_codes[:, lo * P : hi * P].bitcast(I32))

        def weave(chunk, first_group, last_group, copy):
            lo = spans[chunk][0]
            part = results[chunk][:, :, (first_group - lo) * P : (last_group - lo) * P]
            copy(*weave_views(out_grouped[:, first_group * P * PACK : last_group * P * PACK], part))

        for chunk in range(3):
            weave(chunk, *spans[chunk], nc.vector.tensor_copy)
        weave(3, 6, 7, nc.scalar.copy)
        weave(4, 7, 8, nc.scalar.copy)
        planes(0, 4)
        store_words(0, 4)
        weave(3, 5, 6, nc.vector.tensor_copy)
        planes(4, 6)
        planes(6, 7)
        store_words(4, 7)
        planes(7, 8)
        store_words(7, 8)
        store_scales(slice(0, S))
